import numpy as np
import ml_dtypes


def mxq(x, axis, fmt="e4m3"):
    dtype, down = {"e4m3": (ml_dtypes.float8_e4m3fn, 7), "e5m2": (ml_dtypes.float8_e5m2, 14)}[fmt]
    v = np.moveaxis(np.asarray(x, np.float32).astype(ml_dtypes.bfloat16).astype(np.float64), axis, -1)
    blocks = v.reshape(v.shape[:-1] + (-1, 32))
    amax = np.abs(blocks).max(-1, keepdims=True)
    byte = np.maximum(np.where(amax > 0, np.frexp(amax)[1] - 1 + 127, 0) - down, 1)
    scale = np.exp2(byte - 127.0)
    codes = (blocks / scale).astype(np.float32).astype(dtype).astype(np.float64)
    return np.moveaxis((codes * scale).reshape(v.shape), -1, axis)


WIDE = False


def mx_kscale(k):
    if not WIDE:
        return np.ones(k)
    levels = np.array([30, -30])
    if k % 512:
        return np.exp2(np.random.permutation(np.resize(levels, k // 32))).repeat(32)
    a = np.empty((k // 512, 16))
    for p in range(k // 512):
        a[p, :8] = np.random.permutation(np.resize(levels, 8))
        for g in range(8):
            far = levels[np.abs(levels - a[p, g]) >= 10]
            a[p, g + 8] = far[np.random.randint(len(far))]
    return np.exp2(a.ravel()).repeat(32)


def f64(x):
    return np.asarray(x).astype(np.float64)


def striped(idx):
    return np.tile(idx.reshape(-1, 16).T, (8, 1)).astype(np.uint16)


def unstriped(offs):
    return offs[:16].T.reshape(-1).astype(np.int64)


K, T, E, C, N = 128, 2048, 4, 512, 1536


def by_expert(wq, xq):
    return np.concatenate([wq[e].T @ xq[:, e * C:(e + 1) * C] for e in range(E)], axis=1)


def setup_inputs():
    n = np.random.standard_normal
    s = mx_kscale(N)[:, None]
    return {
        "dyT": (n((N, T)) * s).astype(np.float32),
        "w": (n((E, N, K)) / np.sqrt(N) / s[None]).astype(np.float32),
        "gate": np.tile(np.random.uniform(0.2, 1.0, E * C), (N, 1)).astype(np.float32),
        "offs": striped(np.random.permutation(T)[:E * C]),
    }


def reference(dyT, w, gate, offs):
    idx = unstriped(offs)
    gq = mxq(f64(gate) * f64(dyT)[:, idx], 0, "e5m2")
    dx = by_expert(mxq(f64(w), 1, "e4m3"), gq)
    out = np.zeros((K, T))
    out[:, idx] = dx
    return out

@@ -1,0 +1,184 @@
+from contextlib import ExitStack
+
+import concourse.mybir as mybir
+
+K, T, E, C, N = 128, 2048, 4, 512, 1536
+SLOTS = E * C
+P = 128
+PLANES = 4
+PASSES = N // (P * PLANES)
+OFFSETS = 16
+HALF = SLOTS // 2
+RUN = 4
+
+FIRST_CUTS = (0, 128, C, HALF, SLOTS)
+
+FLOPS = 2 * K * N * SLOTS
+BYTES = 4 * (N * T + E * N * K + SLOTS + K * T) + 2 * SLOTS
+
+F32 = mybir.dt.float32
+BF16 = mybir.dt.bfloat16
+U32 = mybir.dt.uint32
+U16 = mybir.dt.uint16
+U8 = mybir.dt.uint8
+E4M3 = mybir.dt.float8_e4m3fn_x4
+E5M2 = mybir.dt.float8_e5m2_x4
+
+
+def tile_moe_bdx_lin_none_kernel(tc, dyT, w, gate, offs, out):
+    nc = tc.nc
+    dy_rows = dyT.rearrange("(g p t) c -> g t p c", p=P, t=PLANES)
+    w_rows = w.rearrange("e (g p t) k -> g p e (t k)", p=P, t=PLANES)
+
+    with ExitStack() as ctx:
+        lists = ctx.enter_context(tc.tile_pool(name="lists", bufs=1))
+        keep = ctx.enter_context(tc.tile_pool(name="keep", bufs=1))
+        dy_pool = ctx.enter_context(tc.tile_pool(name="dy_pool", bufs=8))
+        w_raw_pool = ctx.enter_context(tc.tile_pool(name="w_raw_pool", bufs=2))
+        w_side_pool = ctx.enter_context(tc.tile_pool(name="w_side_pool", bufs=2))
+        half_pool = ctx.enter_context(tc.tile_pool(name="half_pool", bufs=3))
+        expert_pool = ctx.enter_context(tc.tile_pool(name="expert_pool", bufs=3))
+        side_pool = ctx.enter_context(tc.tile_pool(name="side_pool", bufs=3))
+        code_pool = ctx.enter_context(tc.tile_pool(name="code_pool", bufs=3))
+        psum = ctx.enter_context(tc.psum_pool(name="psum", bufs=1))
+
+        offsets = lists.tile([P, SLOTS // OFFSETS], U16, name="offsets")
+        gates = keep.tile([P, SLOTS], F32, name="gates")
+        tokens = keep.tile([P, T], F32, name="tokens")
+        w_codes = [keep.tile([P, E * K], U32, name=f"w_codes{g}", align_bytes=64) for g in range(PASSES)]
+        w_scales = [keep.tile([P, E * K], U8, name=f"w_scales{g}", align_bytes=64) for g in range(PASSES)]
+        results = [keep.tile([P, C], F32, name=f"result{e}") for e in range(E)]
+        banks = [psum.tile([P, C], F32, name=f"bank{e}") for e in range(E)]
+
+        dy = {}
+        w_raw = {}
+
+        def load_gates(first, last):
+            nc.sync.dma_start(out=gates[:, first:last], in_=gate[0:P, first:last])
+
+        def load_dy(g, t):
+            dy[g, t] = dy_pool.tile([P, T], F32, name="dy_block")
+            nc.sync.dma_start(out=dy[g, t][:], in_=dy_rows[g, t])
+
+        def load_w(g):
+            w_raw[g] = w_raw_pool.tile([P, E, PLANES, K], F32, name="w_block")
+            nc.sync.dma_start(out=w_raw[g][:].rearrange("p e t k -> p e (t k)"), in_=w_rows[g])
+
+        nc.sync.dma_start(out=offsets[:], in_=offs)
+        load_gates(FIRST_CUTS[0], FIRST_CUTS[1])
+        load_dy(0, 0)
+        for first, last in zip(FIRST_CUTS[1:], FIRST_CUTS[2:]):
+            load_gates(first, last)
+        load_dy(0, 1)
+        load_dy(0, 2)
+        load_w(0)
+        load_dy(0, 3)
+        for g in range(1, PASSES):
+            for t in range(PLANES):
+                load_dy(g, t)
+            load_w(g)
+
+        def side_by_side(grouped, planes):
+            nc.scalar.copy(
+                out=grouped.rearrange("p (c i) t -> p c t i", i=RUN),
+                in_=planes.rearrange("p t (c i) -> p c t i", i=RUN),
+            )
+
+        def quantise_w(g):
+            grouped = w_side_pool.tile([P, E, K, PLANES], BF16, name="w_grouped", align_bytes=64)
+            for e in range(E):
+                side_by_side(grouped[:, e], w_raw[g][:, e])
+            nc.vector.quantize_mx(
+                out=w_codes[g][:].bitcast(E4M3),
+                scales=w_scales[g][:],
+                in_=grouped[:].rearrange("p e k t -> p (e k t)"),
+            )
+
+        gathered = {}
+        interleaved = {}
+
+        def open_unit(unit):
+            count = unit[2]
+            pool = half_pool if count == HALF else expert_pool
+            gathered[unit] = pool.tile([P, PLANES, count], F32, name="gathered_planes")
+
+        def gather(unit, t, first, last):
+            g, start, count = unit
+            nc.vector.tensor_tensor(
+                gathered[unit][:, t, first - start : last - start],
+                dy[g, t][:].indirect(offsets[:, first // OFFSETS : last // OFFSETS]),
+                gates[:, first:last],
+                mybir.AluOpType.mult,
+            )
+
+        def interleave(unit):
+            count = unit[2]
+            interleaved[unit] = side_pool.tile([P, count, PLANES], BF16, name="grouped", align_bytes=64)
+            for c in range(0, count, C):
+                side_by_side(interleaved[unit][:, c : c + C], gathered[unit][:, :, c : c + C])
+
+        def multiply(unit):
+            g, start, count = unit
+            codes = code_pool.tile([P, count], U32, name="codes", align_bytes=64)
+            scales = code_pool.tile([P, count], U8, name="scales", align_bytes=64)
+            nc.vector.quantize_mx(
+                out=codes[:].bitcast(E5M2),
+                scales=scales[:],
+                in_=interleaved[unit][:].rearrange("p c t -> p (c t)"),
+            )
+            for c in range(0, count, C):
+                e = (start + c) // C
+                nc.tensor.matmul_mx(
+                    out=banks[e][:],
+                    lhsT=w_codes[g][:, e * K : (e + 1) * K].bitcast(E4M3),
+                    lhsT_scale=w_scales[g][:, e * K : (e + 1) * K],
+                    rhs=codes[:, c : c + C].bitcast(E5M2),
+                    rhs_scale=scales[:, c : c + C],
+                    start=(g == 0),
+                    stop=(g == PASSES - 1),
+                )
+
+        def finish(unit):
+            e = unit[1] // C
+            nc.scalar.copy(out=results[e][:], in_=banks[e][:])
+
+        def scatter(e):
+            nc.vector.tensor_copy(
+                tokens[:].indirect(offsets[:, e * C // OFFSETS : (e + 1) * C // OFFSETS]), results[e][:]
+            )
+
+        first_units = [(0, start, HALF) for start in range(0, SLOTS, HALF)]
+        for unit in first_units:
+            open_unit(unit)
+        quantise_w(0)
+        for t in range(PLANES):
+            cuts = FIRST_CUTS if t == 0 else (0, HALF, SLOTS)
+            for first, last in zip(cuts, cuts[1:]):
+                gather(first_units[first // HALF], t, first, last)
+        for unit in first_units:
+            interleave(unit)
+
+        units = list(first_units)
+        for g in range(1, PASSES):
+            size = C if g == PASSES - 1 else HALF
+            for start in range(0, SLOTS, size):
+                unit = (g, start, size)
+                units.append(unit)
+                open_unit(unit)
+                for t in range(PLANES):
+                    gather(unit, t, start, start + size)
+                earlier = units[-3]
+                multiply(earlier)
+                interleave(unit)
+                if start == 0:
+                    quantise_w(g)
+                if earlier[0] == PASSES - 1:
+                    finish(earlier)
+
+        last_units = units[-2:]
+        for e in range(E):
+            scatter(e)
+            if e < len(last_units):
+                multiply(last_units[e])
+                finish(last_units[e])
+        nc.sync.dma_start(out=out, in_=tokens[:])

@@ -9,6 +9,7 @@ PLANES = 4
 PASSES = N // (P * PLANES)
 OFFSETS = 16
 HALF = SLOTS // 2
+SPARE = 16
 RUN = 4
 
 FIRST_CUTS = (0, 128, C, HALF, SLOTS)
@@ -29,6 +30,9 @@ def tile_moe_bdx_lin_none_kernel(tc, dyT, w, gate, offs, out):
     nc = tc.nc
     dy_rows = dyT.rearrange("(g p t) c -> g t p c", p=P, t=PLANES)
     w_rows = w.rearrange("e (g p t) k -> g p e (t k)", p=P, t=PLANES)
+    last_pass = PASSES - 1
+    last_plane = PLANES - 1
+    last_expert = E - 1
 
     with ExitStack() as ctx:
         lists = ctx.enter_context(tc.tile_pool(name="lists", bufs=1))
@@ -36,14 +40,14 @@ def tile_moe_bdx_lin_none_kernel(tc, dyT, w, gate, offs, out):
         dy_pool = ctx.enter_context(tc.tile_pool(name="dy_pool", bufs=8))
         w_raw_pool = ctx.enter_context(tc.tile_pool(name="w_raw_pool", bufs=2))
         w_side_pool = ctx.enter_context(tc.tile_pool(name="w_side_pool", bufs=2))
-        half_pool = ctx.enter_context(tc.tile_pool(name="half_pool", bufs=3))
-        expert_pool = ctx.enter_context(tc.tile_pool(name="expert_pool", bufs=3))
+        pass_pool = ctx.enter_context(tc.tile_pool(name="pass_pool", bufs=2))
         side_pool = ctx.enter_context(tc.tile_pool(name="side_pool", bufs=3))
         code_pool = ctx.enter_context(tc.tile_pool(name="code_pool", bufs=3))
         psum = ctx.enter_context(tc.psum_pool(name="psum", bufs=1))
 
         offsets = lists.tile([P, SLOTS // OFFSETS], U16, name="offsets")
-        gates = keep.tile([P, SLOTS], F32, name="gates")
+        shared = keep.tile([P, C + SLOTS], F32, name="shared")
+        gates = shared[:, C:]
         tokens = keep.tile([P, T], F32, name="tokens")
         w_codes = [keep.tile([P, E * K], U32, name=f"w_codes{g}", align_bytes=64) for g in range(PASSES)]
         w_scales = [keep.tile([P, E * K], U8, name=f"w_scales{g}", align_bytes=64) for g in range(PASSES)]
@@ -57,8 +61,8 @@ def tile_moe_bdx_lin_none_kernel(tc, dyT, w, gate, offs, out):
             nc.sync.dma_start(out=gates[:, first:last], in_=gate[0:P, first:last])
 
         def load_dy(g, t):
-            dy[g, t] = dy_pool.tile([P, T], F32, name="dy_block")
-            nc.sync.dma_start(out=dy[g, t][:], in_=dy_rows[g, t])
+            dy[g, t] = dy_pool.tile([P, T + SPARE], F32, name="dy_block")
+            nc.sync.dma_start(out=dy[g, t][:, :T], in_=dy_rows[g, t])
 
         def load_w(g):
             w_raw[g] = w_raw_pool.tile([P, E, PLANES, K], F32, name="w_block")
@@ -74,9 +78,9 @@ def tile_moe_bdx_lin_none_kernel(tc, dyT, w, gate, offs, out):
         load_w(0)
         load_dy(0, 3)
         for g in range(1, PASSES):
+            load_w(g)
             for t in range(PLANES):
                 load_dy(g, t)
-            load_w(g)
 
         def side_by_side(grouped, planes):
             nc.scalar.copy(
@@ -94,28 +98,21 @@ def tile_moe_bdx_lin_none_kernel(tc, dyT, w, gate, offs, out):
                 in_=grouped[:].rearrange("p e k t -> p (e k t)"),
             )
 
-        gathered = {}
-        interleaved = {}
-
-        def open_unit(unit):
-            count = unit[2]
-            pool = half_pool if count == HALF else expert_pool
-            gathered[unit] = pool.tile([P, PLANES, count], F32, name="gathered_planes")
-
-        def gather(unit, t, first, last):
-            g, start, count = unit
+        def gather(plane, g, t, first, last):
             nc.vector.tensor_tensor(
-                gathered[unit][:, t, first - start : last - start],
+                plane,
                 dy[g, t][:].indirect(offsets[:, first // OFFSETS : last // OFFSETS]),
                 gates[:, first:last],
                 mybir.AluOpType.mult,
             )
 
-        def interleave(unit):
+        interleaved = {}
+
+        def interleave(unit, planes):
             count = unit[2]
             interleaved[unit] = side_pool.tile([P, count, PLANES], BF16, name="grouped", align_bytes=64)
             for c in range(0, count, C):
-                side_by_side(interleaved[unit][:, c : c + C], gathered[unit][:, :, c : c + C])
+                side_by_side(interleaved[unit][:, c : c + C], planes[:, :, c : c + C])
 
         def multiply(unit):
             g, start, count = unit
@@ -135,11 +132,10 @@ def tile_moe_bdx_lin_none_kernel(tc, dyT, w, gate, offs, out):
                     rhs=codes[:, c : c + C].bitcast(E5M2),
                     rhs_scale=scales[:, c : c + C],
                     start=(g == 0),
-                    stop=(g == PASSES - 1),
+                    stop=(g == last_pass),
                 )
 
-        def finish(unit):
-            e = unit[1] // C
+        def finish(e):
             nc.scalar.copy(out=results[e][:], in_=banks[e][:])
 
         def scatter(e):
@@ -147,38 +143,39 @@ def tile_moe_bdx_lin_none_kernel(tc, dyT, w, gate, offs, out):
                 tokens[:].indirect(offsets[:, e * C // OFFSETS : (e + 1) * C // OFFSETS]), results[e][:]
             )
 
-        first_units = [(0, start, HALF) for start in range(0, SLOTS, HALF)]
-        for unit in first_units:
-            open_unit(unit)
-        quantise_w(0)
+        waiting = []
+        for g in range(PASSES):
+            width = SLOTS if g < last_pass else SLOTS - C
+            planes = pass_pool.tile([P, PLANES, width], F32, name="gathered_planes")
+            for t in range(PLANES):
+                if (g, t) == (0, 0):
+                    cuts = FIRST_CUTS
+                elif (g, t) == (last_pass, last_plane):
+                    cuts = (0, C, width)
+                else:
+                    cuts = (0, width)
+                for first, last in zip(cuts, cuts[1:]):
+                    gather(planes[:, t, first:last], g, t, first, last)
+                if 1 <= t <= len(waiting):
+                    multiply(waiting[t - 1])
+            quantise_w(g)
+            if g < last_pass:
+                waiting = [(g, start, HALF) for start in range(0, SLOTS, HALF)]
+                for unit in waiting:
+                    interleave(unit, planes[:, :, unit[1] : unit[1] + HALF])
+
+        units = [(last_pass, e * C, C) for e in range(E)]
+        own = shared[:, : PLANES * C].rearrange("p (t c) -> p t c", t=PLANES)
+        interleave(units[0], planes[:, :, 0:C])
         for t in range(PLANES):
-            cuts = FIRST_CUTS if t == 0 else (0, HALF, SLOTS)
-            for first, last in zip(cuts, cuts[1:]):
-                gather(first_units[first // HALF], t, first, last)
-        for unit in first_units:
-            interleave(unit)
-
-        units = list(first_units)
-        for g in range(1, PASSES):
-            size = C if g == PASSES - 1 else HALF
-            for start in range(0, SLOTS, size):
-                unit = (g, start, size)
-                units.append(unit)
-                open_unit(unit)
-                for t in range(PLANES):
-                    gather(unit, t, start, start + size)
-                earlier = units[-3]
-                multiply(earlier)
-                interleave(unit)
-                if start == 0:
-                    quantise_w(g)
-                if earlier[0] == PASSES - 1:
-                    finish(earlier)
-
-        last_units = units[-2:]
-        for e in range(E):
-            scatter(e)
-            if e < len(last_units):
-                multiply(last_units[e])
-                finish(last_units[e])
+            gather(own[:, t], last_pass, t, last_expert * C, SLOTS)
+            if t == 1:
+                multiply(units[0])
+        for e in range(1, E):
+            interleave(units[e], planes[:, :, e * C : (e + 1) * C] if e < last_expert else own)
+            finish(e - 1)
+            multiply(units[e])
+            scatter(e - 1)
+        finish(last_expert)
+        scatter(last_expert)
         nc.sync.dma_start(out=out, in_=tokens[:])

@@ -78,9 +78,10 @@ def tile_moe_bdx_lin_none_kernel(tc, dyT, w, gate, offs, out):
         load_w(0)
         load_dy(0, 3)
         for g in range(1, PASSES):
-            load_w(g)
             for t in range(PLANES):
                 load_dy(g, t)
+                if t == 1:
+                    load_w(g)
 
         def side_by_side(grouped, planes):
             nc.scalar.copy(

@@ -68,10 +68,9 @@ def tile_moe_bdx_lin_none_kernel(tc, dyT, w, gate, offs, out):
             w_raw[g] = w_raw_pool.tile([P, E, PLANES, K], F32, name="w_block")
             nc.sync.dma_start(out=w_raw[g][:].rearrange("p e t k -> p e (t k)"), in_=w_rows[g])
 
-        nc.sync.dma_start(out=offsets[:], in_=offs)
-        load_gates(FIRST_CUTS[0], FIRST_CUTS[1])
         load_dy(0, 0)
-        for first, last in zip(FIRST_CUTS[1:], FIRST_CUTS[2:]):
+        nc.sync.dma_start(out=offsets[:], in_=offs)
+        for first, last in zip(FIRST_CUTS, FIRST_CUTS[1:]):
             load_gates(first, last)
         load_dy(0, 1)
         load_dy(0, 2)

@@ -12,7 +12,7 @@ HALF = SLOTS // 2
 SPARE = 16
 RUN = 4
 
-FIRST_CUTS = (0, 128, C, HALF, SLOTS)
+FIRST_CUTS = (0, 128, 384, 896, SLOTS)
 
 FLOPS = 2 * K * N * SLOTS
 BYTES = 4 * (N * T + E * N * K + SLOTS + K * T) + 2 * SLOTS
@@ -178,4 +178,5 @@ def tile_moe_bdx_lin_none_kernel(tc, dyT, w, gate, offs, out):
             scatter(e - 1)
         finish(last_expert)
         scatter(last_expert)
-        nc.sync.dma_start(out=out, in_=tokens[:])
+        nc.sync.dma_start(out=out[:, : T // 2], in_=tokens[:, : T // 2])
+        nc.scalar.dma_start(out=out[:, T // 2 :], in_=tokens[:, T // 2 :])

@@ -32,26 +32,28 @@ def tile_moe_bdx_lin_none_kernel(tc, dyT, w, gate, offs, out):
     w_rows = w.rearrange("e (g p t) k -> g p e (t k)", p=P, t=PLANES)
     last_pass = PASSES - 1
     last_plane = PLANES - 1
-    last_expert = E - 1
 
     with ExitStack() as ctx:
         lists = ctx.enter_context(tc.tile_pool(name="lists", bufs=1))
         keep = ctx.enter_context(tc.tile_pool(name="keep", bufs=1))
-        dy_pool = ctx.enter_context(tc.tile_pool(name="dy_pool", bufs=8))
-        w_raw_pool = ctx.enter_context(tc.tile_pool(name="w_raw_pool", bufs=2))
-        w_side_pool = ctx.enter_context(tc.tile_pool(name="w_side_pool", bufs=2))
+        dy_pool = ctx.enter_context(tc.tile_pool(name="dy_pool", bufs=6))
+        w_raw_pool = ctx.enter_context(tc.tile_pool(name="w_raw_pool", bufs=1))
         pass_pool = ctx.enter_context(tc.tile_pool(name="pass_pool", bufs=2))
-        side_pool = ctx.enter_context(tc.tile_pool(name="side_pool", bufs=3))
-        code_pool = ctx.enter_context(tc.tile_pool(name="code_pool", bufs=3))
         psum = ctx.enter_context(tc.psum_pool(name="psum", bufs=1))
 
         offsets = lists.tile([P, SLOTS // OFFSETS], U16, name="offsets")
-        shared = keep.tile([P, C + SLOTS], F32, name="shared")
-        gates = shared[:, C:]
+        gates = keep.tile([P, SLOTS], F32, name="gates", align_bytes=64)
         tokens = keep.tile([P, T], F32, name="tokens")
-        w_codes = [keep.tile([P, E * K], U32, name=f"w_codes{g}", align_bytes=64) for g in range(PASSES)]
-        w_scales = [keep.tile([P, E * K], U8, name=f"w_scales{g}", align_bytes=64) for g in range(PASSES)]
-        results = [keep.tile([P, C], F32, name=f"result{e}") for e in range(E)]
+        w_grouped = keep.tile([P, PASSES * E, K, PLANES], BF16, name="w_grouped", align_bytes=64)
+        w_scales = keep.tile([P, PASSES * E * K], U8, name="w_scales", align_bytes=64)
+        units = [(g, e, 2) for g in range(last_pass) for e in (0, 2)]
+        units.extend([(last_pass, 0, 1), (last_pass, 1, 1), (last_pass, 2, 2)])
+        grouped = {
+            u: keep.tile([P, u[2] * C * PLANES], BF16, name=f"grouped{u[0]}{u[1]}", align_bytes=64) for u in units
+        }
+        scales = {u: keep.tile([P, u[2] * C], U8, name=f"scales{u[0]}{u[1]}", align_bytes=64) for u in units}
+        last_codes = keep.tile([P, SLOTS], U32, name="last_codes", align_bytes=64)
+        first_result = keep.tile([P, C], F32, name="first_result")
         banks = [psum.tile([P, C], F32, name=f"bank{e}") for e in range(E)]
 
         dy = {}
@@ -65,7 +67,8 @@ def tile_moe_bdx_lin_none_kernel(tc, dyT, w, gate, offs, out):
             nc.sync.dma_start(out=dy[g, t][:, :T], in_=dy_rows[g, t])
 
         def load_w(g):
-            w_raw[g] = w_raw_pool.tile([P, E, PLANES, K], F32, name="w_block")
+            tag = "w_last" if g == last_pass else "w_block"
+            w_raw[g] = w_raw_pool.tile([P, E, PLANES, K], F32, name=tag, align_bytes=64)
             nc.sync.dma_start(out=w_raw[g][:].rearrange("p e t k -> p e (t k)"), in_=w_rows[g])
 
         load_dy(0, 0)
@@ -82,20 +85,21 @@ def tile_moe_bdx_lin_none_kernel(tc, dyT, w, gate, offs, out):
                 if t == 1:
                     load_w(g)
 
-        def side_by_side(grouped, planes):
+        def side_by_side(target, planes):
             nc.scalar.copy(
-                out=grouped.rearrange("p (c i) t -> p c t i", i=RUN),
+                out=target.rearrange("p (c i) t -> p c t i", i=RUN),
                 in_=planes.rearrange("p t (c i) -> p c t i", i=RUN),
             )
 
-        def quantise_w(g):
-            grouped = w_side_pool.tile([P, E, K, PLANES], BF16, name="w_grouped", align_bytes=64)
+        def group_w(g):
             for e in range(E):
-                side_by_side(grouped[:, e], w_raw[g][:, e])
+                side_by_side(w_grouped[:, g * E + e], w_raw[g][:, e])
+
+        def quantise_w(first, last):
             nc.vector.quantize_mx(
-                out=w_codes[g][:].bitcast(E4M3),
-                scales=w_scales[g][:],
-                in_=grouped[:].rearrange("p e k t -> p (e k t)"),
+                out=w_codes[:, first * E * K : last * E * K].bitcast(E4M3),
+                scales=w_scales[:, first * E * K : last * E * K],
+                in_=w_grouped[:, first * E : last * E].rearrange("p e k t -> p (e k t)"),
             )
 
         def gather(plane, g, t, first, last):
@@ -106,77 +110,68 @@ def tile_moe_bdx_lin_none_kernel(tc, dyT, w, gate, offs, out):
                 mybir.AluOpType.mult,
             )
 
-        interleaved = {}
+        def interleave(unit, e, planes):
+            c = (e - unit[1]) * C
+            target = grouped[unit][:, c * PLANES : (c + C) * PLANES].rearrange("p (c t) -> p c t", t=PLANES)
+            side_by_side(target, planes[:, :, e * C : (e + 1) * C])
 
-        def interleave(unit, planes):
-            count = unit[2]
-            interleaved[unit] = side_pool.tile([P, count, PLANES], BF16, name="grouped", align_bytes=64)
-            for c in range(0, count, C):
-                side_by_side(interleaved[unit][:, c : c + C], planes[:, :, c : c + C])
-
-        def multiply(unit):
-            g, start, count = unit
-            codes = code_pool.tile([P, count], U32, name="codes", align_bytes=64)
-            scales = code_pool.tile([P, count], U8, name="scales", align_bytes=64)
-            nc.vector.quantize_mx(
-                out=codes[:].bitcast(E5M2),
-                scales=scales[:],
-                in_=interleaved[unit][:].rearrange("p c t -> p (c t)"),
-            )
-            for c in range(0, count, C):
-                e = (start + c) // C
+        def multiply(unit, codes):
+            g, first, count = unit
+            nc.vector.quantize_mx(out=codes.bitcast(E5M2), scales=scales[unit][:], in_=grouped[unit][:])
+            for e in range(first, first + count):
+                columns = slice((g * E + e) * K, (g * E + e + 1) * K)
+                slots = slice((e - first) * C, (e - first + 1) * C)
                 nc.tensor.matmul_mx(
                     out=banks[e][:],
-                    lhsT=w_codes[g][:, e * K : (e + 1) * K].bitcast(E4M3),
-                    lhsT_scale=w_scales[g][:, e * K : (e + 1) * K],
-                    rhs=codes[:, c : c + C].bitcast(E5M2),
-                    rhs_scale=scales[:, c : c + C],
+                    lhsT=w_codes[:, columns].bitcast(E4M3),
+                    lhsT_scale=w_scales[:, columns],
+                    rhs=codes[:, slots].bitcast(E5M2),
+                    rhs_scale=scales[unit][:, slots],
                     start=(g == 0),
                     stop=(g == last_pass),
                 )
 
-        def finish(e):
-            nc.scalar.copy(out=results[e][:], in_=banks[e][:])
+        def scatter(first, last, values):
+            nc.vector.tensor_copy(tokens[:].indirect(offsets[:, first // OFFSETS : last // OFFSETS]), values)
 
-        def scatter(e):
-            nc.vector.tensor_copy(
-                tokens[:].indirect(offsets[:, e * C // OFFSETS : (e + 1) * C // OFFSETS]), results[e][:]
-            )
-
-        waiting = []
         for g in range(PASSES):
-            width = SLOTS if g < last_pass else SLOTS - C
-            planes = pass_pool.tile([P, PLANES, width], F32, name="gathered_planes")
+            planes = pass_pool.tile([P, PLANES, SLOTS], F32, name="gathered_planes", align_bytes=64)
             for t in range(PLANES):
                 if (g, t) == (0, 0):
                     cuts = FIRST_CUTS
                 elif (g, t) == (last_pass, last_plane):
-                    cuts = (0, C, width)
+                    cuts = (0, HALF, SLOTS)
                 else:
-                    cuts = (0, width)
+                    cuts = (0, SLOTS)
                 for first, last in zip(cuts, cuts[1:]):
                     gather(planes[:, t, first:last], g, t, first, last)
-                if 1 <= t <= len(waiting):
-                    multiply(waiting[t - 1])
-            quantise_w(g)
+            group_w(g)
             if g < last_pass:
-                waiting = [(g, start, HALF) for start in range(0, SLOTS, HALF)]
-                for unit in waiting:
-                    interleave(unit, planes[:, :, unit[1] : unit[1] + HALF])
+                for e in range(E):
+                    interleave((g, e - e % 2, 2), e, planes)
 
-        units = [(last_pass, e * C, C) for e in range(E)]
-        own = shared[:, : PLANES * C].rearrange("p (t c) -> p t c", t=PLANES)
-        interleave(units[0], planes[:, :, 0:C])
-        for t in range(PLANES):
-            gather(own[:, t], last_pass, t, last_expert * C, SLOTS)
-            if t == 1:
-                multiply(units[0])
+        held = w_raw_pool.tile([P, PASSES * E * K + 3 * HALF], U32, name="w_last", align_bytes=64)
+        w_codes = held[:, : PASSES * E * K]
+        held_codes = held[:, PASSES * E * K :]
+        interleave(units[4], 0, planes)
+        interleave(units[5], 1, planes)
+        interleave(units[6], 2, planes)
+        quantise_w(0, 1)
+        multiply(units[0], held_codes[:, :HALF])
+        quantise_w(1, PASSES)
+        multiply(units[2], held_codes[:, HALF : 2 * HALF])
+        multiply(units[1], held_codes[:, 2 * HALF :])
+        multiply(units[4], last_codes[:, :C])
+        multiply(units[5], last_codes[:, C:HALF])
+        nc.scalar.copy(out=first_result[:], in_=banks[0][:])
+        after_first = keep.tile([P, HALF], U32, name=f"grouped{last_pass}0", align_bytes=64)
+        multiply(units[3], after_first[:])
+        interleave(units[6], 3, planes)
+        multiply(units[6], last_codes[:, HALF:])
+        scatter(0, C, first_result[:])
+        other_results = planes[:, last_plane, C:]
         for e in range(1, E):
-            interleave(units[e], planes[:, :, e * C : (e + 1) * C] if e < last_expert else own)
-            finish(e - 1)
-            multiply(units[e])
-            scatter(e - 1)
-        finish(last_expert)
-        scatter(last_expert)
+            nc.scalar.copy(out=other_results[:, (e - 1) * C : e * C], in_=banks[e][:])
+        scatter(C, SLOTS, other_results)
         nc.sync.dma_start(out=out[:, : T // 2], in_=tokens[:, : T // 2])
         nc.scalar.dma_start(out=out[:, T // 2 :], in_=tokens[:, T // 2 :])

@@ -14,6 +14,8 @@ RUN = 4
 
 FIRST_CUTS = (0, 128, 384, 896, SLOTS)
 
+LAST_CUT = 704
+
 FLOPS = 2 * K * N * SLOTS
 BYTES = 4 * (N * T + E * N * K + SLOTS + K * T) + 2 * SLOTS
 
@@ -46,13 +48,11 @@ def tile_moe_bdx_lin_none_kernel(tc, dyT, w, gate, offs, out):
         tokens = keep.tile([P, T], F32, name="tokens")
         w_grouped = keep.tile([P, PASSES * E, K, PLANES], BF16, name="w_grouped", align_bytes=64)
         w_scales = keep.tile([P, PASSES * E * K], U8, name="w_scales", align_bytes=64)
-        units = [(g, e, 2) for g in range(last_pass) for e in (0, 2)]
-        units.extend([(last_pass, 0, 1), (last_pass, 1, 1), (last_pass, 2, 2)])
+        units = [(g, e, 2) for g in range(PASSES) for e in (0, 2)]
         grouped = {
             u: keep.tile([P, u[2] * C * PLANES], BF16, name=f"grouped{u[0]}{u[1]}", align_bytes=64) for u in units
         }
         scales = {u: keep.tile([P, u[2] * C], U8, name=f"scales{u[0]}{u[1]}", align_bytes=64) for u in units}
-        last_codes = keep.tile([P, SLOTS], U32, name="last_codes", align_bytes=64)
         first_result = keep.tile([P, C], F32, name="first_result")
         banks = [psum.tile([P, C], F32, name=f"bank{e}") for e in range(E)]
 
@@ -93,13 +93,13 @@ def tile_moe_bdx_lin_none_kernel(tc, dyT, w, gate, offs, out):
 
         def group_w(g):
             for e in range(E):
-                side_by_side(w_grouped[:, g * E + e], w_raw[g][:, e])
+                side_by_side(w_grouped[:, e * PASSES + g], w_raw[g][:, e])
 
         def quantise_w(first, last):
             nc.vector.quantize_mx(
-                out=w_codes[:, first * E * K : last * E * K].bitcast(E4M3),
-                scales=w_scales[:, first * E * K : last * E * K],
-                in_=w_grouped[:, first * E : last * E].rearrange("p e k t -> p (e k t)"),
+                out=w_codes[:, first * K : last * K].bitcast(E4M3),
+                scales=w_scales[:, first * K : last * K],
+                in_=w_grouped[:, first:last].rearrange("p e k t -> p (e k t)"),
             )
 
         def gather(plane, g, t, first, last):
@@ -110,23 +110,26 @@ def tile_moe_bdx_lin_none_kernel(tc, dyT, w, gate, offs, out):
                 mybir.AluOpType.mult,
             )
 
-        def interleave(unit, e, planes):
-            c = (e - unit[1]) * C
-            target = grouped[unit][:, c * PLANES : (c + C) * PLANES].rearrange("p (c t) -> p c t", t=PLANES)
-            side_by_side(target, planes[:, :, e * C : (e + 1) * C])
+        def interleave(g, first, last, planes):
+            unit = (g, first // HALF * 2, 2)
+            c = first % HALF
+            target = grouped[unit][:, c * PLANES : (c + last - first) * PLANES]
+            side_by_side(target.rearrange("p (c t) -> p c t", t=PLANES), planes[:, :, first:last])
 
-        def multiply(unit, codes):
-            g, first, count = unit
-            nc.vector.quantize_mx(out=codes.bitcast(E5M2), scales=scales[unit][:], in_=grouped[unit][:])
-            for e in range(first, first + count):
-                columns = slice((g * E + e) * K, (g * E + e + 1) * K)
-                slots = slice((e - first) * C, (e - first + 1) * C)
+        def quantise(unit):
+            nc.vector.quantize_mx(out=codes[unit].bitcast(E5M2), scales=scales[unit][:], in_=grouped[unit][:])
+
+        def multiply(e):
+            first = e - e % 2
+            slots = slice((e - first) * C, (e - first + 1) * C)
+            for g in range(PASSES):
+                columns = slice((e * PASSES + g) * K, (e * PASSES + g + 1) * K)
                 nc.tensor.matmul_mx(
                     out=banks[e][:],
                     lhsT=w_codes[:, columns].bitcast(E4M3),
                     lhsT_scale=w_scales[:, columns],
-                    rhs=codes[:, slots].bitcast(E5M2),
-                    rhs_scale=scales[unit][:, slots],
+                    rhs=codes[g, first, 2][:, slots].bitcast(E5M2),
+                    rhs_scale=scales[g, first, 2][:, slots],
                     start=(g == 0),
                     stop=(g == last_pass),
                 )
@@ -140,34 +143,31 @@ def tile_moe_bdx_lin_none_kernel(tc, dyT, w, gate, offs, out):
                 if (g, t) == (0, 0):
                     cuts = FIRST_CUTS
                 elif (g, t) == (last_pass, last_plane):
-                    cuts = (0, HALF, SLOTS)
+                    cuts = (0, LAST_CUT, SLOTS)
                 else:
                     cuts = (0, SLOTS)
                 for first, last in zip(cuts, cuts[1:]):
                     gather(planes[:, t, first:last], g, t, first, last)
             group_w(g)
             if g < last_pass:
-                for e in range(E):
-                    interleave((g, e - e % 2, 2), e, planes)
+                for first in (0, HALF):
+                    interleave(g, first, first + HALF, planes)
 
-        held = w_raw_pool.tile([P, PASSES * E * K + 3 * HALF], U32, name="w_last", align_bytes=64)
+        held = w_raw_pool.tile([P, PASSES * E * K + PASSES * SLOTS], U32, name="w_last", align_bytes=64)
         w_codes = held[:, : PASSES * E * K]
-        held_codes = held[:, PASSES * E * K :]
-        interleave(units[4], 0, planes)
-        interleave(units[5], 1, planes)
-        interleave(units[6], 2, planes)
-        quantise_w(0, 1)
-        multiply(units[0], held_codes[:, :HALF])
-        quantise_w(1, PASSES)
-        multiply(units[2], held_codes[:, HALF : 2 * HALF])
-        multiply(units[1], held_codes[:, 2 * HALF :])
-        multiply(units[4], last_codes[:, :C])
-        multiply(units[5], last_codes[:, C:HALF])
+        codes = {
+            u: held[:, PASSES * E * K + i * HALF : PASSES * E * K + (i + 1) * HALF] for i, u in enumerate(units)
+        }
+        for first, last in ((0, LAST_CUT), (LAST_CUT, HALF), (HALF, SLOTS)):
+            interleave(last_pass, first, last, planes)
+        quantise_w(0, 8)
+        for unit in units[:-1]:
+            quantise(unit)
+        quantise_w(8, PASSES * E)
+        quantise(units[-1])
+        for e in range(E):
+            multiply(e)
         nc.scalar.copy(out=first_result[:], in_=banks[0][:])
-        after_first = keep.tile([P, HALF], U32, name=f"grouped{last_pass}0", align_bytes=64)
-        multiply(units[3], after_first[:])
-        interleave(units[6], 3, planes)
-        multiply(units[6], last_codes[:, HALF:])
         scatter(0, C, first_result[:])
         other_results = planes[:, last_plane, C:]
         for e in range(1, E):

@@ -1,6 +1,7 @@
 from contextlib import ExitStack
 
 import concourse.mybir as mybir
+from concourse.masks import make_identity
 
 K, T, E, C, N = 128, 2048, 4, 512, 1536
 SLOTS = E * C
@@ -12,7 +13,8 @@ HALF = SLOTS // 2
 SPARE = 16
 RUN = 4
 
-FIRST_CUTS = (0, 128, 384, 896, SLOTS)
+FIRST_CUTS = (0, HALF, SLOTS)
+GATE_RUN = HALF // P
 
 LAST_CUT = 704
 
@@ -54,13 +56,12 @@ def tile_moe_bdx_lin_none_kernel(tc, dyT, w, gate, offs, out):
         }
         scales = {u: keep.tile([P, u[2] * C], U8, name=f"scales{u[0]}{u[1]}", align_bytes=64) for u in units}
         first_result = keep.tile([P, C], F32, name="first_result")
+        identity = keep.tile([P, P], F32, name="identity")
+        gate_runs = keep.tile([P, 2, GATE_RUN], F32, name="gate_runs")
         banks = [psum.tile([P, C], F32, name=f"bank{e}") for e in range(E)]
 
         dy = {}
         w_raw = {}
-
-        def load_gates(first, last):
-            nc.sync.dma_start(out=gates[:, first:last], in_=gate[0:P, first:last])
 
         def load_dy(g, t):
             dy[g, t] = dy_pool.tile([P, T + SPARE], F32, name="dy_block")
@@ -71,10 +72,9 @@ def tile_moe_bdx_lin_none_kernel(tc, dyT, w, gate, offs, out):
             w_raw[g] = w_raw_pool.tile([P, E, PLANES, K], F32, name=tag, align_bytes=64)
             nc.sync.dma_start(out=w_raw[g][:].rearrange("p e t k -> p e (t k)"), in_=w_rows[g])
 
+        nc.sync.dma_start(out=gate_runs[:], in_=gate[0].rearrange("(h p c) -> p h c", p=P, c=GATE_RUN))
         load_dy(0, 0)
         nc.sync.dma_start(out=offsets[:], in_=offs)
-        for first, last in zip(FIRST_CUTS, FIRST_CUTS[1:]):
-            load_gates(first, last)
         load_dy(0, 1)
         load_dy(0, 2)
         load_w(0)
@@ -84,6 +84,16 @@ def tile_moe_bdx_lin_none_kernel(tc, dyT, w, gate, offs, out):
                 load_dy(g, t)
                 if t == 1:
                     load_w(g)
+
+        make_identity(nc, identity[:])
+        for h in range(2):
+            half = gates[:, h * HALF : (h + 1) * HALF].rearrange("q (p c) -> q p c", c=GATE_RUN)
+            for first in range(0, GATE_RUN, RUN):
+                spread = psum.tile([P, RUN, P], F32, name=f"spread{h}{first}")
+                for c in range(RUN):
+                    column = gate_runs[:, h, first + c : first + c + 1]
+                    nc.tensor.transpose(spread[:, c], column.to_broadcast([P, P]), identity[:])
+                nc.scalar.copy(out=half[:, :, first : first + RUN], in_=spread[:].rearrange("q c p -> q p c"))
 
         def side_by_side(target, planes):
             nc.scalar.copy(

@@ -46,8 +46,8 @@ def tile_moe_bdx_lin_none_kernel(tc, dyT, w, gate, offs, out):
         psum = ctx.enter_context(tc.psum_pool(name="psum", bufs=1))
 
         offsets = lists.tile([P, SLOTS // OFFSETS], U16, name="offsets")
-        gates = keep.tile([P, SLOTS], F32, name="gates", align_bytes=64)
-        tokens = keep.tile([P, T], F32, name="tokens")
+        gates = keep.tile([P, SLOTS], F32, name="gates", align_bytes=256)
+        tokens = keep.tile([P, T], F32, name="tokens", align_bytes=256)
         w_grouped = keep.tile([P, PASSES * E, K, PLANES], BF16, name="w_grouped", align_bytes=64)
         w_scales = keep.tile([P, PASSES * E * K], U8, name="w_scales", align_bytes=64)
         units = [(g, e, 2) for g in range(PASSES) for e in (0, 2)]
@@ -64,7 +64,7 @@ def tile_moe_bdx_lin_none_kernel(tc, dyT, w, gate, offs, out):
         w_raw = {}
 
         def load_dy(g, t):
-            dy[g, t] = dy_pool.tile([P, T + SPARE], F32, name="dy_block")
+            dy[g, t] = dy_pool.tile([P, T + SPARE], F32, name="dy_block", align_bytes=256)
             nc.sync.dma_start(out=dy[g, t][:, :T], in_=dy_rows[g, t])
 
         def load_w(g):
@@ -148,7 +148,7 @@ def tile_moe_bdx_lin_none_kernel(tc, dyT, w, gate, offs, out):
             nc.vector.tensor_copy(tokens[:].indirect(offsets[:, first // OFFSETS : last // OFFSETS]), values)
 
         for g in range(PASSES):
-            planes = pass_pool.tile([P, PLANES, SLOTS], F32, name="gathered_planes", align_bytes=64)
+            planes = pass_pool.tile([P, PLANES, SLOTS], F32, name="gathered_planes", align_bytes=256)
             for t in range(PLANES):
                 if (g, t) == (0, 0):
                     cuts = FIRST_CUTS

@@ -65,7 +65,9 @@ def tile_moe_bdx_lin_none_kernel(tc, dyT, w, gate, offs, out):
 
         def load_dy(g, t):
             dy[g, t] = dy_pool.tile([P, T + SPARE], F32, name="dy_block", align_bytes=256)
-            nc.sync.dma_start(out=dy[g, t][:, :T], in_=dy_rows[g, t])
+            cuts = (0, HALF, T) if (g, t) == (0, 0) else (0, T)
+            for first, last in zip(cuts, cuts[1:]):
+                nc.sync.dma_start(out=dy[g, t][:, first:last], in_=dy_rows[g, t][:, first:last])
 
         def load_w(g):
             tag = "w_last" if g == last_pass else "w_block"
@@ -183,5 +185,5 @@ def tile_moe_bdx_lin_none_kernel(tc, dyT, w, gate, offs, out):
         for e in range(1, E):
             nc.scalar.copy(out=other_results[:, (e - 1) * C : e * C], in_=banks[e][:])
         scatter(C, SLOTS, other_results)
-        nc.sync.dma_start(out=out[:, : T // 2], in_=tokens[:, : T // 2])
-        nc.scalar.dma_start(out=out[:, T // 2 :], in_=tokens[:, T // 2 :])
+        for q, queue in enumerate((nc.sync, nc.scalar, nc.sync, nc.scalar)):
+            queue.dma_start(out=out[:, q * C : (q + 1) * C], in_=tokens[:, q * C : (q + 1) * C])

@@ -12,11 +12,10 @@ OFFSETS = 16
 HALF = SLOTS // 2
 SPARE = 16
 RUN = 4
-
-FIRST_CUTS = (0, HALF, SLOTS)
 GATE_RUN = HALF // P
+PIECE = 256
 
-LAST_CUT = 704
+CUTS = (HALF, 3 * C, SLOTS - PIECE)
 
 FLOPS = 2 * K * N * SLOTS
 BYTES = 4 * (N * T + E * N * K + SLOTS + K * T) + 2 * SLOTS
@@ -28,37 +27,36 @@ U16 = mybir.dt.uint16
 U8 = mybir.dt.uint8
 E4M3 = mybir.dt.float8_e4m3fn_x4
 E5M2 = mybir.dt.float8_e5m2_x4
+MULT = mybir.AluOpType.mult
+COPY = mybir.ActivationFunctionType.Copy
 
 
 def tile_moe_bdx_lin_none_kernel(tc, dyT, w, gate, offs, out):
     nc = tc.nc
     dy_rows = dyT.rearrange("(g p t) c -> g t p c", p=P, t=PLANES)
-    w_rows = w.rearrange("e (g p t) k -> g p e (t k)", p=P, t=PLANES)
-    last_pass = PASSES - 1
-    last_plane = PLANES - 1
+    w_rows = w.rearrange("e (g p t) k -> e p g (t k)", p=P, t=PLANES)
 
     with ExitStack() as ctx:
         lists = ctx.enter_context(tc.tile_pool(name="lists", bufs=1))
         keep = ctx.enter_context(tc.tile_pool(name="keep", bufs=1))
-        dy_pool = ctx.enter_context(tc.tile_pool(name="dy_pool", bufs=6))
-        w_raw_pool = ctx.enter_context(tc.tile_pool(name="w_raw_pool", bufs=1))
-        pass_pool = ctx.enter_context(tc.tile_pool(name="pass_pool", bufs=2))
+        dy_pool = ctx.enter_context(tc.tile_pool(name="dy_pool", bufs=2 * PLANES))
+        w_pool = ctx.enter_context(tc.tile_pool(name="w_pool", bufs=2))
+        grouped_pool = ctx.enter_context(tc.tile_pool(name="grouped_pool", bufs=3))
         psum = ctx.enter_context(tc.psum_pool(name="psum", bufs=1))
 
         offsets = lists.tile([P, SLOTS // OFFSETS], U16, name="offsets")
-        gates = keep.tile([P, SLOTS], F32, name="gates", align_bytes=256)
+        gates = [keep.tile([P, HALF], F32, name=f"gates{h}", align_bytes=256) for h in range(2)]
         tokens = keep.tile([P, T], F32, name="tokens", align_bytes=256)
-        w_grouped = keep.tile([P, PASSES * E, K, PLANES], BF16, name="w_grouped", align_bytes=64)
-        w_scales = keep.tile([P, PASSES * E * K], U8, name="w_scales", align_bytes=64)
-        units = [(g, e, 2) for g in range(PASSES) for e in (0, 2)]
-        grouped = {
-            u: keep.tile([P, u[2] * C * PLANES], BF16, name=f"grouped{u[0]}{u[1]}", align_bytes=64) for u in units
-        }
-        scales = {u: keep.tile([P, u[2] * C], U8, name=f"scales{u[0]}{u[1]}", align_bytes=64) for u in units}
-        first_result = keep.tile([P, C], F32, name="first_result")
+        results = keep.tile([P, SLOTS], F32, name="results", align_bytes=256)
+        narrow = keep.tile([P, PLANES, HALF], F32, name="narrow", align_bytes=256)
+        wide = keep.tile([P, PLANES, CUTS[1]], F32, name="wide", align_bytes=256)
+        gated = keep.tile([P, PLANES, HALF], F32, name="gated", align_bytes=256)
+        codes = keep.tile([P, PASSES, SLOTS], U32, name="codes", align_bytes=64)
+        scales = keep.tile([P, PASSES, SLOTS], U8, name="scales", align_bytes=64)
+        w_codes = keep.tile([P, E, PASSES * K], U32, name="w_codes", align_bytes=64)
+        w_scales = keep.tile([P, E, PASSES * K], U8, name="w_scales", align_bytes=64)
         identity = keep.tile([P, P], F32, name="identity")
-        gate_runs = keep.tile([P, 2, GATE_RUN], F32, name="gate_runs")
-        banks = [psum.tile([P, C], F32, name=f"bank{e}") for e in range(E)]
+        gate_runs = keep.tile([P, GATE_RUN], F32, name="gate_runs")
 
         dy = {}
         w_raw = {}
@@ -69,121 +67,129 @@ def tile_moe_bdx_lin_none_kernel(tc, dyT, w, gate, offs, out):
             for first, last in zip(cuts, cuts[1:]):
                 nc.sync.dma_start(out=dy[g, t][:, first:last], in_=dy_rows[g, t][:, first:last])
 
-        def load_w(g):
-            tag = "w_last" if g == last_pass else "w_block"
-            w_raw[g] = w_raw_pool.tile([P, E, PLANES, K], F32, name=tag, align_bytes=64)
-            nc.sync.dma_start(out=w_raw[g][:].rearrange("p e t k -> p e (t k)"), in_=w_rows[g])
-
-        nc.sync.dma_start(out=gate_runs[:], in_=gate[0].rearrange("(h p c) -> p h c", p=P, c=GATE_RUN))
-        load_dy(0, 0)
-        nc.sync.dma_start(out=offsets[:], in_=offs)
-        load_dy(0, 1)
-        load_dy(0, 2)
-        load_w(0)
-        load_dy(0, 3)
-        for g in range(1, PASSES):
+        nc.sync.dma_start(out=gate_runs[:], in_=gate[0, HALF:].rearrange("(p c) -> p c", c=GATE_RUN))
+        for g in range(PASSES):
             for t in range(PLANES):
                 load_dy(g, t)
-                if t == 1:
-                    load_w(g)
+                if (g, t) == (0, 0):
+                    nc.sync.dma_start(out=offsets[:], in_=offs)
+                if (g, t) == (1, 0):
+                    nc.sync.dma_start(out=gates[0][:], in_=gate[:P, :HALF])
+        for e in range(E):
+            w_raw[e] = w_pool.tile([P, PASSES, PLANES, K], F32, name="w_raw", align_bytes=64)
+            nc.sync.dma_start(out=w_raw[e][:].rearrange("p g t k -> p g (t k)"), in_=w_rows[e])
 
         make_identity(nc, identity[:])
-        for h in range(2):
-            half = gates[:, h * HALF : (h + 1) * HALF].rearrange("q (p c) -> q p c", c=GATE_RUN)
-            for first in range(0, GATE_RUN, RUN):
-                spread = psum.tile([P, RUN, P], F32, name=f"spread{h}{first}")
-                for c in range(RUN):
-                    column = gate_runs[:, h, first + c : first + c + 1]
-                    nc.tensor.transpose(spread[:, c], column.to_broadcast([P, P]), identity[:])
-                nc.scalar.copy(out=half[:, :, first : first + RUN], in_=spread[:].rearrange("q c p -> q p c"))
+        second_half = gates[1][:].rearrange("q (p c) -> q p c", c=GATE_RUN)
+        for first in range(0, GATE_RUN, RUN):
+            spread = psum.tile([P, RUN, P], F32, name=f"spread{first}")
+            for c in range(RUN):
+                column = gate_runs[:, first + c : first + c + 1]
+                nc.tensor.transpose(spread[:, c], column.to_broadcast([P, P]), identity[:])
+            nc.vector.tensor_copy(second_half[:, :, first : first + RUN], spread[:].rearrange("q c p -> q p c"))
 
-        def side_by_side(target, planes):
-            nc.scalar.copy(
-                out=target.rearrange("p (c i) t -> p c t i", i=RUN),
-                in_=planes.rearrange("p t (c i) -> p c t i", i=RUN),
-            )
+        def gate_of(first, last):
+            return gates[first // HALF][:, first % HALF : first % HALF + last - first]
 
-        def group_w(g):
-            for e in range(E):
-                side_by_side(w_grouped[:, e * PASSES + g], w_raw[g][:, e])
+        def listed(tile, first, last):
+            return tile[:].indirect(offsets[:, first // OFFSETS : last // OFFSETS])
 
-        def quantise_w(first, last):
-            nc.vector.quantize_mx(
-                out=w_codes[:, first * K : last * K].bitcast(E4M3),
-                scales=w_scales[:, first * K : last * K],
-                in_=w_grouped[:, first:last].rearrange("p e k t -> p (e k t)"),
-            )
-
-        def gather(plane, g, t, first, last):
-            nc.vector.tensor_tensor(
-                plane,
-                dy[g, t][:].indirect(offsets[:, first // OFFSETS : last // OFFSETS]),
-                gates[:, first:last],
-                mybir.AluOpType.mult,
-            )
-
-        def interleave(g, first, last, planes):
-            unit = (g, first // HALF * 2, 2)
-            c = first % HALF
-            target = grouped[unit][:, c * PLANES : (c + last - first) * PLANES]
-            side_by_side(target.rearrange("p (c t) -> p c t", t=PLANES), planes[:, :, first:last])
-
-        def quantise(unit):
-            nc.vector.quantize_mx(out=codes[unit].bitcast(E5M2), scales=scales[unit][:], in_=grouped[unit][:])
-
-        def multiply(e):
-            first = e - e % 2
-            slots = slice((e - first) * C, (e - first + 1) * C)
-            for g in range(PASSES):
-                columns = slice((e * PASSES + g) * K, (e * PASSES + g + 1) * K)
-                nc.tensor.matmul_mx(
-                    out=banks[e][:],
-                    lhsT=w_codes[:, columns].bitcast(E4M3),
-                    lhsT_scale=w_scales[:, columns],
-                    rhs=codes[g, first, 2][:, slots].bitcast(E5M2),
-                    rhs_scale=scales[g, first, 2][:, slots],
-                    start=(g == 0),
-                    stop=(g == last_pass),
-                )
-
-        def scatter(first, last, values):
-            nc.vector.tensor_copy(tokens[:].indirect(offsets[:, first // OFFSETS : last // OFFSETS]), values)
-
-        for g in range(PASSES):
-            planes = pass_pool.tile([P, PLANES, SLOTS], F32, name="gathered_planes", align_bytes=256)
+        def gather_plain(planes, g, first, last):
             for t in range(PLANES):
-                if (g, t) == (0, 0):
-                    cuts = FIRST_CUTS
-                elif (g, t) == (last_pass, last_plane):
-                    cuts = (0, LAST_CUT, SLOTS)
-                else:
-                    cuts = (0, SLOTS)
-                for first, last in zip(cuts, cuts[1:]):
-                    gather(planes[:, t, first:last], g, t, first, last)
-            group_w(g)
-            if g < last_pass:
-                for first in (0, HALF):
-                    interleave(g, first, first + HALF, planes)
+                nc.scalar.activation(planes[:, t], listed(dy[g, t], first, last), COPY)
 
-        held = w_raw_pool.tile([P, PASSES * E * K + PASSES * SLOTS], U32, name="w_last", align_bytes=64)
-        w_codes = held[:, : PASSES * E * K]
-        codes = {
-            u: held[:, PASSES * E * K + i * HALF : PASSES * E * K + (i + 1) * HALF] for i, u in enumerate(units)
-        }
-        for first, last in ((0, LAST_CUT), (LAST_CUT, HALF), (HALF, SLOTS)):
-            interleave(last_pass, first, last, planes)
-        quantise_w(0, 8)
-        for unit in units[:-1]:
-            quantise(unit)
-        quantise_w(8, PASSES * E)
-        quantise(units[-1])
+        def gather_gated(planes, g, first, last):
+            for t in range(PLANES):
+                nc.vector.tensor_tensor(planes[:, t], listed(dy[g, t], first, last), gate_of(first, last), MULT)
+
+        def grouped_tile(width):
+            grouped = grouped_pool.tile([P, HALF * PLANES], BF16, name="grouped", align_bytes=64)
+            return grouped[:, : width * PLANES]
+
+        def weave(planes):
+            grouped = grouped_tile(planes.shape[2])
+            nc.vector.tensor_copy(
+                grouped.rearrange("p (c i t) -> p c t i", i=RUN, t=PLANES),
+                planes.rearrange("p t (c i) -> p c t i", i=RUN),
+            )
+            return grouped
+
+        def weave_gating(planes, first, last):
+            grouped = grouped_tile(last - first)
+            factor = gate_of(first, last).rearrange("p (c i) -> p c i", i=RUN).unsqueeze(2)
+            nc.vector.tensor_tensor(
+                grouped.rearrange("p (c i t) -> p c t i", i=RUN, t=PLANES),
+                planes.rearrange("p t (c i) -> p c t i", i=RUN),
+                factor.to_broadcast([P, (last - first) // RUN, PLANES, RUN]),
+                MULT,
+            )
+            return grouped
+
+        def quantise(grouped, g, first, last):
+            nc.vector.quantize_mx(
+                out=codes[:, g, first:last].bitcast(E5M2), scales=scales[:, g, first:last], in_=grouped
+            )
+
+        def weave_w(e):
+            grouped = w_pool.tile([P, PASSES * K * PLANES], BF16, name="w_grouped", align_bytes=64)
+            nc.vector.tensor_copy(
+                grouped[:].rearrange("p (g c i t) -> p c g t i", g=PASSES, i=RUN, t=PLANES),
+                w_raw[e][:].rearrange("p g t (c i) -> p c g t i", i=RUN),
+            )
+            return grouped[:]
+
+        def quantise_w(grouped, e):
+            nc.vector.quantize_mx(out=w_codes[:, e].bitcast(E4M3), scales=w_scales[:, e], in_=grouped)
+
+        def finish(first, last):
+            e = first // C
+            bank = psum.tile([P, last - first], F32, name=f"bank{first}")
+            for g in range(PASSES):
+                nc.tensor.matmul_mx(
+                    out=bank[:],
+                    lhsT=w_codes[:, e, g * K : (g + 1) * K].bitcast(E4M3),
+                    lhsT_scale=w_scales[:, e, g * K : (g + 1) * K],
+                    rhs=codes[:, g, first:last].bitcast(E5M2),
+                    rhs_scale=scales[:, g, first:last],
+                    start=(g == 0),
+                    stop=(g == PASSES - 1),
+                )
+            nc.scalar.copy(out=results[:, first:last], in_=bank[:])
+            for start in range(first, last, PIECE):
+                nc.scalar.activation(listed(tokens, start, start + PIECE), results[:, start : start + PIECE], COPY)
+
+        gather_plain(narrow, 0, 0, HALF)
+        gather_gated(gated, 0, HALF, SLOTS)
+        upper = weave(gated[:])
+        lower = weave_gating(narrow[:], 0, HALF)
+        quantise(upper, 0, HALF, SLOTS)
+        quantise(lower, 0, 0, HALF)
+
+        cut = CUTS[1]
+        gather_plain(wide, 1, 0, cut)
+        gather_gated(gated[:, :, : SLOTS - cut], 1, cut, SLOTS)
+        upper = weave(gated[:, :, : SLOTS - cut])
+        lower = weave_gating(wide[:, :, :HALF], 0, HALF)
+        quantise(upper, 1, cut, SLOTS)
+        middle = weave_gating(wide[:, :, HALF:cut], HALF, cut)
+        quantise(lower, 1, 0, HALF)
+        quantise(middle, 1, HALF, cut)
+
+        cut = CUTS[2]
+        gather_plain(narrow, 2, 0, HALF)
+        late = wide[:, :, CUTS[1] - (cut - HALF) :]
+        gather_plain(late, 2, HALF, cut)
         for e in range(E):
-            multiply(e)
-        nc.scalar.copy(out=first_result[:], in_=banks[0][:])
-        scatter(0, C, first_result[:])
-        other_results = planes[:, last_plane, C:]
-        for e in range(1, E):
-            nc.scalar.copy(out=other_results[:, (e - 1) * C : e * C], in_=banks[e][:])
-        scatter(C, SLOTS, other_results)
+            first, last = e * C, min((e + 1) * C, cut)
+            planes = narrow[:, :, first:last] if first < HALF else late[:, :, first - HALF : last - HALF]
+            w_grouped = weave_w(e)
+            grouped = weave_gating(planes, first, last)
+            quantise_w(w_grouped, e)
+            quantise(grouped, 2, first, last)
+            finish(first, last)
+        gather_gated(gated[:, :, : SLOTS - cut], 2, cut, SLOTS)
+        quantise(weave(gated[:, :, : SLOTS - cut]), 2, cut, SLOTS)
+        finish(cut, SLOTS)
+
         for q, queue in enumerate((nc.sync, nc.scalar, nc.sync, nc.scalar)):
             queue.dma_start(out=out[:, q * C : (q + 1) * C], in_=tokens[:, q * C : (q + 1) * C])

@@ -15,7 +15,8 @@ RUN = 4
 GATE_RUN = HALF // P
 PIECE = 256
 
-CUTS = (HALF, 3 * C, SLOTS - PIECE)
+CUT = 1024
+BLOCK_BYTES = 8448
 
 FLOPS = 2 * K * N * SLOTS
 BYTES = 4 * (N * T + E * N * K + SLOTS + K * T) + 2 * SLOTS
@@ -39,7 +40,7 @@ def tile_moe_bdx_lin_none_kernel(tc, dyT, w, gate, offs, out):
     with ExitStack() as ctx:
         lists = ctx.enter_context(tc.tile_pool(name="lists", bufs=1))
         keep = ctx.enter_context(tc.tile_pool(name="keep", bufs=1))
-        dy_pool = ctx.enter_context(tc.tile_pool(name="dy_pool", bufs=2 * PLANES))
+        dy_pool = ctx.enter_context(tc.tile_pool(name="dy_pool", bufs=1))
         w_pool = ctx.enter_context(tc.tile_pool(name="w_pool", bufs=2))
         grouped_pool = ctx.enter_context(tc.tile_pool(name="grouped_pool", bufs=3))
         psum = ctx.enter_context(tc.psum_pool(name="psum", bufs=1))
@@ -48,8 +49,8 @@ def tile_moe_bdx_lin_none_kernel(tc, dyT, w, gate, offs, out):
         gates = [keep.tile([P, HALF], F32, name=f"gates{h}", align_bytes=256) for h in range(2)]
         tokens = keep.tile([P, T], F32, name="tokens", align_bytes=256)
         results = keep.tile([P, SLOTS], F32, name="results", align_bytes=256)
-        narrow = keep.tile([P, PLANES, HALF], F32, name="narrow", align_bytes=256)
-        wide = keep.tile([P, PLANES, CUTS[1]], F32, name="wide", align_bytes=256)
+        outer = [keep.tile([P, PLANES, HALF], F32, name=f"outer{h}", align_bytes=256) for h in range(2)]
+        inner = keep.tile([P, PLANES, CUT], F32, name="inner", align_bytes=256)
         gated = keep.tile([P, PLANES, HALF], F32, name="gated", align_bytes=256)
         codes = keep.tile([P, PASSES, SLOTS], U32, name="codes", align_bytes=64)
         scales = keep.tile([P, PASSES, SLOTS], U8, name="scales", align_bytes=64)
@@ -61,20 +62,27 @@ def tile_moe_bdx_lin_none_kernel(tc, dyT, w, gate, offs, out):
         dy = {}
         w_raw = {}
 
-        def load_dy(g, t):
-            dy[g, t] = dy_pool.tile([P, T + SPARE], F32, name="dy_block", align_bytes=256)
-            cuts = (0, HALF, T) if (g, t) == (0, 0) else (0, T)
-            for first, last in zip(cuts, cuts[1:]):
-                nc.sync.dma_start(out=dy[g, t][:, first:last], in_=dy_rows[g, t][:, first:last])
+        def load_dy(g, t, first, last):
+            if first == 0:
+                place = (g * PLANES + t) % (2 * PLANES) * BLOCK_BYTES
+                dy[g, t] = dy_pool.tile([P, T + SPARE], F32, name=f"dy{g}{t}", offset=place, align_bytes=256)[:]
+            nc.sync.dma_start(out=dy[g, t][:, first:last], in_=dy_rows[g, t][:, first:last])
 
         nc.sync.dma_start(out=gate_runs[:], in_=gate[0, HALF:].rearrange("(p c) -> p c", c=GATE_RUN))
-        for g in range(PASSES):
-            for t in range(PLANES):
-                load_dy(g, t)
-                if (g, t) == (0, 0):
-                    nc.sync.dma_start(out=offsets[:], in_=offs)
-                if (g, t) == (1, 0):
-                    nc.sync.dma_start(out=gates[0][:], in_=gate[:P, :HALF])
+        load_dy(0, 0, 0, HALF)
+        load_dy(0, 0, HALF, T)
+        nc.sync.dma_start(out=offsets[:], in_=offs)
+        for t in range(1, PLANES):
+            load_dy(0, t, 0, T)
+        load_dy(1, 0, 0, T)
+        nc.sync.dma_start(out=gates[0][:], in_=gate[:P, :HALF])
+        for t in range(1, PLANES):
+            load_dy(1, t, 0, T)
+        load_dy(2, 0, 0, T)
+        load_dy(2, 1, 0, T)
+        pair = dy_pool.tile([P, 2, T], F32, name="dy_pair", offset=2 * BLOCK_BYTES, align_bytes=256)
+        nc.sync.dma_start(out=pair[:], in_=dyT.rearrange("(g p t) c -> g p t c", p=P, t=PLANES)[2, :, 2:])
+        dy[2, 2], dy[2, 3] = pair[:, 0], pair[:, 1]
         for e in range(E):
             w_raw[e] = w_pool.tile([P, PASSES, PLANES, K], F32, name="w_raw", align_bytes=64)
             nc.sync.dma_start(out=w_raw[e][:].rearrange("p g t k -> p g (t k)"), in_=w_rows[e])
@@ -91,11 +99,11 @@ def tile_moe_bdx_lin_none_kernel(tc, dyT, w, gate, offs, out):
         def gate_of(first, last):
             return gates[first // HALF][:, first % HALF : first % HALF + last - first]
 
-        def listed(tile, first, last):
-            return tile[:].indirect(offsets[:, first // OFFSETS : last // OFFSETS])
+        def listed(window, first, last):
+            return window.indirect(offsets[:, first // OFFSETS : last // OFFSETS])
 
-        def gather_plain(planes, g, first, last):
-            for t in range(PLANES):
+        def gather_plain(planes, g, which, first, last):
+            for t in which:
                 nc.scalar.activation(planes[:, t], listed(dy[g, t], first, last), COPY)
 
         def gather_gated(planes, g, first, last):
@@ -106,16 +114,13 @@ def tile_moe_bdx_lin_none_kernel(tc, dyT, w, gate, offs, out):
             grouped = grouped_pool.tile([P, HALF * PLANES], BF16, name="grouped", align_bytes=64)
             return grouped[:, : width * PLANES]
 
-        def weave(planes):
-            grouped = grouped_tile(planes.shape[2])
+        def weave(grouped, planes):
             nc.vector.tensor_copy(
                 grouped.rearrange("p (c i t) -> p c t i", i=RUN, t=PLANES),
                 planes.rearrange("p t (c i) -> p c t i", i=RUN),
             )
-            return grouped
 
-        def weave_gating(planes, first, last):
-            grouped = grouped_tile(last - first)
+        def weave_gating(grouped, planes, first, last):
             factor = gate_of(first, last).rearrange("p (c i) -> p c i", i=RUN).unsqueeze(2)
             nc.vector.tensor_tensor(
                 grouped.rearrange("p (c i t) -> p c t i", i=RUN, t=PLANES),
@@ -123,7 +128,6 @@ def tile_moe_bdx_lin_none_kernel(tc, dyT, w, gate, offs, out):
                 factor.to_broadcast([P, (last - first) // RUN, PLANES, RUN]),
                 MULT,
             )
-            return grouped
 
         def quantise(grouped, g, first, last):
             nc.vector.quantize_mx(
@@ -156,40 +160,54 @@ def tile_moe_bdx_lin_none_kernel(tc, dyT, w, gate, offs, out):
                 )
             nc.scalar.copy(out=results[:, first:last], in_=bank[:])
             for start in range(first, last, PIECE):
-                nc.scalar.activation(listed(tokens, start, start + PIECE), results[:, start : start + PIECE], COPY)
+                nc.scalar.activation(listed(tokens[:], start, start + PIECE), results[:, start : start + PIECE], COPY)
 
-        gather_plain(narrow, 0, 0, HALF)
+        gather_plain(outer[0], 0, range(PLANES), 0, HALF)
         gather_gated(gated, 0, HALF, SLOTS)
-        upper = weave(gated[:])
-        lower = weave_gating(narrow[:], 0, HALF)
+        upper = grouped_tile(HALF)
+        weave(upper, gated[:])
+        lower = grouped_tile(HALF)
+        weave_gating(lower, outer[0][:], 0, HALF)
         quantise(upper, 0, HALF, SLOTS)
         quantise(lower, 0, 0, HALF)
 
-        cut = CUTS[1]
-        gather_plain(wide, 1, 0, cut)
+        cut = CUT
+        gather_plain(inner, 1, range(PLANES), 0, cut)
         gather_gated(gated[:, :, : SLOTS - cut], 1, cut, SLOTS)
-        upper = weave(gated[:, :, : SLOTS - cut])
-        lower = weave_gating(wide[:, :, :HALF], 0, HALF)
-        quantise(upper, 1, cut, SLOTS)
-        middle = weave_gating(wide[:, :, HALF:cut], HALF, cut)
+        lower = grouped_tile(HALF)
+        weave_gating(lower, inner[:, :, :HALF], 0, HALF)
         quantise(lower, 1, 0, HALF)
-        quantise(middle, 1, HALF, cut)
 
-        cut = CUTS[2]
-        gather_plain(narrow, 2, 0, HALF)
-        late = wide[:, :, CUTS[1] - (cut - HALF) :]
-        gather_plain(late, 2, HALF, cut)
+        def rest_of_pass_1(e):
+            first, last = e * C, (e + 1) * C
+            middle = min(max(first, cut), last)
+            grouped = grouped_tile(C)
+            if first < middle:
+                weave_gating(grouped[:, : (middle - first) * PLANES], inner[:, :, first:middle], first, middle)
+            weave(grouped[:, (middle - first) * PLANES :], gated[:, :, middle - cut : last - cut])
+            return grouped
+
+        for t in range(PLANES // 2):
+            for h in range(2):
+                gather_plain(outer[h], 2, [t], h * HALF, (h + 1) * HALF)
+        for h in range(2):
+            gather_plain(outer[h], 2, [PLANES - 2], h * HALF, (h + 1) * HALF)
+            for first in (0, C):
+                gather_plain(outer[h][:, :, first : first + C], 2, [PLANES - 1], h * HALF + first, h * HALF + first + C)
         for e in range(E):
-            first, last = e * C, min((e + 1) * C, cut)
-            planes = narrow[:, :, first:last] if first < HALF else late[:, :, first - HALF : last - HALF]
+            first, last = e * C, (e + 1) * C
+            rest = rest_of_pass_1(e) if first >= HALF else None
             w_grouped = weave_w(e)
-            grouped = weave_gating(planes, first, last)
-            quantise_w(w_grouped, e)
-            quantise(grouped, 2, first, last)
-            finish(first, last)
-        gather_gated(gated[:, :, : SLOTS - cut], 2, cut, SLOTS)
-        quantise(weave(gated[:, :, : SLOTS - cut]), 2, cut, SLOTS)
-        finish(cut, SLOTS)
+            if rest is not None:
+                quantise(rest, 1, first, last)
+            ends = (first, last) if e < E - 1 else (first, last - PIECE, last)
+            for start, end in zip(ends, ends[1:]):
+                grouped = grouped_tile(end - start)
+                weave_gating(grouped, outer[start // HALF][:, :, start % HALF : start % HALF + end - start], start, end)
+                if start == first:
+                    quantise_w(w_grouped, e)
+                quantise(grouped, 2, start, end)
+                finish(start, end)
 
         for q, queue in enumerate((nc.sync, nc.scalar, nc.sync, nc.scalar)):
             queue.dma_start(out=out[:, q * C : (q + 1) * C], in_=tokens[:, q * C : (q + 1) * C])

@@ -12,10 +12,8 @@ OFFSETS = 16
 HALF = SLOTS // 2
 SPARE = 16
 RUN = 4
-GATE_RUN = HALF // P
 PIECE = 256
 
-CUT = 1024
 BLOCK_BYTES = 8448
 
 FLOPS = 2 * K * N * SLOTS
@@ -41,63 +39,66 @@ def tile_moe_bdx_lin_none_kernel(tc, dyT, w, gate, offs, out):
         lists = ctx.enter_context(tc.tile_pool(name="lists", bufs=1))
         keep = ctx.enter_context(tc.tile_pool(name="keep", bufs=1))
         dy_pool = ctx.enter_context(tc.tile_pool(name="dy_pool", bufs=1))
-        w_pool = ctx.enter_context(tc.tile_pool(name="w_pool", bufs=2))
-        grouped_pool = ctx.enter_context(tc.tile_pool(name="grouped_pool", bufs=3))
         psum = ctx.enter_context(tc.psum_pool(name="psum", bufs=1))
 
         offsets = lists.tile([P, SLOTS // OFFSETS], U16, name="offsets")
-        gates = [keep.tile([P, HALF], F32, name=f"gates{h}", align_bytes=256) for h in range(2)]
+        gates = keep.tile([P, HALF], F32, name="gates", align_bytes=256)
         tokens = keep.tile([P, T], F32, name="tokens", align_bytes=256)
         results = keep.tile([P, SLOTS], F32, name="results", align_bytes=256)
         outer = [keep.tile([P, PLANES, HALF], F32, name=f"outer{h}", align_bytes=256) for h in range(2)]
-        inner = keep.tile([P, PLANES, CUT], F32, name="inner", align_bytes=256)
+        inner = keep.tile([P, PLANES, HALF], F32, name="inner", align_bytes=256)
         gated = keep.tile([P, PLANES, HALF], F32, name="gated", align_bytes=256)
+        woven = keep.tile([P, 4 * C * PLANES], BF16, name="woven", align_bytes=64)
         codes = keep.tile([P, PASSES, SLOTS], U32, name="codes", align_bytes=64)
         scales = keep.tile([P, PASSES, SLOTS], U8, name="scales", align_bytes=64)
         w_codes = keep.tile([P, E, PASSES * K], U32, name="w_codes", align_bytes=64)
         w_scales = keep.tile([P, E, PASSES * K], U8, name="w_scales", align_bytes=64)
         identity = keep.tile([P, P], F32, name="identity")
-        gate_runs = keep.tile([P, GATE_RUN], F32, name="gate_runs")
+        gate_runs = [keep.tile([P, 2, 2 * RUN], F32, name=f"gate_runs{h}") for h in range(2)]
+        gate_banks = [psum.tile([P, RUN, P], F32, name=f"gate_bank{e}") for e in range(E)]
 
         dy = {}
         w_raw = {}
 
         def load_dy(g, t, first, last):
             if first == 0:
-                place = (g * PLANES + t) % (2 * PLANES) * BLOCK_BYTES
+                place = (g * PLANES + t) * BLOCK_BYTES
                 dy[g, t] = dy_pool.tile([P, T + SPARE], F32, name=f"dy{g}{t}", offset=place, align_bytes=256)[:]
             nc.sync.dma_start(out=dy[g, t][:, first:last], in_=dy_rows[g, t][:, first:last])
 
-        nc.sync.dma_start(out=gate_runs[:], in_=gate[0, HALF:].rearrange("(p c) -> p c", c=GATE_RUN))
+        def load_w(e):
+            w_raw[e] = dy_pool.tile([P, PASSES * PLANES * K], F32, name=f"w_raw{e}", offset=e * BLOCK_BYTES, align_bytes=256)
+            nc.sync.dma_start(out=w_raw[e][:].rearrange("p (g x) -> p g x", g=PASSES), in_=w_rows[e])
+
+        def load_gate(h):
+            half = gate[0, h * HALF : (h + 1) * HALF]
+            nc.sync.dma_start(out=gate_runs[h][:, :, :RUN], in_=half.rearrange("(e p c) -> p e c", p=P, c=RUN))
+
+        load_gate(1)
         load_dy(0, 0, 0, HALF)
         load_dy(0, 0, HALF, T)
         nc.sync.dma_start(out=offsets[:], in_=offs)
-        for t in range(1, PLANES):
-            load_dy(0, t, 0, T)
-        load_dy(1, 0, 0, T)
-        nc.sync.dma_start(out=gates[0][:], in_=gate[:P, :HALF])
-        for t in range(1, PLANES):
-            load_dy(1, t, 0, T)
-        load_dy(2, 0, 0, T)
-        load_dy(2, 1, 0, T)
-        pair = dy_pool.tile([P, 2, T], F32, name="dy_pair", offset=2 * BLOCK_BYTES, align_bytes=256)
+        load_dy(0, 1, 0, T)
+        load_gate(0)
+        for block in range(2, PASSES * PLANES - 2):
+            load_dy(block // PLANES, block % PLANES, 0, T)
+        load_w(0)
+        pair = dy_pool.tile([P, 2, T], F32, name="dy_pair", offset=(PASSES * PLANES - 2) * BLOCK_BYTES, align_bytes=256)
         nc.sync.dma_start(out=pair[:], in_=dyT.rearrange("(g p t) c -> g p t c", p=P, t=PLANES)[2, :, 2:])
         dy[2, 2], dy[2, 3] = pair[:, 0], pair[:, 1]
-        for e in range(E):
-            w_raw[e] = w_pool.tile([P, PASSES, PLANES, K], F32, name="w_raw", align_bytes=64)
-            nc.sync.dma_start(out=w_raw[e][:].rearrange("p g t k -> p g (t k)"), in_=w_rows[e])
+        for e in range(1, E):
+            load_w(e)
 
         make_identity(nc, identity[:])
-        second_half = gates[1][:].rearrange("q (p c) -> q p c", c=GATE_RUN)
-        for first in range(0, GATE_RUN, RUN):
-            spread = psum.tile([P, RUN, P], F32, name=f"spread{first}")
+        unread = keep.tile([P, 1], F32, name="unread")
+        nc.scalar.activation(unread[:], gate_runs[1][:, 0, :1], COPY)
+        for e in (2, 3, 0, 1):
             for c in range(RUN):
-                column = gate_runs[:, first + c : first + c + 1]
-                nc.tensor.transpose(spread[:, c], column.to_broadcast([P, P]), identity[:])
-            nc.vector.tensor_copy(second_half[:, :, first : first + RUN], spread[:].rearrange("q c p -> q p c"))
-
-        def gate_of(first, last):
-            return gates[first // HALF][:, first % HALF : first % HALF + last - first]
+                column = gate_runs[e // 2][:, e % 2, c : c + 1]
+                nc.tensor.transpose(gate_banks[e][:, c], column.to_broadcast([P, P]), identity[:])
+            if e >= 2:
+                target = gates[:, (e - 2) * C : (e - 1) * C].rearrange("q (p c) -> q p c", c=RUN)
+                nc.vector.tensor_copy(target, gate_banks[e][:].rearrange("q c p -> q p c"))
 
         def listed(window, first, last):
             return window.indirect(offsets[:, first // OFFSETS : last // OFFSETS])
@@ -108,11 +109,10 @@ def tile_moe_bdx_lin_none_kernel(tc, dyT, w, gate, offs, out):
 
         def gather_gated(planes, g, first, last):
             for t in range(PLANES):
-                nc.vector.tensor_tensor(planes[:, t], listed(dy[g, t], first, last), gate_of(first, last), MULT)
+                nc.vector.tensor_tensor(planes[:, t], listed(dy[g, t], first, last), gates[:, first - HALF : last - HALF], MULT)
 
-        def grouped_tile(width):
-            grouped = grouped_pool.tile([P, HALF * PLANES], BF16, name="grouped", align_bytes=64)
-            return grouped[:, : width * PLANES]
+        def room(place, width):
+            return woven[:, place * C * PLANES : (place * C + width) * PLANES]
 
         def weave(grouped, planes):
             nc.vector.tensor_copy(
@@ -121,42 +121,43 @@ def tile_moe_bdx_lin_none_kernel(tc, dyT, w, gate, offs, out):
             )
 
         def weave_gating(grouped, planes, first, last):
-            factor = gate_of(first, last).rearrange("p (c i) -> p c i", i=RUN).unsqueeze(2)
-            nc.vector.tensor_tensor(
-                grouped.rearrange("p (c i t) -> p c t i", i=RUN, t=PLANES),
-                planes.rearrange("p t (c i) -> p c t i", i=RUN),
-                factor.to_broadcast([P, (last - first) // RUN, PLANES, RUN]),
-                MULT,
-            )
+            for start in range(first, last, C):
+                width = min(C, last - start)
+                place = start - first
+                runs = gate_banks[start // C][:, :, start % C // RUN : (start % C + width) // RUN]
+                nc.vector.tensor_tensor(
+                    grouped[:, place * PLANES : (place + width) * PLANES].rearrange("p (c i t) -> p c t i", i=RUN, t=PLANES),
+                    planes[:, :, place : place + width].rearrange("p t (c i) -> p c t i", i=RUN),
+                    runs.rearrange("q i c -> q c i").unsqueeze(2).to_broadcast([P, width // RUN, PLANES, RUN]),
+                    MULT,
+                )
 
         def quantise(grouped, g, first, last):
             nc.vector.quantize_mx(
                 out=codes[:, g, first:last].bitcast(E5M2), scales=scales[:, g, first:last], in_=grouped
             )
 
-        def weave_w(e):
-            grouped = w_pool.tile([P, PASSES * K * PLANES], BF16, name="w_grouped", align_bytes=64)
+        def weave_w(grouped, e):
             nc.vector.tensor_copy(
-                grouped[:].rearrange("p (g c i t) -> p c g t i", g=PASSES, i=RUN, t=PLANES),
-                w_raw[e][:].rearrange("p g t (c i) -> p c g t i", i=RUN),
+                grouped.rearrange("p (g c i t) -> p c g t i", g=PASSES, i=RUN, t=PLANES),
+                w_raw[e][:].rearrange("p (g t c i) -> p c g t i", g=PASSES, t=PLANES, i=RUN),
             )
-            return grouped[:]
 
         def quantise_w(grouped, e):
             nc.vector.quantize_mx(out=w_codes[:, e].bitcast(E4M3), scales=w_scales[:, e], in_=grouped)
 
-        def finish(first, last):
+        def finish(first, last, order):
             e = first // C
-            bank = psum.tile([P, last - first], F32, name=f"bank{first}")
-            for g in range(PASSES):
+            bank = psum.tile([P, last - first], F32, name=f"bank{(first + PIECE) // C % E}")
+            for g in order:
                 nc.tensor.matmul_mx(
                     out=bank[:],
                     lhsT=w_codes[:, e, g * K : (g + 1) * K].bitcast(E4M3),
                     lhsT_scale=w_scales[:, e, g * K : (g + 1) * K],
                     rhs=codes[:, g, first:last].bitcast(E5M2),
                     rhs_scale=scales[:, g, first:last],
-                    start=(g == 0),
-                    stop=(g == PASSES - 1),
+                    start=(g == order[0]),
+                    stop=(g == order[-1]),
                 )
             nc.scalar.copy(out=results[:, first:last], in_=bank[:])
             for start in range(first, last, PIECE):
@@ -164,50 +165,56 @@ def tile_moe_bdx_lin_none_kernel(tc, dyT, w, gate, offs, out):
 
         gather_plain(outer[0], 0, range(PLANES), 0, HALF)
         gather_gated(gated, 0, HALF, SLOTS)
-        upper = grouped_tile(HALF)
+        upper = room(0, HALF)
         weave(upper, gated[:])
-        lower = grouped_tile(HALF)
+        lower = room(2, HALF)
         weave_gating(lower, outer[0][:], 0, HALF)
         quantise(upper, 0, HALF, SLOTS)
         quantise(lower, 0, 0, HALF)
 
-        cut = CUT
-        gather_plain(inner, 1, range(PLANES), 0, cut)
-        gather_gated(gated[:, :, : SLOTS - cut], 1, cut, SLOTS)
-        lower = grouped_tile(HALF)
-        weave_gating(lower, inner[:, :, :HALF], 0, HALF)
+        gather_plain(inner, 1, range(PLANES), 0, HALF)
+        gather_gated(gated[:, :, : HALF - PIECE], 1, HALF, SLOTS - PIECE)
+        lower = room(0, HALF)
+        weave_gating(lower, inner[:], 0, HALF)
         quantise(lower, 1, 0, HALF)
 
-        def rest_of_pass_1(e):
-            first, last = e * C, (e + 1) * C
-            middle = min(max(first, cut), last)
-            grouped = grouped_tile(C)
-            if first < middle:
-                weave_gating(grouped[:, : (middle - first) * PLANES], inner[:, :, first:middle], first, middle)
-            weave(grouped[:, (middle - first) * PLANES :], gated[:, :, middle - cut : last - cut])
-            return grouped
+        for t in range(2):
+            gather_plain(outer[0], 2, [t], 0, HALF)
+            gather_plain(outer[1], 2, [t], HALF, SLOTS)
+        gather_plain(outer[0], 2, [2], 0, HALF)
+        for first in (0, C):
+            gather_plain(outer[0][:, :, first : first + C], 2, [PLANES - 1], first, first + C)
+        gather_plain(outer[1], 2, [2, 3], HALF, SLOTS)
 
-        for t in range(PLANES // 2):
-            for h in range(2):
-                gather_plain(outer[h], 2, [t], h * HALF, (h + 1) * HALF)
-        for h in range(2):
-            gather_plain(outer[h], 2, [PLANES - 2], h * HALF, (h + 1) * HALF)
-            for first in (0, C):
-                gather_plain(outer[h][:, :, first : first + C], 2, [PLANES - 1], h * HALF + first, h * HALF + first + C)
+        def spent(e, width):
+            return w_raw[e][:].bitcast(BF16)[:, : width * PLANES]
+
+        def weave_pass_2(grouped, first, last):
+            weave_gating(grouped, outer[first // HALF][:, :, first % HALF : first % HALF + last - first], first, last)
+
         for e in range(E):
-            first, last = e * C, (e + 1) * C
-            rest = rest_of_pass_1(e) if first >= HALF else None
-            w_grouped = weave_w(e)
-            if rest is not None:
-                quantise(rest, 1, first, last)
-            ends = (first, last) if e < E - 1 else (first, last - PIECE, last)
-            for start, end in zip(ends, ends[1:]):
-                grouped = grouped_tile(end - start)
-                weave_gating(grouped, outer[start // HALF][:, :, start % HALF : start % HALF + end - start], start, end)
-                if start == first:
-                    quantise_w(w_grouped, e)
-                quantise(grouped, 2, start, end)
-                finish(start, end)
+            first, last = e * C, min((e + 1) * C, SLOTS - PIECE)
+            w_grouped = room(2 if e == 0 else 0, PASSES * K)
+            grouped = room(0, C) if e == 0 else spent(e, last - first)
+            weave_w(w_grouped, e)
+            if first >= HALF:
+                weave(spent(1, last - first), gated[:, :, first - HALF : last - HALF])
+                quantise_w(w_grouped, e)
+                weave_pass_2(grouped, first, last)
+                quantise(spent(1, last - first), 1, first, last)
+            else:
+                weave_pass_2(grouped, first, last)
+                quantise_w(w_grouped, e)
+            quantise(grouped, 2, first, last)
+            finish(first, last, (0, 1, 2))
+        first, last = SLOTS - PIECE, SLOTS
+        late = outer[1][:, :, :PIECE]
+        gather_gated(late, 1, first, last)
+        weave_pass_2(spent(2, PIECE), first, last)
+        weave(room(0, PIECE), late)
+        quantise(spent(2, PIECE), 2, first, last)
+        quantise(room(0, PIECE), 1, first, last)
+        finish(first, last, (0, 2, 1))
 
         for q, queue in enumerate((nc.sync, nc.scalar, nc.sync, nc.scalar)):
             queue.dma_start(out=out[:, q * C : (q + 1) * C], in_=tokens[:, q * C : (q + 1) * C])

@@ -143,6 +143,16 @@ def tile_moe_bdx_lin_none_kernel(tc, dyT, w, gate, offs, out):
                 w_raw[e][:].rearrange("p (g t c i) -> p c g t i", g=PASSES, t=PLANES, i=RUN),
             )
 
+        def weave_w_aside(grouped, e):
+            nc.gpsimd.tensor_scalar(
+                grouped.rearrange("p (g k t) -> p g k t", g=PASSES, t=PLANES),
+                w_raw[e][:].rearrange("p (g t k) -> p g k t", g=PASSES, t=PLANES),
+                1.0,
+                0.0,
+                MULT,
+                mybir.AluOpType.add,
+            )
+
         def quantise_w(grouped, e):
             nc.vector.quantize_mx(out=w_codes[:, e].bitcast(E4M3), scales=w_scales[:, e], in_=grouped)
 
@@ -192,19 +202,27 @@ def tile_moe_bdx_lin_none_kernel(tc, dyT, w, gate, offs, out):
         def weave_pass_2(grouped, first, last):
             weave_gating(grouped, outer[first // HALF][:, :, first % HALF : first % HALF + last - first], first, last)
 
+        size = PASSES * K * PLANES
+        start = HALF * PLANES
+        w_grouped = [
+            woven[:, start : start + size],
+            woven[:, start - size // 2 : start + size // 2],
+            woven[:, start - size : start],
+            woven[:, start - size : start],
+        ]
+        weave_w(w_grouped[0], 0)
         for e in range(E):
             first, last = e * C, min((e + 1) * C, SLOTS - PIECE)
-            w_grouped = room(2 if e == 0 else 0, PASSES * K)
-            grouped = room(0, C) if e == 0 else spent(e, last - first)
-            weave_w(w_grouped, e)
+            grouped = woven[:, start - size // 2 - C * PLANES : start - size // 2] if e == 0 else spent(e, last - first)
             if first >= HALF:
-                weave(spent(1, last - first), gated[:, :, first - HALF : last - HALF])
-                quantise_w(w_grouped, e)
-                weave_pass_2(grouped, first, last)
-                quantise(spent(1, last - first), 1, first, last)
-            else:
-                weave_pass_2(grouped, first, last)
-                quantise_w(w_grouped, e)
+                earlier = room(0, C) if e == 2 else spent(1, last - first)
+                weave(earlier, gated[:, :, first - HALF : last - HALF])
+            quantise_w(w_grouped[e], e)
+            if e + 1 < E:
+                weave_w_aside(w_grouped[e + 1], e + 1)
+            weave_pass_2(grouped, first, last)
+            if first >= HALF:
+                quantise(earlier, 1, first, last)
             quantise(grouped, 2, first, last)
             finish(first, last, (0, 1, 2))
         first, last = SLOTS - PIECE, SLOTS

@@ -27,6 +27,7 @@ U8 = mybir.dt.uint8
 E4M3 = mybir.dt.float8_e4m3fn_x4
 E5M2 = mybir.dt.float8_e5m2_x4
 MULT = mybir.AluOpType.mult
+ADD = mybir.AluOpType.add
 COPY = mybir.ActivationFunctionType.Copy
 
 
@@ -120,6 +121,11 @@ def tile_moe_bdx_lin_none_kernel(tc, dyT, w, gate, offs, out):
                 planes.rearrange("p t (c i) -> p c t i", i=RUN),
             )
 
+        def weave_aside(grouped, planes):
+            nc.gpsimd.tensor_scalar(
+                grouped.rearrange("p (c t) -> p c t", t=PLANES), planes.rearrange("p t c -> p c t"), 1.0, 0.0, MULT, ADD
+            )
+
         def weave_gating(grouped, planes, first, last):
             for start in range(first, last, C):
                 width = min(C, last - start)
@@ -150,7 +156,7 @@ def tile_moe_bdx_lin_none_kernel(tc, dyT, w, gate, offs, out):
                 1.0,
                 0.0,
                 MULT,
-                mybir.AluOpType.add,
+                ADD,
             )
 
         def quantise_w(grouped, e):
@@ -175,26 +181,29 @@ def tile_moe_bdx_lin_none_kernel(tc, dyT, w, gate, offs, out):
 
         gather_plain(outer[0], 0, range(PLANES), 0, HALF)
         gather_gated(gated, 0, HALF, SLOTS)
-        upper = room(0, HALF)
-        weave(upper, gated[:])
-        lower = room(2, HALF)
-        weave_gating(lower, outer[0][:], 0, HALF)
-        quantise(upper, 0, HALF, SLOTS)
-        quantise(lower, 0, 0, HALF)
+        weave_aside(room(1, C), gated[:, :, C:])
+        weave_gating(room(2, HALF), outer[0][:], 0, HALF)
+        third = outer[0][:, PLANES - 1].bitcast(BF16)
+        weave(third, gated[:, :, :C])
+        quantise(room(2, HALF), 0, 0, HALF)
+        quantise(third, 0, HALF, HALF + C)
+        quantise(room(1, C), 0, HALF + C, SLOTS)
 
         gather_plain(inner, 1, range(PLANES), 0, HALF)
         gather_gated(gated[:, :, : HALF - PIECE], 1, HALF, SLOTS - PIECE)
+        weave_aside(room(3, C), gated[:, :, :C])
         lower = room(0, HALF)
         weave_gating(lower, inner[:], 0, HALF)
         quantise(lower, 1, 0, HALF)
 
+        upper = outer[1][:, :, : HALF - PIECE]
         for t in range(2):
             gather_plain(outer[0], 2, [t], 0, HALF)
-            gather_plain(outer[1], 2, [t], HALF, SLOTS)
+            gather_plain(upper, 2, [t], HALF, SLOTS - PIECE)
         gather_plain(outer[0], 2, [2], 0, HALF)
         for first in (0, C):
             gather_plain(outer[0][:, :, first : first + C], 2, [PLANES - 1], first, first + C)
-        gather_plain(outer[1], 2, [2, 3], HALF, SLOTS)
+        gather_plain(upper, 2, [2, 3], HALF, SLOTS - PIECE)
 
         def spent(e, width):
             return w_raw[e][:].bitcast(BF16)[:, : width * PLANES]
@@ -215,7 +224,8 @@ def tile_moe_bdx_lin_none_kernel(tc, dyT, w, gate, offs, out):
             first, last = e * C, min((e + 1) * C, SLOTS - PIECE)
             grouped = woven[:, start - size // 2 - C * PLANES : start - size // 2] if e == 0 else spent(e, last - first)
             if first >= HALF:
-                earlier = room(0, C) if e == 2 else spent(1, last - first)
+                earlier = room(3, C) if e == 2 else spent(1, last - first)
+            if e == 3:
                 weave(earlier, gated[:, :, first - HALF : last - HALF])
             quantise_w(w_grouped[e], e)
             if e + 1 < E:
@@ -228,11 +238,14 @@ def tile_moe_bdx_lin_none_kernel(tc, dyT, w, gate, offs, out):
         first, last = SLOTS - PIECE, SLOTS
         late = outer[1][:, :, :PIECE]
         gather_gated(late, 1, first, last)
-        weave_pass_2(spent(2, PIECE), first, last)
+        ungated = outer[1][:, :, PIECE : 2 * PIECE]
+        for t in range(PLANES):
+            nc.vector.tensor_copy(ungated[:, t], listed(dy[2, t], first, last))
         weave(room(0, PIECE), late)
-        quantise(spent(2, PIECE), 2, first, last)
+        weave_gating(spent(2, PIECE), ungated, first, last)
         quantise(room(0, PIECE), 1, first, last)
-        finish(first, last, (0, 2, 1))
+        quantise(spent(2, PIECE), 2, first, last)
+        finish(first, last, (0, 1, 2))
 
         for q, queue in enumerate((nc.sync, nc.scalar, nc.sync, nc.scalar)):
             queue.dma_start(out=out[:, q * C : (q + 1) * C], in_=tokens[:, q * C : (q + 1) * C])

@@ -90,6 +90,8 @@ def tile_moe_bdx_lin_none_kernel(tc, dyT, w, gate, offs, out):
         for e in range(1, E):
             load_w(e)
 
+        middle_codes = dy_pool.tile([P, HALF], U32, name="middle_codes", offset=0, align_bytes=256)
+
         make_identity(nc, identity[:])
         unread = keep.tile([P, 1], F32, name="unread")
         nc.scalar.activation(unread[:], gate_runs[1][:, 0, :1], COPY)
@@ -138,9 +140,14 @@ def tile_moe_bdx_lin_none_kernel(tc, dyT, w, gate, offs, out):
                     MULT,
                 )
 
+        def codes_of(g, first, last):
+            if g == 1 and C <= first < 3 * C:
+                return middle_codes[:, first - C : last - C]
+            return codes[:, g, first:last]
+
         def quantise(grouped, g, first, last):
             nc.vector.quantize_mx(
-                out=codes[:, g, first:last].bitcast(E5M2), scales=scales[:, g, first:last], in_=grouped
+                out=codes_of(g, first, last).bitcast(E5M2), scales=scales[:, g, first:last], in_=grouped
             )
 
         def weave_w(grouped, e):
@@ -170,7 +177,7 @@ def tile_moe_bdx_lin_none_kernel(tc, dyT, w, gate, offs, out):
                     out=bank[:],
                     lhsT=w_codes[:, e, g * K : (g + 1) * K].bitcast(E4M3),
                     lhsT_scale=w_scales[:, e, g * K : (g + 1) * K],
-                    rhs=codes[:, g, first:last].bitcast(E5M2),
+                    rhs=codes_of(g, first, last).bitcast(E5M2),
                     rhs_scale=scales[:, g, first:last],
                     start=(g == order[0]),
                     stop=(g == order[-1]),
@@ -191,10 +198,9 @@ def tile_moe_bdx_lin_none_kernel(tc, dyT, w, gate, offs, out):
 
         gather_plain(inner, 1, range(PLANES), 0, HALF)
         gather_gated(gated[:, :, : HALF - PIECE], 1, HALF, SLOTS - PIECE)
-        weave_aside(room(3, C), gated[:, :, :C])
-        lower = room(0, HALF)
-        weave_gating(lower, inner[:], 0, HALF)
-        quantise(lower, 1, 0, HALF)
+        weave_aside(room(2, C), gated[:, :, :C])
+        weave_gating(room(0, HALF), inner[:], 0, HALF)
+        quantise(room(0, C), 1, 0, C)
 
         upper = outer[1][:, :, : HALF - PIECE]
         for t in range(2):
@@ -212,28 +218,22 @@ def tile_moe_bdx_lin_none_kernel(tc, dyT, w, gate, offs, out):
             weave_gating(grouped, outer[first // HALF][:, :, first % HALF : first % HALF + last - first], first, last)
 
         size = PASSES * K * PLANES
-        start = HALF * PLANES
-        w_grouped = [
-            woven[:, start : start + size],
-            woven[:, start - size // 2 : start + size // 2],
-            woven[:, start - size : start],
-            woven[:, start - size : start],
-        ]
+        start = 3 * C * PLANES
+        w_grouped = [woven[:, start : start + size]] * 3 + [woven[:, start - size // 2 : start + size // 2]]
         weave_w(w_grouped[0], 0)
         for e in range(E):
             first, last = e * C, min((e + 1) * C, SLOTS - PIECE)
-            grouped = woven[:, start - size // 2 - C * PLANES : start - size // 2] if e == 0 else spent(e, last - first)
-            if first >= HALF:
-                earlier = room(3, C) if e == 2 else spent(1, last - first)
             if e == 3:
-                weave(earlier, gated[:, :, first - HALF : last - HALF])
+                weave(spent(1, PIECE), gated[:, :, first - HALF : last - HALF])
             quantise_w(w_grouped[e], e)
             if e + 1 < E:
                 weave_w_aside(w_grouped[e + 1], e + 1)
-            weave_pass_2(grouped, first, last)
-            if first >= HALF:
-                quantise(earlier, 1, first, last)
-            quantise(grouped, 2, first, last)
+            weave_pass_2(spent(e, last - first), first, last)
+            if e == 1:
+                quantise(room(1, HALF), 1, C, 3 * C)
+            if e == 3:
+                quantise(spent(1, PIECE), 1, first, last)
+            quantise(spent(e, last - first), 2, first, last)
             finish(first, last, (0, 1, 2))
         first, last = SLOTS - PIECE, SLOTS
         late = outer[1][:, :, :PIECE]

@@ -81,13 +81,13 @@ def tile_moe_bdx_lin_none_kernel(tc, dyT, w, gate, offs, out):
         nc.sync.dma_start(out=offsets[:], in_=offs)
         load_dy(0, 1, 0, T)
         load_gate(0)
-        for block in range(2, PASSES * PLANES - 2):
+        for block in range(2, PASSES * PLANES - 3):
             load_dy(block // PLANES, block % PLANES, 0, T)
-        load_w(0)
-        pair = dy_pool.tile([P, 2, T], F32, name="dy_pair", offset=(PASSES * PLANES - 2) * BLOCK_BYTES, align_bytes=256)
-        nc.sync.dma_start(out=pair[:], in_=dyT.rearrange("(g p t) c -> g p t c", p=P, t=PLANES)[2, :, 2:])
-        dy[2, 2], dy[2, 3] = pair[:, 0], pair[:, 1]
-        for e in range(1, E):
+        joined = dy_pool.tile([P, 3, T], F32, name="dy_joined", offset=(PASSES * PLANES - 3) * BLOCK_BYTES, align_bytes=256)
+        nc.sync.dma_start(out=joined[:], in_=dyT.rearrange("(g p t) c -> g p t c", p=P, t=PLANES)[2, :, 1:])
+        for t in range(1, PLANES):
+            dy[2, t] = joined[:, t - 1]
+        for e in range(E):
             load_w(e)
 
         middle_codes = dy_pool.tile([P, HALF], U32, name="middle_codes", offset=0, align_bytes=256)
@@ -169,7 +169,7 @@ def tile_moe_bdx_lin_none_kernel(tc, dyT, w, gate, offs, out):
         def quantise_w(grouped, e):
             nc.vector.quantize_mx(out=w_codes[:, e].bitcast(E4M3), scales=w_scales[:, e], in_=grouped)
 
-        def finish(first, last, order):
+        def multiply(first, last, order):
             e = first // C
             bank = psum.tile([P, last - first], F32, name=f"bank{(first + PIECE) // C % E}")
             for g in order:
@@ -182,7 +182,9 @@ def tile_moe_bdx_lin_none_kernel(tc, dyT, w, gate, offs, out):
                     start=(g == order[0]),
                     stop=(g == order[-1]),
                 )
-            nc.scalar.copy(out=results[:, first:last], in_=bank[:])
+            return bank
+
+        def scatter(first, last):
             for start in range(first, last, PIECE):
                 nc.scalar.activation(listed(tokens[:], start, start + PIECE), results[:, start : start + PIECE], COPY)
 
@@ -202,14 +204,12 @@ def tile_moe_bdx_lin_none_kernel(tc, dyT, w, gate, offs, out):
         weave_gating(room(0, HALF), inner[:], 0, HALF)
         quantise(room(0, C), 1, 0, C)
 
-        upper = outer[1][:, :, : HALF - PIECE]
-        for t in range(2):
-            gather_plain(outer[0], 2, [t], 0, HALF)
-            gather_plain(upper, 2, [t], HALF, SLOTS - PIECE)
-        gather_plain(outer[0], 2, [2], 0, HALF)
+        gather_plain(outer[0], 2, [0], 0, HALF)
+        gather_plain(outer[1], 2, [0], HALF, SLOTS)
+        gather_plain(outer[0], 2, [1, 2], 0, HALF)
         for first in (0, C):
             gather_plain(outer[0][:, :, first : first + C], 2, [PLANES - 1], first, first + C)
-        gather_plain(upper, 2, [2, 3], HALF, SLOTS - PIECE)
+        gather_plain(outer[1], 2, [1, 2, 3], HALF, SLOTS)
 
         def spent(e, width):
             return w_raw[e][:].bitcast(BF16)[:, : width * PLANES]
@@ -220,32 +220,48 @@ def tile_moe_bdx_lin_none_kernel(tc, dyT, w, gate, offs, out):
         size = PASSES * K * PLANES
         start = 3 * C * PLANES
         w_grouped = [woven[:, start : start + size]] * 3 + [woven[:, start - size // 2 : start + size // 2]]
+
+        def finish(bank, first, last):
+            nc.vector.tensor_copy(results[:, first:last], bank[:])
+            scatter(first, last)
+
+        def finish_on_scalar(bank, first, last):
+            nc.scalar.copy(out=results[:, first:last], in_=bank[:])
+            scatter(first, last)
+
         weave_w(w_grouped[0], 0)
-        for e in range(E):
-            first, last = e * C, min((e + 1) * C, SLOTS - PIECE)
-            if e == 3:
-                weave(spent(1, PIECE), gated[:, :, first - HALF : last - HALF])
+        quantise_w(w_grouped[0], 0)
+        weave_w_aside(w_grouped[1], 1)
+        weave_pass_2(spent(0, C), 0, C)
+        quantise(spent(0, C), 2, 0, C)
+        bank = multiply(0, C, (0, 1, 2))
+        for e in (1, 2):
+            first, middle, last = e * C, e * C + PIECE, (e + 1) * C
             quantise_w(w_grouped[e], e)
-            if e + 1 < E:
-                weave_w_aside(w_grouped[e + 1], e + 1)
-            weave_pass_2(spent(e, last - first), first, last)
+            weave_w_aside(w_grouped[e + 1], e + 1)
+            weave_pass_2(spent(e, PIECE), first, middle)
+            finish(bank, first - C, first)
+            weave_pass_2(spent(e, C)[:, PIECE * PLANES :], middle, last)
             if e == 1:
                 quantise(room(1, HALF), 1, C, 3 * C)
-            if e == 3:
-                quantise(spent(1, PIECE), 1, first, last)
-            quantise(spent(e, last - first), 2, first, last)
-            finish(first, last, (0, 1, 2))
+            quantise(spent(e, C), 2, first, last)
+            bank = multiply(first, last, (0, 1, 2))
+        finish_on_scalar(bank, first, last)
+        first, last = 3 * C, SLOTS - PIECE
+        weave(spent(1, PIECE), gated[:, :, first - HALF : last - HALF])
+        quantise_w(w_grouped[3], 3)
+        weave_pass_2(spent(3, PIECE), first, last)
+        quantise(spent(1, PIECE), 1, first, last)
+        quantise(spent(3, PIECE), 2, first, last)
+        finish_on_scalar(multiply(first, last, (0, 1, 2)), first, last)
         first, last = SLOTS - PIECE, SLOTS
         late = outer[1][:, :, :PIECE]
         gather_gated(late, 1, first, last)
-        ungated = outer[1][:, :, PIECE : 2 * PIECE]
-        for t in range(PLANES):
-            nc.vector.tensor_copy(ungated[:, t], listed(dy[2, t], first, last))
+        weave_pass_2(spent(2, PIECE), first, last)
         weave(room(0, PIECE), late)
-        weave_gating(spent(2, PIECE), ungated, first, last)
-        quantise(room(0, PIECE), 1, first, last)
         quantise(spent(2, PIECE), 2, first, last)
-        finish(first, last, (0, 1, 2))
+        quantise(room(0, PIECE), 1, first, last)
+        finish(multiply(first, last, (0, 2, 1)), first, last)
 
         for q, queue in enumerate((nc.sync, nc.scalar, nc.sync, nc.scalar)):
             queue.dma_start(out=out[:, q * C : (q + 1) * C], in_=tokens[:, q * C : (q + 1) * C])

@@ -246,14 +246,15 @@ def tile_moe_bdx_lin_none_kernel(tc, dyT, w, gate, offs, out):
                 quantise(room(1, HALF), 1, C, 3 * C)
             quantise(spent(e, C), 2, first, last)
             bank = multiply(first, last, (0, 1, 2))
-        finish_on_scalar(bank, first, last)
         first, last = 3 * C, SLOTS - PIECE
-        weave(spent(1, PIECE), gated[:, :, first - HALF : last - HALF])
         quantise_w(w_grouped[3], 3)
+        earlier = w_grouped[3][:, : PIECE * PLANES]
+        weave_aside(earlier, gated[:, :, first - HALF : last - HALF])
         weave_pass_2(spent(3, PIECE), first, last)
-        quantise(spent(1, PIECE), 1, first, last)
+        finish(bank, first - C, first)
         quantise(spent(3, PIECE), 2, first, last)
-        finish_on_scalar(multiply(first, last, (0, 1, 2)), first, last)
+        quantise(earlier, 1, first, last)
+        finish_on_scalar(multiply(first, last, (0, 2, 1)), first, last)
         first, last = SLOTS - PIECE, SLOTS
         late = outer[1][:, :, :PIECE]
         gather_gated(late, 1, first, last)

@@ -79,10 +79,10 @@ def tile_moe_bdx_lin_none_kernel(tc, dyT, w, gate, offs, out):
         load_dy(0, 0, 0, HALF)
         load_dy(0, 0, HALF, T)
         nc.sync.dma_start(out=offsets[:], in_=offs)
-        load_dy(0, 1, 0, T)
-        load_gate(0)
-        for block in range(2, PASSES * PLANES - 3):
+        for block in range(1, PASSES * PLANES - 3):
             load_dy(block // PLANES, block % PLANES, 0, T)
+            if block == PLANES - 1:
+                load_gate(0)
         joined = dy_pool.tile([P, 3, T], F32, name="dy_joined", offset=(PASSES * PLANES - 3) * BLOCK_BYTES, align_bytes=256)
         nc.sync.dma_start(out=joined[:], in_=dyT.rearrange("(g p t) c -> g p t c", p=P, t=PLANES)[2, :, 1:])
         for t in range(1, PLANES):
@@ -262,7 +262,8 @@ def tile_moe_bdx_lin_none_kernel(tc, dyT, w, gate, offs, out):
         weave(room(0, PIECE), late)
         quantise(spent(2, PIECE), 2, first, last)
         quantise(room(0, PIECE), 1, first, last)
-        finish(multiply(first, last, (0, 2, 1)), first, last)
+        nc.vector.tensor_copy(results[:, first:last], multiply(first, last, (0, 2, 1))[:])
+        nc.vector.tensor_copy(listed(tokens[:], first, last), results[:, first:last])
 
         for q, queue in enumerate((nc.sync, nc.scalar, nc.sync, nc.scalar)):
             queue.dma_start(out=out[:, q * C : (q + 1) * C], in_=tokens[:, q * C : (q + 1) * C])

@@ -14,6 +14,7 @@ SPARE = 16
 RUN = 4
 PIECE = 256
 
+SCATTERS = (0, 256, 512, 768, 1024, 1408, 1792)
 BLOCK_BYTES = 8448
 
 FLOPS = 2 * K * N * SLOTS
@@ -185,8 +186,9 @@ def tile_moe_bdx_lin_none_kernel(tc, dyT, w, gate, offs, out):
             return bank
 
         def scatter(first, last):
-            for start in range(first, last, PIECE):
-                nc.scalar.activation(listed(tokens[:], start, start + PIECE), results[:, start : start + PIECE], COPY)
+            for start, end in zip(SCATTERS, SCATTERS[1:]):
+                if first < end <= last:
+                    nc.scalar.activation(listed(tokens[:], start, end), results[:, start:end], COPY)
 
         gather_plain(outer[0], 0, range(PLANES), 0, HALF)
         gather_gated(gated, 0, HALF, SLOTS)

@@ -15,6 +15,7 @@ RUN = 4
 PIECE = 256
 
 SCATTERS = (0, 256, 512, 768, 1024, 1408, 1792)
+OWN = 384
 BLOCK_BYTES = 8448
 
 FLOPS = 2 * K * N * SLOTS
@@ -47,7 +48,8 @@ def tile_moe_bdx_lin_none_kernel(tc, dyT, w, gate, offs, out):
         gates = keep.tile([P, HALF], F32, name="gates", align_bytes=256)
         tokens = keep.tile([P, T], F32, name="tokens", align_bytes=256)
         results = keep.tile([P, SLOTS], F32, name="results", align_bytes=256)
-        outer = [keep.tile([P, PLANES, HALF], F32, name=f"outer{h}", align_bytes=256) for h in range(2)]
+        halves = keep.tile([P, 2 * PLANES, HALF], F32, name="halves", align_bytes=256)
+        outer = [halves[:, :PLANES], halves[:, PLANES:]]
         inner = keep.tile([P, PLANES, HALF], F32, name="inner", align_bytes=256)
         gated = keep.tile([P, PLANES, HALF], F32, name="gated", align_bytes=256)
         woven = keep.tile([P, 4 * C * PLANES], BF16, name="woven", align_bytes=64)
@@ -192,13 +194,14 @@ def tile_moe_bdx_lin_none_kernel(tc, dyT, w, gate, offs, out):
 
         gather_plain(outer[0], 0, range(PLANES), 0, HALF)
         gather_gated(gated, 0, HALF, SLOTS)
-        weave_aside(room(1, C), gated[:, :, C:])
-        weave_gating(room(2, HALF), outer[0][:], 0, HALF)
-        third = outer[0][:, PLANES - 1].bitcast(BF16)
-        weave(third, gated[:, :, :C])
+        seam = 2 * PLANES * HALF - OWN * PLANES
+        upper = halves[:].rearrange("p t c -> p (t c)").bitcast(BF16)[:, seam : seam + HALF * PLANES]
+        weave_aside(upper[:, OWN * PLANES :], gated[:, :, OWN:])
+        weave_gating(room(2, HALF), outer[0], 0, HALF)
+        weave(upper[:, : OWN * PLANES], gated[:, :, :OWN])
         quantise(room(2, HALF), 0, 0, HALF)
-        quantise(third, 0, HALF, HALF + C)
-        quantise(room(1, C), 0, HALF + C, SLOTS)
+        quantise(upper[:, C * PLANES :], 0, HALF + C, SLOTS)
+        quantise(upper[:, : C * PLANES], 0, HALF, HALF + C)
 
         gather_plain(inner, 1, range(PLANES), 0, HALF)
         gather_gated(gated[:, :, : HALF - PIECE], 1, HALF, SLOTS - PIECE)

@@ -1,7 +1,6 @@
 from contextlib import ExitStack
 
 import concourse.mybir as mybir
-from concourse.masks import make_identity
 
 K, T, E, C, N = 128, 2048, 4, 512, 1536
 SLOTS = E * C
@@ -10,13 +9,9 @@ PLANES = 4
 PASSES = N // (P * PLANES)
 OFFSETS = 16
 HALF = SLOTS // 2
-SPARE = 16
 RUN = 4
 PIECE = 256
-
-SCATTERS = (0, 256, 512, 768, 1024, 1408, 1792)
-OWN = 384
-BLOCK_BYTES = 8448
+KIB = 1024
 
 FLOPS = 2 * K * N * SLOTS
 BYTES = 4 * (N * T + E * N * K + SLOTS + K * T) + 2 * SLOTS
@@ -29,7 +24,6 @@ U8 = mybir.dt.uint8
 E4M3 = mybir.dt.float8_e4m3fn_x4
 E5M2 = mybir.dt.float8_e5m2_x4
 MULT = mybir.AluOpType.mult
-ADD = mybir.AluOpType.add
 COPY = mybir.ActivationFunctionType.Copy
 
 
@@ -41,234 +35,91 @@ def tile_moe_bdx_lin_none_kernel(tc, dyT, w, gate, offs, out):
     with ExitStack() as ctx:
         lists = ctx.enter_context(tc.tile_pool(name="lists", bufs=1))
         keep = ctx.enter_context(tc.tile_pool(name="keep", bufs=1))
-        dy_pool = ctx.enter_context(tc.tile_pool(name="dy_pool", bufs=1))
+        room = ctx.enter_context(tc.tile_pool(name="room", bufs=1))
         psum = ctx.enter_context(tc.psum_pool(name="psum", bufs=1))
 
+        def placed(shape, dtype, name, kib):
+            return room.tile(shape, dtype, name=name, offset=kib * KIB, align_bytes=256)
+
         offsets = lists.tile([P, SLOTS // OFFSETS], U16, name="offsets")
-        gates = keep.tile([P, HALF], F32, name="gates", align_bytes=256)
+        gates = keep.tile([P, SLOTS], F32, name="gates", align_bytes=256)
         tokens = keep.tile([P, T], F32, name="tokens", align_bytes=256)
-        results = keep.tile([P, SLOTS], F32, name="results", align_bytes=256)
-        halves = keep.tile([P, 2 * PLANES, HALF], F32, name="halves", align_bytes=256)
-        outer = [halves[:, :PLANES], halves[:, PLANES:]]
-        inner = keep.tile([P, PLANES, HALF], F32, name="inner", align_bytes=256)
-        gated = keep.tile([P, PLANES, HALF], F32, name="gated", align_bytes=256)
-        woven = keep.tile([P, 4 * C * PLANES], BF16, name="woven", align_bytes=64)
-        codes = keep.tile([P, PASSES, SLOTS], U32, name="codes", align_bytes=64)
-        scales = keep.tile([P, PASSES, SLOTS], U8, name="scales", align_bytes=64)
+        woven = [keep.tile([P, SLOTS * PLANES], BF16, name=f"woven{g}", align_bytes=256) for g in range(PASSES)]
         w_codes = keep.tile([P, E, PASSES * K], U32, name="w_codes", align_bytes=64)
         w_scales = keep.tile([P, E, PASSES * K], U8, name="w_scales", align_bytes=64)
-        identity = keep.tile([P, P], F32, name="identity")
-        gate_runs = [keep.tile([P, 2, 2 * RUN], F32, name=f"gate_runs{h}") for h in range(2)]
-        gate_banks = [psum.tile([P, RUN, P], F32, name=f"gate_bank{e}") for e in range(E)]
+        zero = keep.tile([P, 1], F32, name="zero")
+        unread = keep.tile([P, 1], F32, name="unread")
+
+        nc.vector.memset(zero[:], 0.0)
+        nc.scalar.activation(unread[:], zero[:], COPY)
 
         dy = {}
-        w_raw = {}
-
-        def load_dy(g, t, first, last):
-            if first == 0:
-                place = (g * PLANES + t) * BLOCK_BYTES
-                dy[g, t] = dy_pool.tile([P, T + SPARE], F32, name=f"dy{g}{t}", offset=place, align_bytes=256)[:]
-            nc.sync.dma_start(out=dy[g, t][:, first:last], in_=dy_rows[g, t][:, first:last])
-
-        def load_w(e):
-            w_raw[e] = dy_pool.tile([P, PASSES * PLANES * K], F32, name=f"w_raw{e}", offset=e * BLOCK_BYTES, align_bytes=256)
-            nc.sync.dma_start(out=w_raw[e][:].rearrange("p (g x) -> p g x", g=PASSES), in_=w_rows[e])
-
-        def load_gate(h):
-            half = gate[0, h * HALF : (h + 1) * HALF]
-            nc.sync.dma_start(out=gate_runs[h][:, :, :RUN], in_=half.rearrange("(e p c) -> p e c", p=P, c=RUN))
-
-        load_gate(1)
-        load_dy(0, 0, 0, HALF)
-        load_dy(0, 0, HALF, T)
-        nc.sync.dma_start(out=offsets[:], in_=offs)
-        for block in range(1, PASSES * PLANES - 3):
-            load_dy(block // PLANES, block % PLANES, 0, T)
+        for block in range(PASSES * PLANES):
+            g, t = divmod(block, PLANES)
+            dy[g, t] = placed([P, T], F32, f"dy{g}{t}", 8 * block)
+            nc.sync.dma_start(out=dy[g, t][:], in_=dy_rows[g, t])
+            if block == 0:
+                nc.sync.dma_start(out=offsets[:], in_=offs)
             if block == PLANES - 1:
-                load_gate(0)
-        joined = dy_pool.tile([P, 3, T], F32, name="dy_joined", offset=(PASSES * PLANES - 3) * BLOCK_BYTES, align_bytes=256)
-        nc.sync.dma_start(out=joined[:], in_=dyT.rearrange("(g p t) c -> g p t c", p=P, t=PLANES)[2, :, 1:])
-        for t in range(1, PLANES):
-            dy[2, t] = joined[:, t - 1]
-        for e in range(E):
-            load_w(e)
-
-        middle_codes = dy_pool.tile([P, HALF], U32, name="middle_codes", offset=0, align_bytes=256)
-
-        make_identity(nc, identity[:])
-        unread = keep.tile([P, 1], F32, name="unread")
-        nc.scalar.activation(unread[:], gate_runs[1][:, 0, :1], COPY)
-        for e in (2, 3, 0, 1):
-            for c in range(RUN):
-                column = gate_runs[e // 2][:, e % 2, c : c + 1]
-                nc.tensor.transpose(gate_banks[e][:, c], column.to_broadcast([P, P]), identity[:])
-            if e >= 2:
-                target = gates[:, (e - 2) * C : (e - 1) * C].rearrange("q (p c) -> q p c", c=RUN)
-                nc.vector.tensor_copy(target, gate_banks[e][:].rearrange("q c p -> q p c"))
+                nc.sync.dma_start(out=gates[:], in_=gate[:P])
 
         def listed(window, first, last):
             return window.indirect(offsets[:, first // OFFSETS : last // OFFSETS])
 
-        def gather_plain(planes, g, which, first, last):
-            for t in which:
-                nc.scalar.activation(planes[:, t], listed(dy[g, t], first, last), COPY)
-
-        def gather_gated(planes, g, first, last):
+        for g in range(PASSES):
+            start = (96, 128, 0)[g]
+            planes = [placed([P, PLANES, HALF], F32, f"planes{g}{h}", start + 16 * h) for h in range(2)]
             for t in range(PLANES):
-                nc.vector.tensor_tensor(planes[:, t], listed(dy[g, t], first, last), gates[:, first - HALF : last - HALF], MULT)
-
-        def room(place, width):
-            return woven[:, place * C * PLANES : (place * C + width) * PLANES]
-
-        def weave(grouped, planes):
-            nc.vector.tensor_copy(
-                grouped.rearrange("p (c i t) -> p c t i", i=RUN, t=PLANES),
-                planes.rearrange("p t (c i) -> p c t i", i=RUN),
-            )
-
-        def weave_aside(grouped, planes):
-            nc.gpsimd.tensor_scalar(
-                grouped.rearrange("p (c t) -> p c t", t=PLANES), planes.rearrange("p t c -> p c t"), 1.0, 0.0, MULT, ADD
-            )
-
-        def weave_gating(grouped, planes, first, last):
-            for start in range(first, last, C):
-                width = min(C, last - start)
-                place = start - first
-                runs = gate_banks[start // C][:, :, start % C // RUN : (start % C + width) // RUN]
-                nc.vector.tensor_tensor(
-                    grouped[:, place * PLANES : (place + width) * PLANES].rearrange("p (c i t) -> p c t i", i=RUN, t=PLANES),
-                    planes[:, :, place : place + width].rearrange("p t (c i) -> p c t i", i=RUN),
-                    runs.rearrange("q i c -> q c i").unsqueeze(2).to_broadcast([P, width // RUN, PLANES, RUN]),
+                nc.scalar.activation(planes[0][:, t], listed(dy[g, t][:], 0, HALF), COPY)
+                nc.vector.tensor_copy(planes[1][:, t], listed(dy[g, t][:], HALF, SLOTS))
+            for e in range(E):
+                place = e % 2 * C
+                nc.gpsimd.tensor_tensor(
+                    woven[g][:, e * C * PLANES : (e + 1) * C * PLANES].rearrange("p (c i t) -> p c t i", i=RUN, t=PLANES),
+                    planes[e // 2][:, :, place : place + C].rearrange("p t (c i) -> p c t i", i=RUN),
+                    gates[:, e * C : (e + 1) * C]
+                    .rearrange("p (c i) -> p c i", i=RUN)
+                    .unsqueeze(2)
+                    .to_broadcast([P, C // RUN, PLANES, RUN]),
                     MULT,
                 )
 
-        def codes_of(g, first, last):
-            if g == 1 and C <= first < 3 * C:
-                return middle_codes[:, first - C : last - C]
-            return codes[:, g, first:last]
+        w_raw = placed([P, E, PASSES * PLANES * K], F32, "w_raw", 40)
+        for e in range(E):
+            nc.sync.dma_start(out=w_raw[:, e].rearrange("p (g x) -> p g x", g=PASSES), in_=w_rows[e])
+        codes = placed([P, PASSES, SLOTS], U32, "codes", 0)
+        w_woven = placed([P, E, PASSES * PLANES * K], BF16, "w_woven", 24)
+        scales = placed([P, PASSES, SLOTS], U8, "scales", 64)
+        results = placed([P, SLOTS], F32, "results", 72)
 
-        def quantise(grouped, g, first, last):
-            nc.vector.quantize_mx(
-                out=codes_of(g, first, last).bitcast(E5M2), scales=scales[:, g, first:last], in_=grouped
-            )
-
-        def weave_w(grouped, e):
+        for e in range(E):
             nc.vector.tensor_copy(
-                grouped.rearrange("p (g c i t) -> p c g t i", g=PASSES, i=RUN, t=PLANES),
-                w_raw[e][:].rearrange("p (g t c i) -> p c g t i", g=PASSES, t=PLANES, i=RUN),
+                w_woven[:, e].rearrange("p (g c i t) -> p c g t i", g=PASSES, i=RUN, t=PLANES),
+                w_raw[:, e].rearrange("p (g t c i) -> p c g t i", g=PASSES, t=PLANES, i=RUN),
             )
-
-        def weave_w_aside(grouped, e):
-            nc.gpsimd.tensor_scalar(
-                grouped.rearrange("p (g k t) -> p g k t", g=PASSES, t=PLANES),
-                w_raw[e][:].rearrange("p (g t k) -> p g k t", g=PASSES, t=PLANES),
-                1.0,
-                0.0,
-                MULT,
-                ADD,
-            )
-
-        def quantise_w(grouped, e):
-            nc.vector.quantize_mx(out=w_codes[:, e].bitcast(E4M3), scales=w_scales[:, e], in_=grouped)
-
-        def multiply(first, last, order):
-            e = first // C
-            bank = psum.tile([P, last - first], F32, name=f"bank{(first + PIECE) // C % E}")
-            for g in order:
+        for e in range(E):
+            nc.vector.quantize_mx(out=w_codes[:, e].bitcast(E4M3), scales=w_scales[:, e], in_=w_woven[:, e])
+        for h in range(2):
+            for g in range(PASSES):
+                nc.vector.quantize_mx(
+                    out=codes[:, g, h * HALF : (h + 1) * HALF].bitcast(E5M2),
+                    scales=scales[:, g, h * HALF : (h + 1) * HALF],
+                    in_=woven[g][:, h * HALF * PLANES : (h + 1) * HALF * PLANES],
+                )
+        for e in range(E):
+            bank = psum.tile([P, C], F32, name=f"bank{e}")
+            for g in range(PASSES):
                 nc.tensor.matmul_mx(
                     out=bank[:],
                     lhsT=w_codes[:, e, g * K : (g + 1) * K].bitcast(E4M3),
                     lhsT_scale=w_scales[:, e, g * K : (g + 1) * K],
-                    rhs=codes_of(g, first, last).bitcast(E5M2),
-                    rhs_scale=scales[:, g, first:last],
-                    start=(g == order[0]),
-                    stop=(g == order[-1]),
+                    rhs=codes[:, g, e * C : (e + 1) * C].bitcast(E5M2),
+                    rhs_scale=scales[:, g, e * C : (e + 1) * C],
+                    start=(g == 0),
+                    stop=(g == PASSES - 1),
                 )
-            return bank
-
-        def scatter(first, last):
-            for start, end in zip(SCATTERS, SCATTERS[1:]):
-                if first < end <= last:
-                    nc.scalar.activation(listed(tokens[:], start, end), results[:, start:end], COPY)
-
-        gather_plain(outer[0], 0, range(PLANES), 0, HALF)
-        gather_gated(gated, 0, HALF, SLOTS)
-        seam = 2 * PLANES * HALF - OWN * PLANES
-        upper = halves[:].rearrange("p t c -> p (t c)").bitcast(BF16)[:, seam : seam + HALF * PLANES]
-        weave_aside(upper[:, OWN * PLANES :], gated[:, :, OWN:])
-        weave_gating(room(2, HALF), outer[0], 0, HALF)
-        weave(upper[:, : OWN * PLANES], gated[:, :, :OWN])
-        quantise(room(2, HALF), 0, 0, HALF)
-        quantise(upper[:, C * PLANES :], 0, HALF + C, SLOTS)
-        quantise(upper[:, : C * PLANES], 0, HALF, HALF + C)
-
-        gather_plain(inner, 1, range(PLANES), 0, HALF)
-        gather_gated(gated[:, :, : HALF - PIECE], 1, HALF, SLOTS - PIECE)
-        weave_aside(room(2, C), gated[:, :, :C])
-        weave_gating(room(0, HALF), inner[:], 0, HALF)
-        quantise(room(0, C), 1, 0, C)
-
-        gather_plain(outer[0], 2, [0], 0, HALF)
-        gather_plain(outer[1], 2, [0], HALF, SLOTS)
-        gather_plain(outer[0], 2, [1, 2], 0, HALF)
-        for first in (0, C):
-            gather_plain(outer[0][:, :, first : first + C], 2, [PLANES - 1], first, first + C)
-        gather_plain(outer[1], 2, [1, 2, 3], HALF, SLOTS)
-
-        def spent(e, width):
-            return w_raw[e][:].bitcast(BF16)[:, : width * PLANES]
-
-        def weave_pass_2(grouped, first, last):
-            weave_gating(grouped, outer[first // HALF][:, :, first % HALF : first % HALF + last - first], first, last)
-
-        size = PASSES * K * PLANES
-        start = 3 * C * PLANES
-        w_grouped = [woven[:, start : start + size]] * 3 + [woven[:, start - size // 2 : start + size // 2]]
-
-        def finish(bank, first, last):
-            nc.vector.tensor_copy(results[:, first:last], bank[:])
-            scatter(first, last)
-
-        def finish_on_scalar(bank, first, last):
-            nc.scalar.copy(out=results[:, first:last], in_=bank[:])
-            scatter(first, last)
-
-        weave_w(w_grouped[0], 0)
-        quantise_w(w_grouped[0], 0)
-        weave_w_aside(w_grouped[1], 1)
-        weave_pass_2(spent(0, C), 0, C)
-        quantise(spent(0, C), 2, 0, C)
-        bank = multiply(0, C, (0, 1, 2))
-        for e in (1, 2):
-            first, middle, last = e * C, e * C + PIECE, (e + 1) * C
-            quantise_w(w_grouped[e], e)
-            weave_w_aside(w_grouped[e + 1], e + 1)
-            weave_pass_2(spent(e, PIECE), first, middle)
-            finish(bank, first - C, first)
-            weave_pass_2(spent(e, C)[:, PIECE * PLANES :], middle, last)
-            if e == 1:
-                quantise(room(1, HALF), 1, C, 3 * C)
-            quantise(spent(e, C), 2, first, last)
-            bank = multiply(first, last, (0, 1, 2))
-        first, last = 3 * C, SLOTS - PIECE
-        quantise_w(w_grouped[3], 3)
-        earlier = w_grouped[3][:, : PIECE * PLANES]
-        weave_aside(earlier, gated[:, :, first - HALF : last - HALF])
-        weave_pass_2(spent(3, PIECE), first, last)
-        finish(bank, first - C, first)
-        quantise(spent(3, PIECE), 2, first, last)
-        quantise(earlier, 1, first, last)
-        finish_on_scalar(multiply(first, last, (0, 2, 1)), first, last)
-        first, last = SLOTS - PIECE, SLOTS
-        late = outer[1][:, :, :PIECE]
-        gather_gated(late, 1, first, last)
-        weave_pass_2(spent(2, PIECE), first, last)
-        weave(room(0, PIECE), late)
-        quantise(spent(2, PIECE), 2, first, last)
-        quantise(room(0, PIECE), 1, first, last)
-        nc.vector.tensor_copy(results[:, first:last], multiply(first, last, (0, 2, 1))[:])
-        nc.vector.tensor_copy(listed(tokens[:], first, last), results[:, first:last])
-
+            nc.scalar.copy(out=results[:, e * C : (e + 1) * C], in_=bank[:])
+        for h in range(2):
+            nc.vector.tensor_copy(listed(tokens[:], h * HALF, (h + 1) * HALF), results[:, h * HALF : (h + 1) * HALF])
         for q, queue in enumerate((nc.sync, nc.scalar, nc.sync, nc.scalar)):
             queue.dma_start(out=out[:, q * C : (q + 1) * C], in_=tokens[:, q * C : (q + 1) * C])

@@ -1,6 +1,7 @@
 from contextlib import ExitStack
 
 import concourse.mybir as mybir
+from concourse.masks import make_identity
 
 K, T, E, C, N = 128, 2048, 4, 512, 1536
 SLOTS = E * C
@@ -11,6 +12,7 @@ OFFSETS = 16
 HALF = SLOTS // 2
 RUN = 4
 PIECE = 256
+LATE = SLOTS - PIECE
 KIB = 1024
 
 FLOPS = 2 * K * N * SLOTS
@@ -24,6 +26,7 @@ U8 = mybir.dt.uint8
 E4M3 = mybir.dt.float8_e4m3fn_x4
 E5M2 = mybir.dt.float8_e5m2_x4
 MULT = mybir.AluOpType.mult
+ADD = mybir.AluOpType.add
 COPY = mybir.ActivationFunctionType.Copy
 
 
@@ -35,91 +38,268 @@ def tile_moe_bdx_lin_none_kernel(tc, dyT, w, gate, offs, out):
     with ExitStack() as ctx:
         lists = ctx.enter_context(tc.tile_pool(name="lists", bufs=1))
         keep = ctx.enter_context(tc.tile_pool(name="keep", bufs=1))
-        room = ctx.enter_context(tc.tile_pool(name="room", bufs=1))
+        shared = ctx.enter_context(tc.tile_pool(name="shared", bufs=1))
         psum = ctx.enter_context(tc.psum_pool(name="psum", bufs=1))
 
         def placed(shape, dtype, name, kib):
-            return room.tile(shape, dtype, name=name, offset=kib * KIB, align_bytes=256)
+            return shared.tile(shape, dtype, name=name, offset=int(kib * KIB), align_bytes=256)
 
         offsets = lists.tile([P, SLOTS // OFFSETS], U16, name="offsets")
-        gates = keep.tile([P, SLOTS], F32, name="gates", align_bytes=256)
+        gates = keep.tile([P, HALF], F32, name="gates", align_bytes=256)
         tokens = keep.tile([P, T], F32, name="tokens", align_bytes=256)
-        woven = [keep.tile([P, SLOTS * PLANES], BF16, name=f"woven{g}", align_bytes=256) for g in range(PASSES)]
-        w_codes = keep.tile([P, E, PASSES * K], U32, name="w_codes", align_bytes=64)
+        lower = keep.tile([P, PLANES, HALF], F32, name="lower", align_bytes=256)
+        early = keep.tile([P, 6 * HALF], F32, name="early", align_bytes=256)
+        later = keep.tile([P, C + 3 * PLANES * C], F32, name="later", align_bytes=256)
+        woven = keep.tile([P, 8 * C * PLANES], BF16, name="woven", align_bytes=64)
+        first_codes = keep.tile([P, 3 * C], U32, name="first_codes", align_bytes=64)
+        scales = keep.tile([P, PASSES, SLOTS], U8, name="scales", align_bytes=64)
         w_scales = keep.tile([P, E, PASSES * K], U8, name="w_scales", align_bytes=64)
-        zero = keep.tile([P, 1], F32, name="zero")
-        unread = keep.tile([P, 1], F32, name="unread")
+        identity = keep.tile([P, P], F32, name="identity")
+        gate_runs = [keep.tile([P, 2, 2 * RUN], F32, name=f"gate_runs{h}") for h in range(2)]
+        gate_banks = [psum.tile([P, RUN, P], F32, name=f"gate_bank{e}") for e in range(E)]
 
-        nc.vector.memset(zero[:], 0.0)
-        nc.scalar.activation(unread[:], zero[:], COPY)
+        def planes_in(tile, start, width):
+            return tile[:, start : start + PLANES * width].rearrange("p (t c) -> p t c", t=PLANES)
+
+        lower_1 = planes_in(early, 0, HALF)
+        upper_0 = planes_in(early, 2 * HALF, HALF)
+        upper_2 = planes_in(later, C, C)
+        upper_1 = {e: planes_in(later, C + (e - 1) * PLANES * C, C) for e in (2, 3)}
 
         dy = {}
+        w_raw = {}
+
+        def load_gate(h):
+            half = gate[0, h * HALF : (h + 1) * HALF]
+            nc.sync.dma_start(out=gate_runs[h][:, :, :RUN], in_=half.rearrange("(e p c) -> p e c", p=P, c=RUN))
+
+        load_gate(1)
         for block in range(PASSES * PLANES):
             g, t = divmod(block, PLANES)
-            dy[g, t] = placed([P, T], F32, f"dy{g}{t}", 8 * block)
-            nc.sync.dma_start(out=dy[g, t][:], in_=dy_rows[g, t])
+            if (g, t) == (1, 3):
+                continue
+            if (g, t) == (1, 2):
+                pair = placed([P, 2, T], F32, "dy_pair", 8 * block)
+                nc.sync.dma_start(out=pair[:], in_=dyT.rearrange("(g p t) c -> g p t c", p=P, t=PLANES)[1, :, 2:])
+                dy[1, 2], dy[1, 3] = pair[:, 0], pair[:, 1]
+                continue
+            dy[g, t] = placed([P, T], F32, f"dy{g}{t}", 8 * block)[:]
             if block == 0:
+                for h in range(2):
+                    nc.sync.dma_start(out=dy[g, t][:, h * HALF : (h + 1) * HALF], in_=dy_rows[g, t][:, h * HALF : (h + 1) * HALF])
                 nc.sync.dma_start(out=offsets[:], in_=offs)
+            else:
+                nc.sync.dma_start(out=dy[g, t], in_=dy_rows[g, t])
             if block == PLANES - 1:
-                nc.sync.dma_start(out=gates[:], in_=gate[:P])
+                load_gate(0)
+        for e in range(E):
+            if e == 0:
+                tail = placed([P, PLANES, K], F32, "w_tail", 4)
+                w_raw[e] = planes_in(later, 0, C)[:, :, : 2 * K]
+                targets = [w_raw[e][:, :, :K], w_raw[e][:, :, K:], tail[:]]
+            else:
+                w_raw[e] = placed([P, PLANES, PASSES * K], F32, f"w_raw{e}", 8 * e)[:]
+                targets = [w_raw[e][:, :, g * K : (g + 1) * K] for g in range(PASSES)]
+            for g in range(PASSES):
+                nc.sync.dma_start(out=targets[g], in_=w_rows[e, :, g].rearrange("p (t k) -> p t k", t=PLANES))
+
+        results = placed([P, SLOTS], F32, "results", 32)
+        last_codes = [placed([P, C], U32, f"last_codes{e}", place) for e, place in enumerate((52, 46, 40, 42))]
+        middle_codes = [placed([P, C], U32, f"middle_codes{e}", place) for e, place in enumerate((4, 16, 18, 24))]
+        held_codes = placed([P, C], U32, "held_codes", 26)
+        held_scales = placed([P, C], U8, "held_scales", 21.5)
+        w_codes = [placed([P, PASSES * K], U32, f"w_codes{e}", place) for e, place in enumerate((44, 20, 48, 50))]
+
+        make_identity(nc, identity[:])
+        unread = keep.tile([P, 1], F32, name="unread")
+        nc.scalar.activation(unread[:], gate_runs[1][:, 0, :1], COPY)
+        for e in (2, 3, 0, 1):
+            for c in range(RUN):
+                column = gate_runs[e // 2][:, e % 2, c : c + 1]
+                nc.tensor.transpose(gate_banks[e][:, c], column.to_broadcast([P, P]), identity[:])
+            if e >= 2:
+                target = gates[:, (e - 2) * C : (e - 1) * C].rearrange("q (p c) -> q p c", c=RUN)
+                nc.vector.tensor_copy(target, gate_banks[e][:].rearrange("q c p -> q p c"))
 
         def listed(window, first, last):
             return window.indirect(offsets[:, first // OFFSETS : last // OFFSETS])
 
-        for g in range(PASSES):
-            start = (96, 128, 0)[g]
-            planes = [placed([P, PLANES, HALF], F32, f"planes{g}{h}", start + 16 * h) for h in range(2)]
+        def gather_on_scalar(plane, g, t, first, last):
+            nc.scalar.activation(plane, listed(dy[g, t], first, last), COPY)
+
+        def gather_on_vector(plane, g, t, first, last):
+            nc.vector.tensor_copy(plane, listed(dy[g, t], first, last))
+
+        def gather_gated(planes, g, first, last):
             for t in range(PLANES):
-                nc.scalar.activation(planes[0][:, t], listed(dy[g, t][:], 0, HALF), COPY)
-                nc.vector.tensor_copy(planes[1][:, t], listed(dy[g, t][:], HALF, SLOTS))
-            for e in range(E):
-                place = e % 2 * C
-                nc.gpsimd.tensor_tensor(
-                    woven[g][:, e * C * PLANES : (e + 1) * C * PLANES].rearrange("p (c i t) -> p c t i", i=RUN, t=PLANES),
-                    planes[e // 2][:, :, place : place + C].rearrange("p t (c i) -> p c t i", i=RUN),
-                    gates[:, e * C : (e + 1) * C]
-                    .rearrange("p (c i) -> p c i", i=RUN)
-                    .unsqueeze(2)
-                    .to_broadcast([P, C // RUN, PLANES, RUN]),
-                    MULT,
-                )
+                nc.vector.tensor_tensor(planes[:, t], listed(dy[g, t], first, last), gates[:, first - HALF : last - HALF], MULT)
 
-        w_raw = placed([P, E, PASSES * PLANES * K], F32, "w_raw", 40)
-        for e in range(E):
-            nc.sync.dma_start(out=w_raw[:, e].rearrange("p (g x) -> p g x", g=PASSES), in_=w_rows[e])
-        codes = placed([P, PASSES, SLOTS], U32, "codes", 0)
-        w_woven = placed([P, E, PASSES * PLANES * K], BF16, "w_woven", 24)
-        scales = placed([P, PASSES, SLOTS], U8, "scales", 64)
-        results = placed([P, SLOTS], F32, "results", 72)
+        def room(place, width):
+            return woven[:, place * PLANES : (place + width) * PLANES]
 
-        for e in range(E):
-            nc.vector.tensor_copy(
-                w_woven[:, e].rearrange("p (g c i t) -> p c g t i", g=PASSES, i=RUN, t=PLANES),
-                w_raw[:, e].rearrange("p (g t c i) -> p c g t i", g=PASSES, t=PLANES, i=RUN),
+        def in_runs(grouped, planes):
+            return (
+                grouped.rearrange("p (c i t) -> p c t i", i=RUN, t=PLANES),
+                planes.rearrange("p t (c i) -> p c t i", i=RUN),
             )
-        for e in range(E):
-            nc.vector.quantize_mx(out=w_codes[:, e].bitcast(E4M3), scales=w_scales[:, e], in_=w_woven[:, e])
-        for h in range(2):
-            for g in range(PASSES):
-                nc.vector.quantize_mx(
-                    out=codes[:, g, h * HALF : (h + 1) * HALF].bitcast(E5M2),
-                    scales=scales[:, g, h * HALF : (h + 1) * HALF],
-                    in_=woven[g][:, h * HALF * PLANES : (h + 1) * HALF * PLANES],
-                )
-        for e in range(E):
-            bank = psum.tile([P, C], F32, name=f"bank{e}")
-            for g in range(PASSES):
+
+        def weave(grouped, planes):
+            nc.vector.tensor_copy(*in_runs(grouped, planes))
+
+        def weave_aside(grouped, planes):
+            nc.gpsimd.tensor_scalar(*in_runs(grouped, planes), 1.0, 0.0, MULT, ADD)
+
+        def weave_gating(grouped, planes, first, last):
+            width = last - first
+            runs = gate_banks[first // C][:, :, first % C // RUN : (first % C + width) // RUN]
+            spread = runs.rearrange("q i c -> q c i").unsqueeze(2).to_broadcast([P, width // RUN, PLANES, RUN])
+            nc.vector.tensor_tensor(*in_runs(grouped, planes), spread, MULT)
+
+        def weave_gating_aside(grouped, planes, first, last):
+            columns = gates[:, first - HALF : last - HALF]
+            runs = columns.rearrange("q (c i) -> q c i", i=RUN)
+            spread = runs.unsqueeze(2).to_broadcast([P, (last - first) // RUN, PLANES, RUN])
+            nc.gpsimd.tensor_tensor(*in_runs(grouped, planes), spread, MULT)
+
+        def codes_of(g, first, last):
+            e = first // C
+            if g == 2:
+                return last_codes[e][:, first - e * C : last - e * C]
+            if g == 1:
+                return middle_codes[e][:, first - e * C : last - e * C]
+            if e == E - 1:
+                return held_codes[:, first - e * C : last - e * C]
+            return first_codes[:, first:last]
+
+        def scales_of(g, first, last):
+            if (g, first) == (2, C):
+                return held_scales[:]
+            return scales[:, g, first:last]
+
+        def quantise(grouped, g, first, last):
+            nc.vector.quantize_mx(out=codes_of(g, first, last).bitcast(E5M2), scales=scales_of(g, first, last), in_=grouped)
+
+        def weave_w(grouped, e):
+            weave_aside(grouped, w_raw[e])
+
+        def quantise_w(grouped, e):
+            nc.vector.quantize_mx(out=w_codes[e][:].bitcast(E4M3), scales=w_scales[:, e], in_=grouped)
+
+        def multiply(first, last, order):
+            e = first // C
+            bank = psum.tile([P, last - first], F32, name=f"bank{(first + PIECE) // C % E}")
+            for g in order:
                 nc.tensor.matmul_mx(
                     out=bank[:],
-                    lhsT=w_codes[:, e, g * K : (g + 1) * K].bitcast(E4M3),
+                    lhsT=w_codes[e][:, g * K : (g + 1) * K].bitcast(E4M3),
                     lhsT_scale=w_scales[:, e, g * K : (g + 1) * K],
-                    rhs=codes[:, g, e * C : (e + 1) * C].bitcast(E5M2),
-                    rhs_scale=scales[:, g, e * C : (e + 1) * C],
-                    start=(g == 0),
-                    stop=(g == PASSES - 1),
+                    rhs=codes_of(g, first, last).bitcast(E5M2),
+                    rhs_scale=scales_of(g, first, last),
+                    start=(g == order[0]),
+                    stop=(g == order[-1]),
                 )
-            nc.scalar.copy(out=results[:, e * C : (e + 1) * C], in_=bank[:])
-        for h in range(2):
-            nc.vector.tensor_copy(listed(tokens[:], h * HALF, (h + 1) * HALF), results[:, h * HALF : (h + 1) * HALF])
+            return bank
+
+        def empty_on_scalar(bank, start, first, last):
+            nc.scalar.copy(out=results[:, first:last], in_=bank[:, first - start : last - start])
+
+        def empty_on_vector(bank, start, first, last):
+            nc.vector.tensor_copy(results[:, first:last], bank[:, first - start : last - start])
+
+        def scatter(first, last):
+            nc.scalar.activation(listed(tokens[:], first, last), results[:, first:last], COPY)
+
+        for t in range(PLANES - 1):
+            gather_on_scalar(lower[:, t], 0, t, 0, HALF)
+        for e in range(2):
+            gather_on_scalar(lower[:, 3, e * C : (e + 1) * C], 0, 3, e * C, (e + 1) * C)
+        gather_gated(upper_0, 0, HALF, SLOTS)
+        weave_aside(room(HALF, LATE - HALF), upper_0[:, :, : LATE - HALF])
+        for e in range(2):
+            weave_gating(room(e * C, C), lower[:, :, e * C : (e + 1) * C], e * C, (e + 1) * C)
+        quantise(room(2 * C, C), 0, 2 * C, 3 * C)
+        quantise(room(0, HALF), 0, 0, HALF)
+        weave_aside(room(0, PIECE), upper_0[:, :, LATE - HALF :])
+
+        w_width = PASSES * K
+        w_start = LATE + HALF
+        middle_room = [room(w_start + w_width - PIECE, C), room(C, C), room(LATE, C), room(LATE + C, C)]
+        w_grouped = [room(HALF - w_width // 2, w_width), room(w_start, w_width)]
+        for t in range(2):
+            for e in (2, 3):
+                gather_on_scalar(upper_1[e][:, t], 1, t, e * C, (e + 1) * C)
+            gather_on_scalar(lower_1[:, t], 1, t, 0, HALF)
+        for e in (2, 3):
+            for t in (2, 3):
+                gather_on_vector(upper_1[e][:, t], 1, t, e * C, (e + 1) * C)
+            weave_gating_aside(middle_room[e], upper_1[e], e * C, (e + 1) * C)
+        for t in (2, 3):
+            gather_on_vector(lower_1[:, t], 1, t, 0, HALF)
+        weave_gating(middle_room[0], lower_1[:, :, :C], 0, C)
+
+        weave_aside(w_grouped[0][:, : 2 * K * PLANES], w_raw[0])
+        weave_aside(w_grouped[0][:, 2 * K * PLANES :], tail[:])
+        for t in range(PLANES - 1):
+            gather_on_scalar(lower[:, t], 2, t, 0, HALF)
+        for e in range(2):
+            gather_on_scalar(lower[:, 3, e * C : (e + 1) * C], 2, 3, e * C, (e + 1) * C)
+        for t in (3, 0, 1, 2):
+            gather_on_scalar(upper_2[:, t], 2, t, HALF, HALF + C)
+        first = 3 * C
+
+        weave_gating(room(7 * C, C), lower[:, :, :C], 0, C)
+        quantise_w(w_grouped[0], 0)
+        quantise(room(7 * C, C), 2, 0, C)
+        quantise(middle_room[0], 1, 0, C)
+        bank = multiply(0, C, (0, 1, 2))
+        empty_on_scalar(bank, 0, 0, C)
+        ending = placed([P, 7 * PIECE], F32, "ending", 52)
+        late = planes_in(ending, 0, PIECE)
+        w_grouped.extend(ending[:, at * PIECE : (at + 3) * PIECE].bitcast(BF16) for at in (2, 4))
+        for t in range(2):
+            gather_on_scalar(late[:, t], 2, t, first, LATE)
+            scatter(t * PIECE, (t + 1) * PIECE)
+
+        weave_w(w_grouped[1], 1)
+        weave_w(w_grouped[2], 2)
+        weave_gating(middle_room[1], lower_1[:, :, C:], C, 2 * C)
+        weave_gating(room(HALF, C), lower[:, :, C:], C, 2 * C)
+        quantise_w(w_grouped[1], 1)
+        quantise(middle_room[1], 1, C, 2 * C)
+        quantise(room(HALF, C), 2, C, 2 * C)
+        quantise(middle_room[2], 1, 2 * C, 3 * C)
+        quantise_w(w_grouped[2], 2)
+        bank = multiply(C, 2 * C, (0, 1, 2))
+        empty_on_scalar(bank, C, C, C + PIECE)
+        empty_on_scalar(bank, C, C + PIECE, 2 * C)
+        scatter(C, C + PIECE)
+        gather_on_scalar(late[:, 2], 2, 2, first, LATE)
+        scatter(C + PIECE, 2 * C)
+
+        weave_w(w_grouped[3], 3)
+        weave_gating(room(HALF, C), upper_2, 2 * C, 3 * C)
+        gather_on_vector(late[:, 3], 2, 3, first, LATE)
+        quantise(room(HALF, C), 2, 2 * C, 3 * C)
+        quantise_w(w_grouped[3], 3)
+        quantise(room(LATE + C, PIECE), 1, first, LATE)
+        bank = multiply(2 * C, 3 * C, (0, 1, 2))
+        middle = (HALF + LATE) // 2
+        empty_on_scalar(bank, HALF, HALF, middle)
+        empty_on_scalar(bank, HALF, middle, first)
+        scatter(HALF, middle)
+
+        weave_gating(room(HALF, PIECE), late, first, LATE)
+        quantise(room(first, PIECE), 0, first, LATE)
+        quantise(room(HALF, PIECE), 2, first, LATE)
+        empty_on_scalar(multiply(first, LATE, (1, 0, 2)), first, first, LATE)
+        scatter(middle, LATE)
+        gather_gated(late, 2, LATE, SLOTS)
+        quantise(room(0, PIECE), 0, LATE, SLOTS)
+        weave(room(HALF + PIECE, PIECE), late)
+        quantise(room(LATE + C + PIECE, PIECE), 1, LATE, SLOTS)
+        quantise(room(HALF + PIECE, PIECE), 2, LATE, SLOTS)
+        nc.vector.tensor_copy(results[:, LATE:], multiply(LATE, SLOTS, (0, 1, 2))[:])
+        nc.vector.tensor_copy(listed(tokens[:], LATE, SLOTS), results[:, LATE:])
+
         for q, queue in enumerate((nc.sync, nc.scalar, nc.sync, nc.scalar)):
             queue.dma_start(out=out[:, q * C : (q + 1) * C], in_=tokens[:, q * C : (q + 1) * C])

@@ -13,7 +13,10 @@ HALF = SLOTS // 2
 RUN = 4
 PIECE = 256
 LATE = SLOTS - PIECE
+W_WIDTH = PASSES * K
 KIB = 1024
+
+TURN = {(1, 0): 2, (1, 1): 2, (1, 2): 1, (2, 2): 3}
 
 FLOPS = 2 * K * N * SLOTS
 BYTES = 4 * (N * T + E * N * K + SLOTS + K * T) + 2 * SLOTS
@@ -32,8 +35,8 @@ COPY = mybir.ActivationFunctionType.Copy
 
 def tile_moe_bdx_lin_none_kernel(tc, dyT, w, gate, offs, out):
     nc = tc.nc
-    dy_rows = dyT.rearrange("(g p t) c -> g t p c", p=P, t=PLANES)
-    w_rows = w.rearrange("e (g p t) k -> e p g (t k)", p=P, t=PLANES)
+    dy_rows = dyT.rearrange("(g p t) c -> g p t c", p=P, t=PLANES)
+    w_rows = w.rearrange("e (g p t) k -> e g p t k", p=P, t=PLANES)
 
     with ExitStack() as ctx:
         lists = ctx.enter_context(tc.tile_pool(name="lists", bufs=1))
@@ -42,18 +45,17 @@ def tile_moe_bdx_lin_none_kernel(tc, dyT, w, gate, offs, out):
         psum = ctx.enter_context(tc.psum_pool(name="psum", bufs=1))
 
         def placed(shape, dtype, name, kib):
-            return shared.tile(shape, dtype, name=name, offset=int(kib * KIB), align_bytes=256)
+            return shared.tile(shape, dtype, name=name, offset=kib * KIB, align_bytes=256)
 
         offsets = lists.tile([P, SLOTS // OFFSETS], U16, name="offsets")
         gates = keep.tile([P, HALF], F32, name="gates", align_bytes=256)
         tokens = keep.tile([P, T], F32, name="tokens", align_bytes=256)
-        lower = keep.tile([P, PLANES, HALF], F32, name="lower", align_bytes=256)
-        early = keep.tile([P, 6 * HALF], F32, name="early", align_bytes=256)
-        later = keep.tile([P, C + 3 * PLANES * C], F32, name="later", align_bytes=256)
+        outer = keep.tile([P, PLANES * (HALF + C) + PIECE], F32, name="outer", align_bytes=256)
+        inner = keep.tile([P, 2 * HALF + PLANES * SLOTS], F32, name="inner", align_bytes=256)
         woven = keep.tile([P, 8 * C * PLANES], BF16, name="woven", align_bytes=64)
         first_codes = keep.tile([P, 3 * C], U32, name="first_codes", align_bytes=64)
-        scales = keep.tile([P, PASSES, SLOTS], U8, name="scales", align_bytes=64)
-        w_scales = keep.tile([P, E, PASSES * K], U8, name="w_scales", align_bytes=64)
+        scales = keep.tile([P, PASSES * SLOTS], U8, name="scales", align_bytes=64)
+        w_scales = keep.tile([P, E, W_WIDTH], U8, name="w_scales", align_bytes=64)
         identity = keep.tile([P, P], F32, name="identity")
         gate_runs = [keep.tile([P, 2, 2 * RUN], F32, name=f"gate_runs{h}") for h in range(2)]
         gate_banks = [psum.tile([P, RUN, P], F32, name=f"gate_bank{e}") for e in range(E)]
@@ -61,54 +63,60 @@ def tile_moe_bdx_lin_none_kernel(tc, dyT, w, gate, offs, out):
         def planes_in(tile, start, width):
             return tile[:, start : start + PLANES * width].rearrange("p (t c) -> p t c", t=PLANES)
 
-        lower_1 = planes_in(early, 0, HALF)
-        upper_0 = planes_in(early, 2 * HALF, HALF)
-        upper_2 = planes_in(later, C, C)
-        upper_1 = {e: planes_in(later, C + (e - 1) * PLANES * C, C) for e in (2, 3)}
+        lower = planes_in(outer, 0, HALF)
+        expert_2 = planes_in(outer, PLANES * HALF, C)
+        upper = planes_in(inner, 0, HALF)
+        start = 2 * HALF
+        lower_1 = planes_in(inner, start, HALF)
+        upper_1 = {e: planes_in(inner, start + PLANES * e * C, C) for e in (2, 3)}
 
         dy = {}
-        w_raw = {}
 
         def load_gate(h):
             half = gate[0, h * HALF : (h + 1) * HALF]
             nc.sync.dma_start(out=gate_runs[h][:, :, :RUN], in_=half.rearrange("(e p c) -> p e c", p=P, c=RUN))
 
+        def load_dy(g, t, cuts):
+            dy[g, t] = placed([P, T], F32, f"dy{g}{t}", 8 * (PLANES * g + t))[:]
+            for first, last in zip(cuts, cuts[1:]):
+                nc.sync.dma_start(out=dy[g, t][:, first:last], in_=dy_rows[g, :, t, first:last])
+
+        def load_w(target, g, e):
+            turn = TURN.get((g, e), 0)
+            nc.sync.dma_start(out=target[:, : PLANES - turn], in_=w_rows[e, g, :, turn:])
+            if turn:
+                nc.sync.dma_start(out=target[:, PLANES - turn :], in_=w_rows[e, g, :, :turn])
+
         load_gate(1)
-        for block in range(PASSES * PLANES):
-            g, t = divmod(block, PLANES)
-            if (g, t) == (1, 3):
-                continue
-            if (g, t) == (1, 2):
-                pair = placed([P, 2, T], F32, "dy_pair", 8 * block)
-                nc.sync.dma_start(out=pair[:], in_=dyT.rearrange("(g p t) c -> g p t c", p=P, t=PLANES)[1, :, 2:])
-                dy[1, 2], dy[1, 3] = pair[:, 0], pair[:, 1]
-                continue
-            dy[g, t] = placed([P, T], F32, f"dy{g}{t}", 8 * block)[:]
-            if block == 0:
-                for h in range(2):
-                    nc.sync.dma_start(out=dy[g, t][:, h * HALF : (h + 1) * HALF], in_=dy_rows[g, t][:, h * HALF : (h + 1) * HALF])
-                nc.sync.dma_start(out=offsets[:], in_=offs)
-            else:
-                nc.sync.dma_start(out=dy[g, t], in_=dy_rows[g, t])
-            if block == PLANES - 1:
-                load_gate(0)
-        for e in range(E):
-            if e == 0:
-                tail = placed([P, PLANES, K], F32, "w_tail", 4)
-                w_raw[e] = planes_in(later, 0, C)[:, :, : 2 * K]
-                targets = [w_raw[e][:, :, :K], w_raw[e][:, :, K:], tail[:]]
-            else:
-                w_raw[e] = placed([P, PLANES, PASSES * K], F32, f"w_raw{e}", 8 * e)[:]
-                targets = [w_raw[e][:, :, g * K : (g + 1) * K] for g in range(PASSES)]
+        load_dy(0, 0, (0, HALF, T))
+        nc.sync.dma_start(out=offsets[:], in_=offs)
+        for t in range(1, PLANES):
+            load_dy(0, t, (0, T))
+        load_gate(0)
+        for t in range(2):
+            load_dy(1, t, (0, T))
+        pair = placed([P, 2, T], F32, "dy_pair", 8 * (PLANES + 2))
+        nc.sync.dma_start(out=pair[:], in_=dy_rows[1, :, 2:])
+        dy[1, 2], dy[1, 3] = pair[:, 0], pair[:, 1]
+        for t in range(PLANES):
+            load_dy(2, t, (0, T))
+
+        w_front = outer[:, PLANES * HALF + C - PIECE :].rearrange("p (t c) -> p t c", t=PLANES)[:, :, PIECE:]
+        w_back = placed([P, PLANES, K], F32, "w_back", 0)
+        for g in range(2):
+            load_w(w_front[:, :, g * K : (g + 1) * K], g, 0)
+        load_w(w_back[:], 2, 0)
+        w_raw = {e: placed([P, PLANES, W_WIDTH], F32, f"w_raw{e}", 8 * e) for e in range(1, E)}
+        for e in range(1, E):
             for g in range(PASSES):
-                nc.sync.dma_start(out=targets[g], in_=w_rows[e, :, g].rearrange("p (t k) -> p t k", t=PLANES))
+                load_w(w_raw[e][:, :, g * K : (g + 1) * K], g, e)
 
         results = placed([P, SLOTS], F32, "results", 32)
-        last_codes = [placed([P, C], U32, f"last_codes{e}", place) for e, place in enumerate((52, 46, 40, 42))]
-        middle_codes = [placed([P, C], U32, f"middle_codes{e}", place) for e, place in enumerate((4, 16, 18, 24))]
-        held_codes = placed([P, C], U32, "held_codes", 26)
-        held_scales = placed([P, C], U8, "held_scales", 21.5)
-        w_codes = [placed([P, PASSES * K], U32, f"w_codes{e}", place) for e, place in enumerate((44, 20, 48, 50))]
+        codes_0 = placed([P, 2 * C], U32, "codes_0", 0)
+        codes_1 = placed([P, 2 * C], U32, "codes_1", 14)
+        codes_2 = [placed([P, C], U32, f"codes_2{g}", place) for g, place in ((1, 18), (2, 40))]
+        codes_3 = [placed([P, 2 * C], U32, "codes_3", 24), placed([P, C], U32, "codes_32", 42)]
+        w_codes = [placed([P, W_WIDTH], U32, f"w_codes{e}", place) for e, place in enumerate((44, 20, 48, 50))]
 
         make_identity(nc, identity[:])
         unread = keep.tile([P, 1], F32, name="unread")
@@ -124,11 +132,11 @@ def tile_moe_bdx_lin_none_kernel(tc, dyT, w, gate, offs, out):
         def listed(window, first, last):
             return window.indirect(offsets[:, first // OFFSETS : last // OFFSETS])
 
-        def gather_on_scalar(plane, g, t, first, last):
-            nc.scalar.activation(plane, listed(dy[g, t], first, last), COPY)
+        def gather_on_scalar(target, g, t, first, last):
+            nc.scalar.activation(target, listed(dy[g, t], first, last), COPY)
 
-        def gather_on_vector(plane, g, t, first, last):
-            nc.vector.tensor_copy(plane, listed(dy[g, t], first, last))
+        def gather_on_vector(target, g, t, first, last):
+            nc.vector.tensor_copy(target, listed(dy[g, t], first, last))
 
         def gather_gated(planes, g, first, last):
             for t in range(PLANES):
@@ -161,144 +169,132 @@ def tile_moe_bdx_lin_none_kernel(tc, dyT, w, gate, offs, out):
             spread = runs.unsqueeze(2).to_broadcast([P, (last - first) // RUN, PLANES, RUN])
             nc.gpsimd.tensor_tensor(*in_runs(grouped, planes), spread, MULT)
 
-        def codes_of(g, first, last):
-            e = first // C
-            if g == 2:
-                return last_codes[e][:, first - e * C : last - e * C]
-            if g == 1:
-                return middle_codes[e][:, first - e * C : last - e * C]
-            if e == E - 1:
-                return held_codes[:, first - e * C : last - e * C]
-            return first_codes[:, first:last]
+        made = {}
+        used = [0]
 
-        def scales_of(g, first, last):
-            if (g, first) == (2, C):
-                return held_scales[:]
-            return scales[:, g, first:last]
-
-        def quantise(grouped, g, first, last):
-            nc.vector.quantize_mx(out=codes_of(g, first, last).bitcast(E5M2), scales=scales_of(g, first, last), in_=grouped)
-
-        def weave_w(grouped, e):
-            weave_aside(grouped, w_raw[e])
+        def quantise(grouped, codes, *parts):
+            width = sum(last - first for g, first, last in parts)
+            plane = scales[:, used[0] : used[0] + width]
+            used[0] = used[0] + width
+            nc.vector.quantize_mx(out=codes.bitcast(E5M2), scales=plane, in_=grouped)
+            at = 0
+            for g, first, last in parts:
+                made[g, first] = (codes[:, at : at + last - first], plane[:, at : at + last - first])
+                at = at + last - first
 
         def quantise_w(grouped, e):
             nc.vector.quantize_mx(out=w_codes[e][:].bitcast(E4M3), scales=w_scales[:, e], in_=grouped)
 
-        def multiply(first, last, order):
+        def multiply(first, last):
             e = first // C
             bank = psum.tile([P, last - first], F32, name=f"bank{(first + PIECE) // C % E}")
-            for g in order:
+            for g in range(PASSES):
+                codes, plane = made[g, first]
                 nc.tensor.matmul_mx(
                     out=bank[:],
                     lhsT=w_codes[e][:, g * K : (g + 1) * K].bitcast(E4M3),
                     lhsT_scale=w_scales[:, e, g * K : (g + 1) * K],
-                    rhs=codes_of(g, first, last).bitcast(E5M2),
-                    rhs_scale=scales_of(g, first, last),
-                    start=(g == order[0]),
-                    stop=(g == order[-1]),
+                    rhs=codes.bitcast(E5M2),
+                    rhs_scale=plane,
+                    start=(g == 0),
+                    stop=(g == PASSES - 1),
                 )
             return bank
 
-        def empty_on_scalar(bank, start, first, last):
-            nc.scalar.copy(out=results[:, first:last], in_=bank[:, first - start : last - start])
-
-        def empty_on_vector(bank, start, first, last):
-            nc.vector.tensor_copy(results[:, first:last], bank[:, first - start : last - start])
+        def empty(bank, base, first, last):
+            nc.scalar.copy(out=results[:, first:last], in_=bank[:, first - base : last - base])
 
         def scatter(first, last):
             nc.scalar.activation(listed(tokens[:], first, last), results[:, first:last], COPY)
+
+        third = 3 * C
+        w_grouped = [room(HALF - W_WIDTH // 2, W_WIDTH), room(6 * C - K, W_WIDTH)]
 
         for t in range(PLANES - 1):
             gather_on_scalar(lower[:, t], 0, t, 0, HALF)
         for e in range(2):
             gather_on_scalar(lower[:, 3, e * C : (e + 1) * C], 0, 3, e * C, (e + 1) * C)
-        gather_gated(upper_0, 0, HALF, SLOTS)
-        weave_aside(room(HALF, LATE - HALF), upper_0[:, :, : LATE - HALF])
+        gather_gated(upper, 0, HALF, SLOTS)
+        weave_aside(room(HALF, LATE - HALF), upper[:, :, : LATE - HALF])
         for e in range(2):
             weave_gating(room(e * C, C), lower[:, :, e * C : (e + 1) * C], e * C, (e + 1) * C)
-        quantise(room(2 * C, C), 0, 2 * C, 3 * C)
-        quantise(room(0, HALF), 0, 0, HALF)
-        weave_aside(room(0, PIECE), upper_0[:, :, LATE - HALF :])
+        quantise(room(HALF, C), first_codes[:, HALF:], (0, HALF, third))
+        quantise(room(0, HALF), first_codes[:, :HALF], (0, 0, C), (0, C, HALF))
+        weave_aside(room(0, PIECE), upper[:, :, LATE - HALF :])
 
-        w_width = PASSES * K
-        w_start = LATE + HALF
-        middle_room = [room(w_start + w_width - PIECE, C), room(C, C), room(LATE, C), room(LATE + C, C)]
-        w_grouped = [room(HALF - w_width // 2, w_width), room(w_start, w_width)]
-        for t in range(2):
-            for e in (2, 3):
-                gather_on_scalar(upper_1[e][:, t], 1, t, e * C, (e + 1) * C)
-            gather_on_scalar(lower_1[:, t], 1, t, 0, HALF)
-        for e in (2, 3):
+        seam = start + PLANES * HALF
+        gather_on_scalar(inner[:, seam + 3 * C : seam + 5 * C], 1, 0, HALF, SLOTS)
+        gather_on_scalar(lower_1[:, 2], 1, 0, 0, HALF)
+        gather_on_scalar(inner[:, seam - HALF : seam + C], 1, 1, 0, third)
+        gather_on_scalar(upper_1[3][:, 1], 1, 1, third, SLOTS)
+        for e, place in ((2, LATE + C), (3, LATE)):
             for t in (2, 3):
-                gather_on_vector(upper_1[e][:, t], 1, t, e * C, (e + 1) * C)
-            weave_gating_aside(middle_room[e], upper_1[e], e * C, (e + 1) * C)
+                gather_on_vector(upper_1[e][:, t - TURN.get((1, e), 0)], 1, t, e * C, (e + 1) * C)
+            weave_gating_aside(room(place, C), upper_1[e], e * C, (e + 1) * C)
         for t in (2, 3):
-            gather_on_vector(lower_1[:, t], 1, t, 0, HALF)
-        weave_gating(middle_room[0], lower_1[:, :, :C], 0, C)
+            gather_on_vector(lower_1[:, t - 2], 1, t, 0, HALF)
+        weave_gating(room(6 * C, C), lower_1[:, :, :C], 0, C)
 
-        weave_aside(w_grouped[0][:, : 2 * K * PLANES], w_raw[0])
-        weave_aside(w_grouped[0][:, 2 * K * PLANES :], tail[:])
+        weave_aside(w_grouped[0][:, : 2 * K * PLANES], w_front)
+        weave_aside(w_grouped[0][:, 2 * K * PLANES :], w_back[:])
         for t in range(PLANES - 1):
             gather_on_scalar(lower[:, t], 2, t, 0, HALF)
-        for e in range(2):
-            gather_on_scalar(lower[:, 3, e * C : (e + 1) * C], 2, 3, e * C, (e + 1) * C)
-        for t in (3, 0, 1, 2):
-            gather_on_scalar(upper_2[:, t], 2, t, HALF, HALF + C)
-        first = 3 * C
+        gather_on_scalar(lower[:, 3, :C], 2, 3, 0, C)
+        gather_on_scalar(outer[:, PLANES * HALF - C : PLANES * HALF + C], 2, 3, C, third)
+        for t in range(PLANES - 1):
+            gather_on_scalar(expert_2[:, t + 1], 2, t, HALF, third)
 
         weave_gating(room(7 * C, C), lower[:, :, :C], 0, C)
         quantise_w(w_grouped[0], 0)
-        quantise(room(7 * C, C), 2, 0, C)
-        quantise(middle_room[0], 1, 0, C)
-        bank = multiply(0, C, (0, 1, 2))
-        empty_on_scalar(bank, 0, 0, C)
-        ending = placed([P, 7 * PIECE], F32, "ending", 52)
+        quantise(room(6 * C, HALF), codes_0[:], (1, 0, C), (2, 0, C))
+        bank = multiply(0, C)
+        empty(bank, 0, 0, C)
+        ending = placed([P, 7 * PIECE], F32, "ending", 0)
         late = planes_in(ending, 0, PIECE)
         w_grouped.extend(ending[:, at * PIECE : (at + 3) * PIECE].bitcast(BF16) for at in (2, 4))
         for t in range(2):
-            gather_on_scalar(late[:, t], 2, t, first, LATE)
+            gather_on_scalar(late[:, t], 2, t, third, LATE)
             scatter(t * PIECE, (t + 1) * PIECE)
 
-        weave_w(w_grouped[1], 1)
-        weave_w(w_grouped[2], 2)
-        weave_gating(middle_room[1], lower_1[:, :, C:], C, 2 * C)
-        weave_gating(room(HALF, C), lower[:, :, C:], C, 2 * C)
+        for e in (1, 2):
+            weave_aside(w_grouped[e], w_raw[e][:])
+        weave_gating(room(C, C), lower_1[:, :, C:], C, HALF)
+        weave_gating(room(HALF, C), lower[:, :, C:], C, HALF)
         quantise_w(w_grouped[1], 1)
-        quantise(middle_room[1], 1, C, 2 * C)
-        quantise(room(HALF, C), 2, C, 2 * C)
-        quantise(middle_room[2], 1, 2 * C, 3 * C)
+        quantise(room(C, C), codes_1[:, :C], (1, C, HALF))
+        quantise(room(HALF, C), codes_1[:, C:], (2, C, HALF))
+        quantise(room(LATE + C, C), codes_2[0][:], (1, HALF, third))
         quantise_w(w_grouped[2], 2)
-        bank = multiply(C, 2 * C, (0, 1, 2))
-        empty_on_scalar(bank, C, C, C + PIECE)
-        empty_on_scalar(bank, C, C + PIECE, 2 * C)
+        bank = multiply(C, HALF)
+        empty(bank, C, C, C + PIECE)
+        empty(bank, C, C + PIECE, HALF)
         scatter(C, C + PIECE)
-        gather_on_scalar(late[:, 2], 2, 2, first, LATE)
-        scatter(C + PIECE, 2 * C)
+        gather_on_scalar(late[:, 2], 2, 2, third, LATE)
+        scatter(C + PIECE, HALF)
 
-        weave_w(w_grouped[3], 3)
-        weave_gating(room(HALF, C), upper_2, 2 * C, 3 * C)
-        gather_on_vector(late[:, 3], 2, 3, first, LATE)
-        quantise(room(HALF, C), 2, 2 * C, 3 * C)
+        weave_aside(w_grouped[3], w_raw[3][:])
+        weave_gating(room(HALF, C), expert_2, HALF, third)
+        gather_on_vector(late[:, 3], 2, 3, third, LATE)
+        quantise(room(HALF, C), codes_2[1][:], (2, HALF, third))
         quantise_w(w_grouped[3], 3)
-        quantise(room(LATE + C, PIECE), 1, first, LATE)
-        bank = multiply(2 * C, 3 * C, (0, 1, 2))
+        quantise(room(LATE, PIECE), codes_3[0][:, PIECE:C], (1, third, LATE))
+        bank = multiply(HALF, third)
         middle = (HALF + LATE) // 2
-        empty_on_scalar(bank, HALF, HALF, middle)
-        empty_on_scalar(bank, HALF, middle, first)
+        empty(bank, HALF, HALF, middle)
+        empty(bank, HALF, middle, third)
         scatter(HALF, middle)
 
-        weave_gating(room(HALF, PIECE), late, first, LATE)
-        quantise(room(first, PIECE), 0, first, LATE)
-        quantise(room(HALF, PIECE), 2, first, LATE)
-        empty_on_scalar(multiply(first, LATE, (1, 0, 2)), first, first, LATE)
+        weave_gating(room(HALF, PIECE), late, third, LATE)
+        quantise(room(third, PIECE), codes_3[0][:, :PIECE], (0, third, LATE))
+        quantise(room(HALF, PIECE), codes_3[1][:, :PIECE], (2, third, LATE))
+        empty(multiply(third, LATE), third, third, LATE)
         scatter(middle, LATE)
         gather_gated(late, 2, LATE, SLOTS)
-        quantise(room(0, PIECE), 0, LATE, SLOTS)
+        quantise(room(0, PIECE), codes_3[0][:, C : C + PIECE], (0, LATE, SLOTS))
         weave(room(HALF + PIECE, PIECE), late)
-        quantise(room(LATE + C + PIECE, PIECE), 1, LATE, SLOTS)
-        quantise(room(HALF + PIECE, PIECE), 2, LATE, SLOTS)
-        nc.vector.tensor_copy(results[:, LATE:], multiply(LATE, SLOTS, (0, 1, 2))[:])
+        quantise(room(LATE + PIECE, PIECE), codes_3[0][:, C + PIECE :], (1, LATE, SLOTS))
+        quantise(room(HALF + PIECE, PIECE), codes_3[1][:, PIECE:], (2, LATE, SLOTS))
+        nc.vector.tensor_copy(results[:, LATE:], multiply(LATE, SLOTS)[:])
         nc.vector.tensor_copy(listed(tokens[:], LATE, SLOTS), results[:, LATE:])
 
         for q, queue in enumerate((nc.sync, nc.scalar, nc.sync, nc.scalar)):

@@ -15,6 +15,8 @@ PIECE = 256
 LATE = SLOTS - PIECE
 W_WIDTH = PASSES * K
 KIB = 1024
+SHARE = 64
+FRONT = 608
 
 TURN = {(1, 0): 2, (1, 1): 2, (1, 2): 1, (2, 2): 3}
 
@@ -49,6 +51,7 @@ def tile_moe_bdx_lin_none_kernel(tc, dyT, w, gate, offs, out):
 
         offsets = lists.tile([P, SLOTS // OFFSETS], U16, name="offsets")
         gates = keep.tile([P, HALF], F32, name="gates", align_bytes=256)
+        share_gates = keep.tile([P, SHARE], F32, name="share_gates", align_bytes=256)
         tokens = keep.tile([P, T], F32, name="tokens", align_bytes=256)
         outer = keep.tile([P, PLANES * (HALF + C) + PIECE], F32, name="outer", align_bytes=256)
         inner = keep.tile([P, 2 * HALF + PLANES * SLOTS], F32, name="inner", align_bytes=256)
@@ -93,6 +96,7 @@ def tile_moe_bdx_lin_none_kernel(tc, dyT, w, gate, offs, out):
         for t in range(1, PLANES):
             load_dy(0, t, (0, T))
         load_gate(0)
+        nc.sync.dma_start(out=share_gates[:], in_=gate[:P, HALF - SHARE : HALF])
         for t in range(2):
             load_dy(1, t, (0, T))
         pair = placed([P, 2, T], F32, "dy_pair", 8 * (PLANES + 2))
@@ -164,7 +168,7 @@ def tile_moe_bdx_lin_none_kernel(tc, dyT, w, gate, offs, out):
             nc.vector.tensor_tensor(*in_runs(grouped, planes), spread, MULT)
 
         def weave_gating_aside(grouped, planes, first, last):
-            columns = gates[:, first - HALF : last - HALF]
+            columns = gates[:, first - HALF : last - HALF] if first >= HALF else share_gates[:]
             runs = columns.rearrange("q (c i) -> q c i", i=RUN)
             spread = runs.unsqueeze(2).to_broadcast([P, (last - first) // RUN, PLANES, RUN])
             nc.gpsimd.tensor_tensor(*in_runs(grouped, planes), spread, MULT)
@@ -208,26 +212,28 @@ def tile_moe_bdx_lin_none_kernel(tc, dyT, w, gate, offs, out):
             nc.scalar.activation(listed(tokens[:], first, last), results[:, first:last], COPY)
 
         third = 3 * C
-        w_grouped = [room(HALF - W_WIDTH // 2, W_WIDTH), room(6 * C - K, W_WIDTH)]
+        w_grouped = [room(third - W_WIDTH // 2, W_WIDTH), room(6 * C + K, W_WIDTH)]
 
         for t in range(PLANES - 1):
             gather_on_scalar(lower[:, t], 0, t, 0, HALF)
         for e in range(2):
             gather_on_scalar(lower[:, 3, e * C : (e + 1) * C], 0, 3, e * C, (e + 1) * C)
         gather_gated(upper, 0, HALF, SLOTS)
-        weave_aside(room(HALF, LATE - HALF), upper[:, :, : LATE - HALF])
-        for e in range(2):
-            weave_gating(room(e * C, C), lower[:, :, e * C : (e + 1) * C], e * C, (e + 1) * C)
-        quantise(room(HALF, C), first_codes[:, HALF:], (0, HALF, third))
-        quantise(room(0, HALF), first_codes[:, :HALF], (0, 0, C), (0, C, HALF))
-        weave_aside(room(0, PIECE), upper[:, :, LATE - HALF :])
+        weave_aside(room(0, FRONT), upper[:, :, :FRONT])
+        cut = HALF - SHARE
+        weave_gating_aside(room(FRONT + cut, SHARE), lower[:, :, cut:], cut, HALF)
+        weave_gating(room(FRONT, C), lower[:, :, :C], 0, C)
+        weave_gating(room(FRONT + C, cut - C), lower[:, :, C:cut], C, cut)
+        quantise(room(0, C), first_codes[:, HALF:], (0, HALF, third))
+        quantise(room(FRONT, HALF), first_codes[:, :HALF], (0, 0, C), (0, C, HALF))
+        weave_aside(room(FRONT, HALF - FRONT), upper[:, :, FRONT:])
 
         seam = start + PLANES * HALF
         gather_on_scalar(inner[:, seam + 3 * C : seam + 5 * C], 1, 0, HALF, SLOTS)
         gather_on_scalar(lower_1[:, 2], 1, 0, 0, HALF)
         gather_on_scalar(inner[:, seam - HALF : seam + C], 1, 1, 0, third)
         gather_on_scalar(upper_1[3][:, 1], 1, 1, third, SLOTS)
-        for e, place in ((2, LATE + C), (3, LATE)):
+        for e, place in ((2, 4 * C), (3, 5 * C)):
             for t in (2, 3):
                 gather_on_vector(upper_1[e][:, t - TURN.get((1, e), 0)], 1, t, e * C, (e + 1) * C)
             weave_gating_aside(room(place, C), upper_1[e], e * C, (e + 1) * C)
@@ -258,12 +264,12 @@ def tile_moe_bdx_lin_none_kernel(tc, dyT, w, gate, offs, out):
 
         for e in (1, 2):
             weave_aside(w_grouped[e], w_raw[e][:])
-        weave_gating(room(C, C), lower_1[:, :, C:], C, HALF)
-        weave_gating(room(HALF, C), lower[:, :, C:], C, HALF)
+        weave_gating(room(HALF, C), lower_1[:, :, C:], C, HALF)
+        weave_gating(room(3 * C, C), lower[:, :, C:], C, HALF)
         quantise_w(w_grouped[1], 1)
-        quantise(room(C, C), codes_1[:, :C], (1, C, HALF))
-        quantise(room(HALF, C), codes_1[:, C:], (2, C, HALF))
-        quantise(room(LATE + C, C), codes_2[0][:], (1, HALF, third))
+        quantise(room(HALF, C), codes_1[:, :C], (1, C, HALF))
+        quantise(room(3 * C, C), codes_1[:, C:], (2, C, HALF))
+        quantise(room(4 * C, C), codes_2[0][:], (1, HALF, third))
         quantise_w(w_grouped[2], 2)
         bank = multiply(C, HALF)
         empty(bank, C, C, C + PIECE)
@@ -273,27 +279,27 @@ def tile_moe_bdx_lin_none_kernel(tc, dyT, w, gate, offs, out):
         scatter(C + PIECE, HALF)
 
         weave_aside(w_grouped[3], w_raw[3][:])
-        weave_gating(room(HALF, C), expert_2, HALF, third)
+        weave_gating(room(3 * C, C), expert_2, HALF, third)
         gather_on_vector(late[:, 3], 2, 3, third, LATE)
-        quantise(room(HALF, C), codes_2[1][:], (2, HALF, third))
+        quantise(room(3 * C, C), codes_2[1][:], (2, HALF, third))
         quantise_w(w_grouped[3], 3)
-        quantise(room(LATE, PIECE), codes_3[0][:, PIECE:C], (1, third, LATE))
+        quantise(room(5 * C, PIECE), codes_3[0][:, PIECE:C], (1, third, LATE))
         bank = multiply(HALF, third)
         middle = (HALF + LATE) // 2
         empty(bank, HALF, HALF, middle)
         empty(bank, HALF, middle, third)
         scatter(HALF, middle)
 
-        weave_gating(room(HALF, PIECE), late, third, LATE)
-        quantise(room(third, PIECE), codes_3[0][:, :PIECE], (0, third, LATE))
-        quantise(room(HALF, PIECE), codes_3[1][:, :PIECE], (2, third, LATE))
+        weave_gating(room(3 * C, PIECE), late, third, LATE)
+        quantise(room(C, PIECE), codes_3[0][:, :PIECE], (0, third, LATE))
+        quantise(room(3 * C, PIECE), codes_3[1][:, :PIECE], (2, third, LATE))
         empty(multiply(third, LATE), third, third, LATE)
         scatter(middle, LATE)
         gather_gated(late, 2, LATE, SLOTS)
-        quantise(room(0, PIECE), codes_3[0][:, C : C + PIECE], (0, LATE, SLOTS))
-        weave(room(HALF + PIECE, PIECE), late)
-        quantise(room(LATE + PIECE, PIECE), codes_3[0][:, C + PIECE :], (1, LATE, SLOTS))
-        quantise(room(HALF + PIECE, PIECE), codes_3[1][:, PIECE:], (2, LATE, SLOTS))
+        quantise(room(C + PIECE, PIECE), codes_3[0][:, C : C + PIECE], (0, LATE, SLOTS))
+        weave(room(LATE, PIECE), late)
+        quantise(room(5 * C + PIECE, PIECE), codes_3[0][:, C + PIECE :], (1, LATE, SLOTS))
+        quantise(room(LATE, PIECE), codes_3[1][:, PIECE:], (2, LATE, SLOTS))
         nc.vector.tensor_copy(results[:, LATE:], multiply(LATE, SLOTS)[:])
         nc.vector.tensor_copy(listed(tokens[:], LATE, SLOTS), results[:, LATE:])
 

from contextlib import ExitStack

import concourse.mybir as mybir
from concourse.masks import make_identity

K, T, E, C, N = 128, 2048, 4, 512, 1536
SLOTS = E * C
P = 128
PLANES = 4
PASSES = N // (P * PLANES)
OFFSETS = 16
HALF = SLOTS // 2
RUN = 4
PIECE = 256
LATE = SLOTS - PIECE
W_WIDTH = PASSES * K
KIB = 1024
SHARE = 64
FRONT = 608

TURN = {(1, 0): 2, (1, 1): 2, (1, 2): 1, (2, 2): 3}

FLOPS = 2 * K * N * SLOTS
BYTES = 4 * (N * T + E * N * K + SLOTS + K * T) + 2 * SLOTS

F32 = mybir.dt.float32
BF16 = mybir.dt.bfloat16
U32 = mybir.dt.uint32
U16 = mybir.dt.uint16
U8 = mybir.dt.uint8
E4M3 = mybir.dt.float8_e4m3fn_x4
E5M2 = mybir.dt.float8_e5m2_x4
MULT = mybir.AluOpType.mult
ADD = mybir.AluOpType.add
COPY = mybir.ActivationFunctionType.Copy


def tile_moe_bdx_lin_none_kernel(tc, dyT, w, gate, offs, out):
    nc = tc.nc
    dy_rows = dyT.rearrange("(g p t) c -> g p t c", p=P, t=PLANES)
    w_rows = w.rearrange("e (g p t) k -> e g p t k", p=P, t=PLANES)

    with ExitStack() as ctx:
        lists = ctx.enter_context(tc.tile_pool(name="lists", bufs=1))
        keep = ctx.enter_context(tc.tile_pool(name="keep", bufs=1))
        shared = ctx.enter_context(tc.tile_pool(name="shared", bufs=1))
        psum = ctx.enter_context(tc.psum_pool(name="psum", bufs=1))

        def placed(shape, dtype, name, kib):
            return shared.tile(shape, dtype, name=name, offset=kib * KIB, align_bytes=256)

        offsets = lists.tile([P, SLOTS // OFFSETS], U16, name="offsets")
        gates = keep.tile([P, HALF], F32, name="gates", align_bytes=256)
        share_gates = keep.tile([P, SHARE], F32, name="share_gates", align_bytes=256)
        tokens = keep.tile([P, T], F32, name="tokens", align_bytes=256)
        outer = keep.tile([P, PLANES * (HALF + C) + PIECE], F32, name="outer", align_bytes=256)
        inner = keep.tile([P, 2 * HALF + PLANES * SLOTS], F32, name="inner", align_bytes=256)
        woven = keep.tile([P, 8 * C * PLANES], BF16, name="woven", align_bytes=64)
        first_codes = keep.tile([P, 3 * C], U32, name="first_codes", align_bytes=64)
        scales = keep.tile([P, PASSES * SLOTS], U8, name="scales", align_bytes=64)
        w_scales = keep.tile([P, E, W_WIDTH], U8, name="w_scales", align_bytes=64)
        identity = keep.tile([P, P], F32, name="identity")
        gate_runs = [keep.tile([P, 2, 2 * RUN], F32, name=f"gate_runs{h}") for h in range(2)]
        gate_banks = [psum.tile([P, RUN, P], F32, name=f"gate_bank{e}") for e in range(E)]

        def planes_in(tile, start, width):
            return tile[:, start : start + PLANES * width].rearrange("p (t c) -> p t c", t=PLANES)

        lower = planes_in(outer, 0, HALF)
        expert_2 = planes_in(outer, PLANES * HALF, C)
        upper = planes_in(inner, 0, HALF)
        start = 2 * HALF
        lower_1 = planes_in(inner, start, HALF)
        upper_1 = {e: planes_in(inner, start + PLANES * e * C, C) for e in (2, 3)}

        dy = {}

        def load_gate(h):
            half = gate[0, h * HALF : (h + 1) * HALF]
            nc.sync.dma_start(out=gate_runs[h][:, :, :RUN], in_=half.rearrange("(e p c) -> p e c", p=P, c=RUN))

        def load_dy(g, t, cuts):
            dy[g, t] = placed([P, T], F32, f"dy{g}{t}", 8 * (PLANES * g + t))[:]
            for first, last in zip(cuts, cuts[1:]):
                nc.sync.dma_start(out=dy[g, t][:, first:last], in_=dy_rows[g, :, t, first:last])

        def load_w(target, g, e):
            turn = TURN.get((g, e), 0)
            nc.sync.dma_start(out=target[:, : PLANES - turn], in_=w_rows[e, g, :, turn:])
            if turn:
                nc.sync.dma_start(out=target[:, PLANES - turn :], in_=w_rows[e, g, :, :turn])

        load_gate(1)
        load_dy(0, 0, (0, HALF, T))
        nc.sync.dma_start(out=offsets[:], in_=offs)
        for t in range(1, PLANES):
            load_dy(0, t, (0, T))
        load_gate(0)
        nc.sync.dma_start(out=share_gates[:], in_=gate[:P, HALF - SHARE : HALF])
        for t in range(2):
            load_dy(1, t, (0, T))
        pair = placed([P, 2, T], F32, "dy_pair", 8 * (PLANES + 2))
        nc.sync.dma_start(out=pair[:], in_=dy_rows[1, :, 2:])
        dy[1, 2], dy[1, 3] = pair[:, 0], pair[:, 1]
        for t in range(PLANES):
            load_dy(2, t, (0, T))

        w_front = outer[:, PLANES * HALF + C - PIECE :].rearrange("p (t c) -> p t c", t=PLANES)[:, :, PIECE:]
        w_back = placed([P, PLANES, K], F32, "w_back", 0)
        for g in range(2):
            load_w(w_front[:, :, g * K : (g + 1) * K], g, 0)
        load_w(w_back[:], 2, 0)
        w_raw = {e: placed([P, PLANES, W_WIDTH], F32, f"w_raw{e}", 8 * e) for e in range(1, E)}
        for e in range(1, E):
            for g in range(PASSES):
                load_w(w_raw[e][:, :, g * K : (g + 1) * K], g, e)

        results = placed([P, SLOTS], F32, "results", 32)
        codes_0 = placed([P, 2 * C], U32, "codes_0", 0)
        codes_1 = placed([P, 2 * C], U32, "codes_1", 14)
        codes_2 = [placed([P, C], U32, f"codes_2{g}", place) for g, place in ((1, 18), (2, 40))]
        codes_3 = [placed([P, 2 * C], U32, "codes_3", 24), placed([P, C], U32, "codes_32", 42)]
        w_codes = [placed([P, W_WIDTH], U32, f"w_codes{e}", place) for e, place in enumerate((44, 20, 48, 50))]

        make_identity(nc, identity[:])
        unread = keep.tile([P, 1], F32, name="unread")
        nc.scalar.activation(unread[:], gate_runs[1][:, 0, :1], COPY)
        for e in (2, 3, 0, 1):
            for c in range(RUN):
                column = gate_runs[e // 2][:, e % 2, c : c + 1]
                nc.tensor.transpose(gate_banks[e][:, c], column.to_broadcast([P, P]), identity[:])
            if e >= 2:
                target = gates[:, (e - 2) * C : (e - 1) * C].rearrange("q (p c) -> q p c", c=RUN)
                nc.vector.tensor_copy(target, gate_banks[e][:].rearrange("q c p -> q p c"))

        def listed(window, first, last):
            return window.indirect(offsets[:, first // OFFSETS : last // OFFSETS])

        def gather_on_scalar(target, g, t, first, last):
            nc.scalar.activation(target, listed(dy[g, t], first, last), COPY)

        def gather_on_vector(target, g, t, first, last):
            nc.vector.tensor_copy(target, listed(dy[g, t], first, last))

        def gather_gated(planes, g, first, last):
            for t in range(PLANES):
                nc.vector.tensor_tensor(planes[:, t], listed(dy[g, t], first, last), gates[:, first - HALF : last - HALF], MULT)

        def room(place, width):
            return woven[:, place * PLANES : (place + width) * PLANES]

        def in_runs(grouped, planes):
            return (
                grouped.rearrange("p (c i t) -> p c t i", i=RUN, t=PLANES),
                planes.rearrange("p t (c i) -> p c t i", i=RUN),
            )

        def weave(grouped, planes):
            nc.vector.tensor_copy(*in_runs(grouped, planes))

        def weave_aside(grouped, planes):
            nc.gpsimd.tensor_scalar(*in_runs(grouped, planes), 1.0, 0.0, MULT, ADD)

        def weave_gating(grouped, planes, first, last):
            width = last - first
            runs = gate_banks[first // C][:, :, first % C // RUN : (first % C + width) // RUN]
            spread = runs.rearrange("q i c -> q c i").unsqueeze(2).to_broadcast([P, width // RUN, PLANES, RUN])
            nc.vector.tensor_tensor(*in_runs(grouped, planes), spread, MULT)

        def weave_gating_aside(grouped, planes, first, last):
            columns = gates[:, first - HALF : last - HALF] if first >= HALF else share_gates[:]
            runs = columns.rearrange("q (c i) -> q c i", i=RUN)
            spread = runs.unsqueeze(2).to_broadcast([P, (last - first) // RUN, PLANES, RUN])
            nc.gpsimd.tensor_tensor(*in_runs(grouped, planes), spread, MULT)

        made = {}
        used = [0]

        def quantise(grouped, codes, *parts):
            width = sum(last - first for g, first, last in parts)
            plane = scales[:, used[0] : used[0] + width]
            used[0] = used[0] + width
            nc.vector.quantize_mx(out=codes.bitcast(E5M2), scales=plane, in_=grouped)
            at = 0
            for g, first, last in parts:
                made[g, first] = (codes[:, at : at + last - first], plane[:, at : at + last - first])
                at = at + last - first

        def quantise_w(grouped, e):
            nc.vector.quantize_mx(out=w_codes[e][:].bitcast(E4M3), scales=w_scales[:, e], in_=grouped)

        def multiply(first, last):
            e = first // C
            bank = psum.tile([P, last - first], F32, name=f"bank{(first + PIECE) // C % E}")
            for g in range(PASSES):
                codes, plane = made[g, first]
                nc.tensor.matmul_mx(
                    out=bank[:],
                    lhsT=w_codes[e][:, g * K : (g + 1) * K].bitcast(E4M3),
                    lhsT_scale=w_scales[:, e, g * K : (g + 1) * K],
                    rhs=codes.bitcast(E5M2),
                    rhs_scale=plane,
                    start=(g == 0),
                    stop=(g == PASSES - 1),
                )
            return bank

        def empty(bank, base, first, last):
            nc.scalar.copy(out=results[:, first:last], in_=bank[:, first - base : last - base])

        def scatter(first, last):
            nc.scalar.activation(listed(tokens[:], first, last), results[:, first:last], COPY)

        third = 3 * C
        w_grouped = [room(third - W_WIDTH // 2, W_WIDTH), room(6 * C + K, W_WIDTH)]

        for t in range(PLANES - 1):
            gather_on_scalar(lower[:, t], 0, t, 0, HALF)
        for e in range(2):
            gather_on_scalar(lower[:, 3, e * C : (e + 1) * C], 0, 3, e * C, (e + 1) * C)
        gather_gated(upper, 0, HALF, SLOTS)
        weave_aside(room(0, FRONT), upper[:, :, :FRONT])
        cut = HALF - SHARE
        weave_gating_aside(room(FRONT + cut, SHARE), lower[:, :, cut:], cut, HALF)
        weave_gating(room(FRONT, C), lower[:, :, :C], 0, C)
        weave_gating(room(FRONT + C, cut - C), lower[:, :, C:cut], C, cut)
        quantise(room(0, C), first_codes[:, HALF:], (0, HALF, third))
        quantise(room(FRONT, HALF), first_codes[:, :HALF], (0, 0, C), (0, C, HALF))
        weave_aside(room(FRONT, HALF - FRONT), upper[:, :, FRONT:])

        seam = start + PLANES * HALF
        gather_on_scalar(inner[:, seam + 3 * C : seam + 5 * C], 1, 0, HALF, SLOTS)
        gather_on_scalar(lower_1[:, 2], 1, 0, 0, HALF)
        gather_on_scalar(inner[:, seam - HALF : seam + C], 1, 1, 0, third)
        gather_on_scalar(upper_1[3][:, 1], 1, 1, third, SLOTS)
        for e, place in ((2, 4 * C), (3, 5 * C)):
            for t in (2, 3):
                gather_on_vector(upper_1[e][:, t - TURN.get((1, e), 0)], 1, t, e * C, (e + 1) * C)
            weave_gating_aside(room(place, C), upper_1[e], e * C, (e + 1) * C)
        for t in (2, 3):
            gather_on_vector(lower_1[:, t - 2], 1, t, 0, HALF)
        weave_gating(room(6 * C, C), lower_1[:, :, :C], 0, C)

        weave_aside(w_grouped[0][:, : 2 * K * PLANES], w_front)
        weave_aside(w_grouped[0][:, 2 * K * PLANES :], w_back[:])
        for t in range(PLANES - 1):
            gather_on_scalar(lower[:, t], 2, t, 0, HALF)
        gather_on_scalar(lower[:, 3, :C], 2, 3, 0, C)
        gather_on_scalar(outer[:, PLANES * HALF - C : PLANES * HALF + C], 2, 3, C, third)
        for t in range(PLANES - 1):
            gather_on_scalar(expert_2[:, t + 1], 2, t, HALF, third)

        weave_gating(room(7 * C, C), lower[:, :, :C], 0, C)
        quantise_w(w_grouped[0], 0)
        quantise(room(6 * C, HALF), codes_0[:], (1, 0, C), (2, 0, C))
        bank = multiply(0, C)
        empty(bank, 0, 0, C)
        ending = placed([P, 7 * PIECE], F32, "ending", 0)
        late = planes_in(ending, 0, PIECE)
        w_grouped.extend(ending[:, at * PIECE : (at + 3) * PIECE].bitcast(BF16) for at in (2, 4))
        for t in range(2):
            gather_on_scalar(late[:, t], 2, t, third, LATE)
            scatter(t * PIECE, (t + 1) * PIECE)

        for e in (1, 2):
            weave_aside(w_grouped[e], w_raw[e][:])
        weave_gating(room(HALF, C), lower_1[:, :, C:], C, HALF)
        weave_gating(room(3 * C, C), lower[:, :, C:], C, HALF)
        quantise_w(w_grouped[1], 1)
        quantise(room(HALF, C), codes_1[:, :C], (1, C, HALF))
        quantise(room(3 * C, C), codes_1[:, C:], (2, C, HALF))
        quantise(room(4 * C, C), codes_2[0][:], (1, HALF, third))
        quantise_w(w_grouped[2], 2)
        bank = multiply(C, HALF)
        empty(bank, C, C, C + PIECE)
        empty(bank, C, C + PIECE, HALF)
        scatter(C, C + PIECE)
        gather_on_scalar(late[:, 2], 2, 2, third, LATE)
        scatter(C + PIECE, HALF)

        weave_aside(w_grouped[3], w_raw[3][:])
        weave_gating(room(3 * C, C), expert_2, HALF, third)
        gather_on_vector(late[:, 3], 2, 3, third, LATE)
        quantise(room(3 * C, C), codes_2[1][:], (2, HALF, third))
        quantise_w(w_grouped[3], 3)
        quantise(room(5 * C, PIECE), codes_3[0][:, PIECE:C], (1, third, LATE))
        bank = multiply(HALF, third)
        middle = (HALF + LATE) // 2
        empty(bank, HALF, HALF, middle)
        empty(bank, HALF, middle, third)
        scatter(HALF, middle)

        weave_gating(room(3 * C, PIECE), late, third, LATE)
        quantise(room(C, PIECE), codes_3[0][:, :PIECE], (0, third, LATE))
        quantise(room(3 * C, PIECE), codes_3[1][:, :PIECE], (2, third, LATE))
        empty(multiply(third, LATE), third, third, LATE)
        scatter(middle, LATE)
        gather_gated(late, 2, LATE, SLOTS)
        quantise(room(C + PIECE, PIECE), codes_3[0][:, C : C + PIECE], (0, LATE, SLOTS))
        weave(room(LATE, PIECE), late)
        quantise(room(5 * C + PIECE, PIECE), codes_3[0][:, C + PIECE :], (1, LATE, SLOTS))
        quantise(room(LATE, PIECE), codes_3[1][:, PIECE:], (2, LATE, SLOTS))
        nc.vector.tensor_copy(results[:, LATE:], multiply(LATE, SLOTS)[:])
        nc.vector.tensor_copy(listed(tokens[:], LATE, SLOTS), results[:, LATE:])

        for q, queue in enumerate((nc.sync, nc.scalar, nc.sync, nc.scalar)):
            queue.dma_start(out=out[:, q * C : (q + 1) * C], in_=tokens[:, q * C : (q + 1) * C])
